import numpy as np
import ml_dtypes


def mxq(x, axis, fmt="e4m3"):
    dtype, down = {"e4m3": (ml_dtypes.float8_e4m3fn, 7), "e5m2": (ml_dtypes.float8_e5m2, 14)}[fmt]
    v = np.moveaxis(np.asarray(x, np.float32).astype(ml_dtypes.bfloat16).astype(np.float64), axis, -1)
    blocks = v.reshape(v.shape[:-1] + (-1, 32))
    amax = np.abs(blocks).max(-1, keepdims=True)
    byte = np.maximum(np.where(amax > 0, np.frexp(amax)[1] - 1 + 127, 0) - down, 1)
    scale = np.exp2(byte - 127.0)
    codes = (blocks / scale).astype(np.float32).astype(dtype).astype(np.float64)
    return np.moveaxis((codes * scale).reshape(v.shape), -1, axis)


WIDE = False


def mx_kscale(k):
    if not WIDE:
        return np.ones(k)
    levels = np.array([18, -18])
    if k % 512:
        return np.exp2(np.random.permutation(np.resize(levels, k // 32))).repeat(32)
    a = np.empty((k // 512, 16))
    for p in range(k // 512):
        a[p, :8] = np.random.permutation(np.resize(levels, 8))
        for g in range(8):
            far = levels[np.abs(levels - a[p, g]) >= 10]
            a[p, g + 8] = far[np.random.randint(len(far))]
    return np.exp2(a.ravel()).repeat(32)


def f64(x):
    return np.asarray(x).astype(np.float64)


def striped(idx):
    return np.tile(np.asarray(idx).reshape(-1, 16).T, (8, 1)).astype(np.uint16)


def unstriped(offs):
    return offs[:16].T.reshape(-1).astype(np.int64)


def setup_inputs():
    n = np.random.standard_normal
    uni = np.random.uniform
    idx = np.random.permutation(2048)[:512]
    f_d = mx_kscale(512)
    f_i = np.ones(2048)
    f_i[idx] = mx_kscale(512)
    return {
        "xT": (0.5 * n((512, 512)) * f_d[:, None]).astype(np.float32),
        "wT": (n((512, 2048)) / np.sqrt(512) / f_d[:, None] * f_i[None, :]).astype(np.float32),
        "adv": (n((512, 512))).astype(np.float32),
        "us": (uni(0.75, 1.3, (512, 1))).astype(np.float32),
        "ts": np.tile(uni(0.75, 1.3, 2048) / f_i, (128, 1)).astype(np.float32),
        "wt": (uni(0.75, 1.3, (512, 1)) / np.sqrt(512)).astype(np.float32),
        "be": (uni(1.0, 3.0, (512, 1))).astype(np.float32),
        "offs": striped(idx),
    }


def reference(xT, wT, adv, us, ts, wt, be, offs):
    idx = unstriped(offs)
    wT_i = f64(wT)[:, idx]
    ts_i = f64(ts)[:1][:, idx]
    a = mxq(f64(xT), 0, "e4m3").T @ mxq(wT_i, 0, "e4m3")
    z = f64(us) * ts_i * a
    m = (z).max(-1, keepdims=True)
    e = np.exp(z - m)
    tot = (e).sum(-1, keepdims=True)
    p = e / tot
    l = z - m - np.log(tot)
    h = (p * l).sum(-1, keepdims=True)
    s = (f64(adv)).sum(-1, keepdims=True)
    g = f64(us) * ts_i * (f64(wt) * (p * s - f64(adv)) + f64(be) * p * (l - h))
    out = mxq(g, 1, "e5m2") @ mxq(wT_i, 1, "e4m3").T
    return out

@@ -1,0 +1,275 @@
+from contextlib import ExitStack
+
+import concourse.mybir as mybir
+from concourse.masks import make_identity
+
+R, D, SLOTS, T = 512, 512, 512, 2048
+FLOPS = 2 * 2 * R * D * SLOTS
+BYTES = 4 * (D * R + D * T + R * SLOTS + T + 3 * R + R * D) + 2 * 128 * SLOTS // 16
+
+F32 = mybir.dt.float32
+BF16 = mybir.dt.bfloat16
+U32 = mybir.dt.uint32
+U16 = mybir.dt.uint16
+U8 = mybir.dt.uint8
+E4M3 = mybir.dt.float8_e4m3fn_x4
+E5M2 = mybir.dt.float8_e5m2_x4
+ALU = mybir.AluOpType
+ACT = mybir.ActivationFunctionType
+AX = mybir.AxisListType
+
+P = 128
+PACK = 4
+TILES = R // P
+
+
+def tile_attend_gpgent_x_kernel(tc, xT, wT, adv, us, ts, wt, be, offs, out):
+    nc = tc.nc
+    with ExitStack() as ctx:
+        keep = ctx.enter_context(tc.tile_pool(name="keep", bufs=1))
+        stream = ctx.enter_context(tc.tile_pool(name="stream", bufs=1))
+        work = ctx.enter_context(tc.tile_pool(name="work", bufs=2))
+        psum = ctx.enter_context(tc.psum_pool(name="psum", bufs=1))
+        product_banks = [psum.tile([P, SLOTS], F32, name=f"product{m}") for m in range(TILES)]
+        grad_banks = [psum.tile([P, PACK, P], F32, name=f"grad{m}") for m in range(TILES)]
+
+        offsets = keep.tile([P, SLOTS // 16], U16, name="offsets")
+        row_vecs = keep.tile([P, P], F32, name="row_vecs")
+        ts_window = stream.tile([P, T], F32, name="window", align_bytes=64)
+        nc.vector.memset(ts_window[:, 0 : T // 2], 0.0)
+        nc.gpsimd.memset(ts_window[:, T // 2 : T], 0.0)
+        nc.gpsimd.memset(row_vecs[:], 0.0)
+        nc.scalar.dma_start(out=ts_window[0:1, :], in_=ts[0:1, :])
+
+        w_view = wT.rearrange("(p t) c -> p t c", t=PACK)
+        x_view = xT.rearrange("(p t) r -> p t r", t=PACK)
+        nc.sync.dma_start(offsets[:], offs)
+        w_planes = []
+        for t in range(PACK):
+            w_planes.append(stream.tile([P, T], F32, name=f"staged{t}"))
+            nc.sync.dma_start(out=w_planes[t][:], in_=w_view[:, t, :])
+        for j, vec in enumerate((us, wt, be)):
+            nc.scalar.dma_start(
+                out=row_vecs[j * TILES : (j + 1) * TILES, :], in_=vec.rearrange("(m p) o -> m (p o)", p=P)
+            )
+        x_halves = []
+        for h in range(2):
+            x_halves.append(stream.tile([P, PACK, R // 2], F32, name=f"staged{h}"))
+            nc.sync.dma_start(out=x_halves[h][:], in_=x_view[:, :, h * (R // 2) : (h + 1) * (R // 2)])
+        adv_tiles = []
+        for h in range(2):
+            pair = stream.tile([P, 2 * SLOTS], F32, name=f"staged{2 + h}")
+            nc.sync.dma_start(
+                out=pair[:].rearrange("p (e i) -> p e i", e=2),
+                in_=adv[2 * h * P : 2 * (h + 1) * P, :].rearrange("(e p) i -> p e i", e=2),
+            )
+            adv_tiles.extend(pair[:, e * SLOTS : (e + 1) * SLOTS] for e in range(2))
+
+        ident32 = keep.tile([P, P], F32, name="ident32")
+        make_identity(nc, ident32[:])
+        ident16 = keep.tile([P, P], BF16, name="ident16")
+        make_identity(nc, ident16[:])
+
+        warm = keep.tile([P, 1], F32, name="warm")
+        nc.scalar.activation(warm[:], ident32[:, 0:1], ACT.Exp)
+
+        ts_listed = keep.tile([P, SLOTS], F32, name="ts_listed")
+        nc.vector.tensor_copy(ts_listed[:], ts_window[:].indirect(offsets[:]))
+        turned = grad_banks[0]
+        for s in range(PACK):
+            nc.tensor.transpose(turned[:, s, :], ts_listed[:, s::PACK], ident32[:])
+        ts_cols = keep.tile([P, PACK], F32, name="ts_cols")
+        nc.scalar.copy(ts_cols[:], turned[:, :, 0])
+        spread = grad_banks[1]
+        for s in range(PACK):
+            nc.tensor.transpose(spread[:, s, :], ts_cols[:, s : s + 1].to_broadcast([P, P]), ident32[:])
+        ts_rows = keep.tile([P, PACK, P], F32, name="ts_rows")
+        nc.scalar.copy(ts_rows[:], spread[:])
+
+        vec_ps = product_banks[1][:, 0:P]
+        nc.tensor.transpose(vec_ps, row_vecs[:], ident32[:])
+        vec_cols = keep.tile([P, 3 * TILES], F32, name="vec_cols")
+        nc.scalar.copy(vec_cols[:], vec_ps[:, 0 : 3 * TILES])
+        us_cols = vec_cols[:, 0:TILES]
+        adv_scale = keep.tile([P, TILES], F32, name="adv_scale")
+        us_wt = keep.tile([P, TILES], F32, name="us_wt")
+        nc.gpsimd.tensor_tensor(us_wt[:], us_cols, vec_cols[:, TILES : 2 * TILES], ALU.mult)
+        nc.gpsimd.tensor_scalar(adv_scale[:], us_wt[:], -1.0, 0.0, ALU.mult, ALU.add)
+        consts = keep.tile([P, TILES, 8], F32, name="consts")
+        nc.gpsimd.memset(consts[:], -1.0)
+        nc.gpsimd.tensor_tensor(consts[:, :, 1], us_cols, vec_cols[:, 2 * TILES : 3 * TILES], ALU.mult)
+
+        w_by_d = stream.tile([P, SLOTS, PACK], BF16, name="window", align_bytes=64)
+        wd_codes = keep.tile([P, SLOTS], U32, name="wd_codes", align_bytes=64)
+        wd_scales = keep.tile([P, SLOTS], U8, name="wd_scales", align_bytes=64)
+        wi_codes = keep.tile([P, D], U32, name="wi_codes", align_bytes=64)
+        wi_scales = keep.tile([P, D], U8, name="wi_scales", align_bytes=64)
+
+        def gather_plane(t):
+            nc.vector.tensor_copy(w_by_d[:, :, t], w_planes[t][:].indirect(offsets[:]))
+
+        staging = [keep.tile([P, P, PACK], BF16, name=f"staging{j}", align_bytes=64) for j in range(TILES)]
+
+        def turn_plane(t, bank32, w_by_i):
+            bank = bank32.bitcast(BF16)[:, 0 : PACK * P].rearrange("q (s p) -> q s p", s=PACK)
+            for s in range(PACK):
+                nc.tensor.transpose(bank[:, s, :], w_by_d[:, s::PACK, t], ident16[:])
+            nc.scalar.copy(w_by_i[:], bank.rearrange("q s p -> q p s"))
+            cols = slice(t * P, (t + 1) * P)
+            nc.vector.quantize_mx(
+                out=wi_codes[:, cols].bitcast(E4M3),
+                scales=wi_scales[:, cols],
+                in_=w_by_i[:].rearrange("q p s -> q (p s)"),
+            )
+
+        x_codes = [keep.tile([P, P], U32, name=f"x_codes{m}", align_bytes=64) for m in range(TILES)]
+        x_scales = [keep.tile([P, P], U8, name=f"x_scales{m}", align_bytes=64) for m in range(TILES)]
+
+        def quantise_x(m):
+            h, e = divmod(m, 2)
+            grouped = work.tile([P, P, PACK], BF16, name="x_grouped", align_bytes=64, bufs=4)
+            nc.scalar.copy(
+                grouped[:].rearrange("p (c i) t -> p c t i", i=4),
+                x_halves[h][:, :, e * P : (e + 1) * P].rearrange("p t (c i) -> p c t i", i=4),
+            )
+            nc.vector.quantize_mx(
+                out=x_codes[m][:].bitcast(E4M3),
+                scales=x_scales[m][:],
+                in_=grouped[:].rearrange("p r t -> p (r t)"),
+            )
+
+        for t in range(PACK - 1):
+            gather_plane(t)
+            turn_plane(t, grad_banks[t % 2][:].rearrange("q s p -> q (s p)"), staging[t])
+        gather_plane(PACK - 1)
+        nc.vector.quantize_mx(
+            out=wd_codes[:].bitcast(E4M3), scales=wd_scales[:], in_=w_by_d[:].rearrange("p i t -> p (i t)")
+        )
+        quantise_x(0)
+        quantise_x(1)
+
+        state = {}
+
+        def add_turned(m, src, first, last):
+            for s in range(PACK):
+                nc.tensor.matmul(
+                    state["grad", m][:, s, :],
+                    lhsT=src[:, s, :],
+                    rhs=ident32[:],
+                    is_transpose=True,
+                    start=(first and s == 0),
+                    stop=(last and s == PACK - 1),
+                )
+
+        def scores(m):
+            acc = product_banks[m]
+            nc.tensor.matmul_mx(
+                out=acc[:],
+                lhsT=x_codes[m][:].bitcast(E4M3),
+                lhsT_scale=x_scales[m][:],
+                rhs=wd_codes[:].bitcast(E4M3),
+                rhs_scale=wd_scales[:],
+                start=True,
+                stop=True,
+            )
+            z = work.tile([P, PACK, P], F32, name="z", bufs=4)
+            nc.vector.scalar_tensor_tensor(
+                z[:], acc[:].rearrange("r (q s) -> r s q", s=PACK), us_cols[:, m : m + 1], ts_rows[:],
+                ALU.mult, ALU.mult,
+            )
+            state["z", m] = z
+
+        def softmax_sums(m):
+            z = state["z", m]
+            neg_max = work.tile([P, 1], F32, name="neg_max", bufs=4)
+            nc.vector.tensor_reduce(neg_max[:], z[:].rearrange("r s q -> r (s q)"), AX.X, ALU.max, negate=True)
+            e = work.tile([P, PACK, P], F32, name="e", bufs=4)
+            tot = work.tile([P, 1], F32, name="tot", bufs=4)
+            nc.scalar.activation(e[:], z[:], ACT.Exp, bias=neg_max[:], accum_out=tot[:])
+            state["e", m] = e
+            state["tot", m] = tot
+
+        def adv_term(m):
+            term = work.tile([P, PACK, P], F32, name="adv_term")
+            adv_sum = work.tile([P, 1], F32, name="adv_sum", bufs=4)
+            nc.scalar.activation(
+                term[:].rearrange("r s q -> r q s"),
+                adv_tiles[m].rearrange("r (q s) -> r q s", s=PACK),
+                ACT.Copy,
+                scale=adv_scale[:, m : m + 1],
+                accum_out=adv_sum[:],
+            )
+            nc.gpsimd.tensor_scalar(consts[:, m, 2:3], adv_sum[:], -1.0, 0.0, ALU.mult, ALU.add)
+            state["grad", m] = grad_banks[m]
+            add_turned(m, term, True, False)
+
+        def policy_terms(m):
+            z, e = state["z", m], state["e", m]
+            inv = work.tile([P, 1], F32, name="inv", bufs=4)
+            nc.vector.reciprocal(inv[:], state["tot", m][:])
+            scaled = work.tile([P, 3], F32, name="scaled", bufs=4)
+            nc.scalar.activation(scaled[:], consts[:, m, 0:3], ACT.Copy, scale=inv[:])
+            ze = work.tile([P, PACK, P], F32, name="ze")
+            ze_sum = work.tile([P, 1], F32, name="ze_sum", bufs=4)
+            nc.vector.scalar_tensor_tensor(ze[:], z[:], scaled[:, 1:2], e[:], ALU.mult, ALU.mult, accum_out=ze_sum[:])
+            add_turned(m, ze, False, False)
+            e_scale = work.tile([P, 1], F32, name="e_scale", bufs=4)
+            nc.scalar.activation(e_scale[:], ze_sum[:], ACT.Identity, scale=scaled[:, 0:1], bias=scaled[:, 2:3])
+            e_term = work.tile([P, PACK, P], F32, name="e_term")
+            nc.scalar.activation(e_term[:], e[:], ACT.Copy, scale=e_scale[:])
+            add_turned(m, e_term, False, True)
+
+        def finish_g(m):
+            g = work.tile([P, P, PACK], BF16, name="g", align_bytes=64)
+            nc.vector.tensor_tensor(
+                g[:],
+                state["grad", m][:].rearrange("q s r -> q r s"),
+                ts_cols[:].unsqueeze(1).to_broadcast([P, P, PACK]),
+                ALU.mult,
+            )
+            state["g", m] = g
+
+        def rows_gradient(m):
+            g_codes = work.tile([P, P], U32, name="g_codes", align_bytes=64)
+            g_scales = work.tile([P, P], U8, name="g_scales", align_bytes=64)
+            nc.vector.quantize_mx(
+                out=g_codes[:].bitcast(E5M2), scales=g_scales[:], in_=state["g", m][:].rearrange("q r s -> q (r s)")
+            )
+            acc = product_banks[m]
+            nc.tensor.matmul_mx(
+                out=acc[:],
+                lhsT=g_codes[:].bitcast(E5M2),
+                lhsT_scale=g_scales[:],
+                rhs=wi_codes[:].bitcast(E4M3),
+                rhs_scale=wi_scales[:],
+                start=True,
+                stop=True,
+            )
+            res = work.tile([P, P, PACK], F32, name="res", bufs=4)
+            nc.scalar.copy(res[:], acc[:].rearrange("r (t p) -> r p t", t=PACK))
+            nc.sync.dma_start(out=out[m * P : (m + 1) * P, :], in_=res[:].rearrange("r p t -> r (p t)"))
+
+        scores(0)
+        quantise_x(2)
+        quantise_x(3)
+        turn_plane(PACK - 1, grad_banks[1][:].rearrange("q s p -> q (s p)"), staging[3])
+        adv_term(0)
+        softmax_sums(0)
+        scores(1)
+        adv_term(1)
+        softmax_sums(1)
+        scores(2)
+        policy_terms(0)
+        adv_term(2)
+        softmax_sums(2)
+        scores(3)
+        policy_terms(1)
+        adv_term(3)
+        softmax_sums(3)
+        policy_terms(2)
+        finish_g(0)
+        policy_terms(3)
+        for m in range(1, TILES):
+            finish_g(m)
+            rows_gradient(m - 1)
+        rows_gradient(TILES - 1)

@@ -30,41 +30,23 @@ def tile_attend_gpgent_x_kernel(tc, xT, wT, adv, us, ts, wt, be, offs, out):
         stream = ctx.enter_context(tc.tile_pool(name="stream", bufs=1))
         work = ctx.enter_context(tc.tile_pool(name="work", bufs=2))
         psum = ctx.enter_context(tc.psum_pool(name="psum", bufs=1))
-        product_banks = [psum.tile([P, SLOTS], F32, name=f"product{m}") for m in range(TILES)]
         grad_banks = [psum.tile([P, PACK, P], F32, name=f"grad{m}") for m in range(TILES)]
 
         offsets = keep.tile([P, SLOTS // 16], U16, name="offsets")
-        row_vecs = keep.tile([P, P], F32, name="row_vecs")
-        ts_window = stream.tile([P, T], F32, name="window", align_bytes=64)
-        nc.vector.memset(ts_window[:, 0 : T // 2], 0.0)
-        nc.gpsimd.memset(ts_window[:, T // 2 : T], 0.0)
-        nc.gpsimd.memset(row_vecs[:], 0.0)
-        nc.scalar.dma_start(out=ts_window[0:1, :], in_=ts[0:1, :])
+        ts_folded = stream.tile([P, T // P], F32, name="small")
+        nc.sync.dma_start(out=ts_folded[:], in_=ts[0:1, :].rearrange("o (p j) -> (o p) j", p=P))
 
         w_view = wT.rearrange("(p t) c -> p t c", t=PACK)
         x_view = xT.rearrange("(p t) r -> p t r", t=PACK)
+        w_planes = [stream.tile([P, T], F32, name=f"staged{t}", align_bytes=64) for t in range(PACK)]
+        nc.sync.dma_start(out=w_planes[0][:], in_=w_view[:, 0, :])
         nc.sync.dma_start(offsets[:], offs)
-        w_planes = []
-        for t in range(PACK):
-            w_planes.append(stream.tile([P, T], F32, name=f"staged{t}"))
+        for t in range(1, PACK):
             nc.sync.dma_start(out=w_planes[t][:], in_=w_view[:, t, :])
-        for j, vec in enumerate((us, wt, be)):
-            nc.scalar.dma_start(
-                out=row_vecs[j * TILES : (j + 1) * TILES, :], in_=vec.rearrange("(m p) o -> m (p o)", p=P)
-            )
         x_halves = []
         for h in range(2):
-            x_halves.append(stream.tile([P, PACK, R // 2], F32, name=f"staged{h}"))
+            x_halves.append(stream.tile([P, PACK, R // 2], F32, name=f"staged{2 * h}", align_bytes=64))
             nc.sync.dma_start(out=x_halves[h][:], in_=x_view[:, :, h * (R // 2) : (h + 1) * (R // 2)])
-        adv_tiles = []
-        for h in range(2):
-            pair = stream.tile([P, 2 * SLOTS], F32, name=f"staged{2 + h}")
-            nc.sync.dma_start(
-                out=pair[:].rearrange("p (e i) -> p e i", e=2),
-                in_=adv[2 * h * P : 2 * (h + 1) * P, :].rearrange("(e p) i -> p e i", e=2),
-            )
-            adv_tiles.extend(pair[:, e * SLOTS : (e + 1) * SLOTS] for e in range(2))
-
         ident32 = keep.tile([P, P], F32, name="ident32")
         make_identity(nc, ident32[:])
         ident16 = keep.tile([P, P], BF16, name="ident16")
@@ -73,62 +55,77 @@ def tile_attend_gpgent_x_kernel(tc, xT, wT, adv, us, ts, wt, be, offs, out):
         warm = keep.tile([P, 1], F32, name="warm")
         nc.scalar.activation(warm[:], ident32[:, 0:1], ACT.Exp)
 
+        ts_window = stream.tile([P, T], F32, name="window", align_bytes=64)
+        window_view = ts_window[:].rearrange("m (p j) -> m p j", p=P)
+        for a in range(T // P // PACK):
+            spread = psum.tile([P, PACK, P], F32, name=f"product{a}")
+            for j in range(PACK):
+                col = a * PACK + j
+                nc.tensor.transpose(spread[:, j, :], ts_folded[:, col : col + 1].to_broadcast([P, P]), ident32[:])
+            nc.scalar.copy(window_view[:, :, a * PACK : (a + 1) * PACK], spread[:].rearrange("m j p -> m p j"))
+        product_banks = [psum.tile([P, SLOTS], F32, name=f"product{m}") for m in range(TILES)]
+        row_vecs = stream.tile([P, P], F32, name="small")
+        nc.gpsimd.memset(row_vecs[:], 0.0)
+        for j, vec in enumerate((us, wt, be)):
+            nc.sync.dma_start(
+                out=row_vecs[j * TILES : (j + 1) * TILES, :], in_=vec.rearrange("(m p) o -> m (p o)", p=P)
+            )
         ts_listed = keep.tile([P, SLOTS], F32, name="ts_listed")
         nc.vector.tensor_copy(ts_listed[:], ts_window[:].indirect(offsets[:]))
-        turned = grad_banks[0]
+        ts_rows = keep.tile([P, PACK, P], F32, name="ts_rows")
+        nc.scalar.copy(ts_rows[:].rearrange("m s q -> m q s"), ts_listed[:].rearrange("m (q s) -> m q s", s=PACK))
+        turned = grad_banks[2]
         for s in range(PACK):
-            nc.tensor.transpose(turned[:, s, :], ts_listed[:, s::PACK], ident32[:])
+            nc.tensor.transpose(turned[:, s, :], ts_rows[:, s, :], ident32[:])
         ts_cols = keep.tile([P, PACK], F32, name="ts_cols")
         nc.scalar.copy(ts_cols[:], turned[:, :, 0])
-        spread = grad_banks[1]
-        for s in range(PACK):
-            nc.tensor.transpose(spread[:, s, :], ts_cols[:, s : s + 1].to_broadcast([P, P]), ident32[:])
-        ts_rows = keep.tile([P, PACK, P], F32, name="ts_rows")
-        nc.scalar.copy(ts_rows[:], spread[:])
 
-        vec_ps = product_banks[1][:, 0:P]
-        nc.tensor.transpose(vec_ps, row_vecs[:], ident32[:])
-        vec_cols = keep.tile([P, 3 * TILES], F32, name="vec_cols")
-        nc.scalar.copy(vec_cols[:], vec_ps[:, 0 : 3 * TILES])
-        us_cols = vec_cols[:, 0:TILES]
-        adv_scale = keep.tile([P, TILES], F32, name="adv_scale")
-        us_wt = keep.tile([P, TILES], F32, name="us_wt")
-        nc.gpsimd.tensor_tensor(us_wt[:], us_cols, vec_cols[:, TILES : 2 * TILES], ALU.mult)
-        nc.gpsimd.tensor_scalar(adv_scale[:], us_wt[:], -1.0, 0.0, ALU.mult, ALU.add)
-        consts = keep.tile([P, TILES, 8], F32, name="consts")
-        nc.gpsimd.memset(consts[:], -1.0)
-        nc.gpsimd.tensor_tensor(consts[:, :, 1], us_cols, vec_cols[:, 2 * TILES : 3 * TILES], ALU.mult)
-
-        w_by_d = stream.tile([P, SLOTS, PACK], BF16, name="window", align_bytes=64)
+        w_by_d = stream.tile([P, PACK, P, PACK], BF16, name="window", align_bytes=64)
+        low_planes = stream.tile([P, 2 * SLOTS], BF16, name="low_planes", align_bytes=64)[:]
         wd_codes = keep.tile([P, SLOTS], U32, name="wd_codes", align_bytes=64)
         wd_scales = keep.tile([P, SLOTS], U8, name="wd_scales", align_bytes=64)
-        wi_codes = keep.tile([P, D], U32, name="wi_codes", align_bytes=64)
         wi_scales = keep.tile([P, D], U8, name="wi_scales", align_bytes=64)
 
         def gather_plane(t):
-            nc.vector.tensor_copy(w_by_d[:, :, t], w_planes[t][:].indirect(offsets[:]))
+            nc.vector.tensor_copy(w_by_d[:, :, :, t].rearrange("p s q -> p q s"), w_planes[t][:].indirect(offsets[:]))
 
-        staging = [keep.tile([P, P, PACK], BF16, name=f"staging{j}", align_bytes=64) for j in range(TILES)]
+        x_grouped = [stream.tile([P, P, PACK], BF16, name=f"x_grouped{m}", align_bytes=64) for m in range(TILES)]
+
+        def low_pair():
+            for t in range(2):
+                nc.vector.tensor_copy(low_planes[:, t * SLOTS : (t + 1) * SLOTS], w_planes[t][:].indirect(offsets[:]))
+            words = low_planes.bitcast(F32)
+            bank = grad_banks[0]
+            for t in range(2):
+                for u in range(2):
+                    first = t * (SLOTS // 2) + u
+                    nc.tensor.transpose(bank[:, 2 * t + u, :], words[:, first : (t + 1) * (SLOTS // 2) : 2], ident32[:])
+            nc.scalar.copy(w_by_d[:, :, :, 0:2], low_planes.rearrange("p (t q s) -> p s q t", t=2, s=PACK))
+            w_by_i = keep.tile([P, 2 * P * PACK], BF16, name="low_by_i", align_bytes=64)
+            nc.scalar.copy(
+                w_by_i[:].bitcast(F32).rearrange("q (t p u) -> q t p u", t=2, u=2),
+                bank[:].rearrange("q (t u) p -> q t p u", t=2),
+            )
+            return w_by_i
 
         def turn_plane(t, bank32, w_by_i):
             bank = bank32.bitcast(BF16)[:, 0 : PACK * P].rearrange("q (s p) -> q s p", s=PACK)
             for s in range(PACK):
-                nc.tensor.transpose(bank[:, s, :], w_by_d[:, s::PACK, t], ident16[:])
+                nc.tensor.transpose(bank[:, s, :], w_by_d[:, s, :, t], ident16[:])
             nc.scalar.copy(w_by_i[:], bank.rearrange("q s p -> q p s"))
-            cols = slice(t * P, (t + 1) * P)
-            nc.vector.quantize_mx(
-                out=wi_codes[:, cols].bitcast(E4M3),
-                scales=wi_scales[:, cols],
-                in_=w_by_i[:].rearrange("q p s -> q (p s)"),
-            )
+
+        def quantise_by_slot(first, planes, w_by_i):
+            cols = slice(first * P, (first + planes) * P)
+            nc.vector.quantize_mx(out=wi_codes[:, cols].bitcast(E4M3), scales=wi_scales[:, cols], in_=w_by_i)
 
         x_codes = [keep.tile([P, P], U32, name=f"x_codes{m}", align_bytes=64) for m in range(TILES)]
         x_scales = [keep.tile([P, P], U8, name=f"x_scales{m}", align_bytes=64) for m in range(TILES)]
 
         def quantise_x(m):
             h, e = divmod(m, 2)
-            grouped = work.tile([P, P, PACK], BF16, name="x_grouped", align_bytes=64, bufs=4)
-            nc.scalar.copy(
+            grouped = x_grouped[m]
+            cast = nc.scalar.copy if m < 2 else nc.vector.tensor_copy
+            cast(
                 grouped[:].rearrange("p (c i) t -> p c t i", i=4),
                 x_halves[h][:, :, e * P : (e + 1) * P].rearrange("p t (c i) -> p c t i", i=4),
             )
@@ -138,16 +135,34 @@ def tile_attend_gpgent_x_kernel(tc, xT, wT, adv, us, ts, wt, be, offs, out):
                 in_=grouped[:].rearrange("p r t -> p (r t)"),
             )
 
-        for t in range(PACK - 1):
-            gather_plane(t)
-            turn_plane(t, grad_banks[t % 2][:].rearrange("q s p -> q (s p)"), staging[t])
+        low_by_i = low_pair()
+        vec_ps = grad_banks[2][:, 0, :]
+        nc.tensor.transpose(vec_ps, row_vecs[:], ident32[:])
+        vec_cols = keep.tile([P, 3 * TILES], F32, name="vec_cols")
+        nc.vector.tensor_copy(vec_cols[:], vec_ps[:, 0 : 3 * TILES])
+        us_cols = vec_cols[:, 0:TILES]
+        adv_scale = keep.tile([P, TILES], F32, name="adv_scale")
+        us_wt = keep.tile([P, TILES], F32, name="us_wt")
+        nc.gpsimd.tensor_tensor(us_wt[:], us_cols, vec_cols[:, TILES : 2 * TILES], ALU.mult)
+        nc.gpsimd.tensor_scalar(adv_scale[:], us_wt[:], -1.0, 0.0, ALU.mult, ALU.add)
+        consts = keep.tile([P, TILES, 2], F32, name="consts")
+        nc.gpsimd.memset(consts[:], -1.0)
+        nc.gpsimd.tensor_tensor(consts[:, :, 1], us_cols, vec_cols[:, 2 * TILES : 3 * TILES], ALU.mult)
+
+        gather_plane(2)
+        adv_tiles = []
+        for h in range(2):
+            pair = stream.tile([P, 2 * SLOTS], F32, name=("low_planes", "staged0")[h], align_bytes=64)
+            nc.sync.dma_start(
+                out=pair[:].rearrange("p (e i) -> p e i", e=2),
+                in_=adv[2 * h * P : 2 * (h + 1) * P, :].rearrange("(e p) i -> p e i", e=2),
+            )
+            adv_tiles.extend(pair[:, e * SLOTS : (e + 1) * SLOTS] for e in range(2))
+
         gather_plane(PACK - 1)
         nc.vector.quantize_mx(
-            out=wd_codes[:].bitcast(E4M3), scales=wd_scales[:], in_=w_by_d[:].rearrange("p i t -> p (i t)")
+            out=wd_codes[:].bitcast(E4M3), scales=wd_scales[:], in_=w_by_d[:].rearrange("p s q t -> p (s q t)")
         )
-        quantise_x(0)
-        quantise_x(1)
-
         state = {}
 
         def add_turned(m, src, first, last):
@@ -174,7 +189,7 @@ def tile_attend_gpgent_x_kernel(tc, xT, wT, adv, us, ts, wt, be, offs, out):
             )
             z = work.tile([P, PACK, P], F32, name="z", bufs=4)
             nc.vector.scalar_tensor_tensor(
-                z[:], acc[:].rearrange("r (q s) -> r s q", s=PACK), us_cols[:, m : m + 1], ts_rows[:],
+                z[:], acc[:].rearrange("r (s q) -> r s q", s=PACK), us_cols[:, m : m + 1], ts_rows[:],
                 ALU.mult, ALU.mult,
             )
             state["z", m] = z
@@ -186,12 +201,14 @@ def tile_attend_gpgent_x_kernel(tc, xT, wT, adv, us, ts, wt, be, offs, out):
             e = work.tile([P, PACK, P], F32, name="e", bufs=4)
             tot = work.tile([P, 1], F32, name="tot", bufs=4)
             nc.scalar.activation(e[:], z[:], ACT.Exp, bias=neg_max[:], accum_out=tot[:])
+            state["neg_max", m] = neg_max
             state["e", m] = e
             state["tot", m] = tot
 
         def adv_term(m):
-            term = work.tile([P, PACK, P], F32, name="adv_term")
+            term = work.tile([P, PACK, P], F32, name="adv_term", bufs=4)
             adv_sum = work.tile([P, 1], F32, name="adv_sum", bufs=4)
+            state["adv_sum", m] = adv_sum
             nc.scalar.activation(
                 term[:].rearrange("r s q -> r q s"),
                 adv_tiles[m].rearrange("r (q s) -> r q s", s=PACK),
@@ -199,7 +216,6 @@ def tile_attend_gpgent_x_kernel(tc, xT, wT, adv, us, ts, wt, be, offs, out):
                 scale=adv_scale[:, m : m + 1],
                 accum_out=adv_sum[:],
             )
-            nc.gpsimd.tensor_scalar(consts[:, m, 2:3], adv_sum[:], -1.0, 0.0, ALU.mult, ALU.add)
             state["grad", m] = grad_banks[m]
             add_turned(m, term, True, False)
 
@@ -207,16 +223,19 @@ def tile_attend_gpgent_x_kernel(tc, xT, wT, adv, us, ts, wt, be, offs, out):
             z, e = state["z", m], state["e", m]
             inv = work.tile([P, 1], F32, name="inv", bufs=4)
             nc.vector.reciprocal(inv[:], state["tot", m][:])
-            scaled = work.tile([P, 3], F32, name="scaled", bufs=4)
-            nc.scalar.activation(scaled[:], consts[:, m, 0:3], ACT.Copy, scale=inv[:])
-            ze = work.tile([P, PACK, P], F32, name="ze")
+            scaled = work.tile([P, 2], F32, name="scaled", bufs=4)
+            nc.vector.tensor_scalar(scaled[:], consts[:, m, :], inv[:], None, ALU.mult)
+            ze = work.tile([P, PACK, P], F32, name="ze", bufs=4)
             ze_sum = work.tile([P, 1], F32, name="ze_sum", bufs=4)
             nc.vector.scalar_tensor_tensor(ze[:], z[:], scaled[:, 1:2], e[:], ALU.mult, ALU.mult, accum_out=ze_sum[:])
             add_turned(m, ze, False, False)
             e_scale = work.tile([P, 1], F32, name="e_scale", bufs=4)
-            nc.scalar.activation(e_scale[:], ze_sum[:], ACT.Identity, scale=scaled[:, 0:1], bias=scaled[:, 2:3])
-            e_term = work.tile([P, PACK, P], F32, name="e_term")
-            nc.scalar.activation(e_term[:], e[:], ACT.Copy, scale=e_scale[:])
+            nc.vector.tensor_scalar(e_scale[:], ze_sum[:], state["adv_sum", m][:], scaled[:, 0:1], ALU.add, ALU.mult)
+            e_term = work.tile([P, PACK, P], F32, name="e_term", bufs=4)
+            pieces = 2 if m == TILES - 1 else 1
+            for j in range(pieces):
+                part = slice(j * PACK // pieces, (j + 1) * PACK // pieces)
+                nc.scalar.activation(e_term[:, part, :], e[:, part, :], ACT.Copy, scale=e_scale[:])
             add_turned(m, e_term, False, True)
 
         def finish_g(m):
@@ -246,30 +265,46 @@ def tile_attend_gpgent_x_kernel(tc, xT, wT, adv, us, ts, wt, be, offs, out):
                 stop=True,
             )
             res = work.tile([P, P, PACK], F32, name="res", bufs=4)
-            nc.scalar.copy(res[:], acc[:].rearrange("r (t p) -> r p t", t=PACK))
-            nc.sync.dma_start(out=out[m * P : (m + 1) * P, :], in_=res[:].rearrange("r p t -> r (p t)"))
+            pieces = 2 if m == TILES - 1 else 1
+            for j in range(pieces):
+                part = slice(j * P // pieces, (j + 1) * P // pieces)
+                nc.scalar.copy(res[:, part, :], acc[:].rearrange("r (t p) -> r p t", t=PACK)[:, part, :])
+                nc.sync.dma_start(
+                    out=out[m * P : (m + 1) * P, j * D // pieces : (j + 1) * D // pieces],
+                    in_=res[:, part, :].rearrange("r p t -> r (p t)"),
+                )
 
-        scores(0)
+        quantise_x(0)
+        quantise_x(1)
+        wi_codes = stream.tile([P, D], U32, name="x_grouped0", align_bytes=64)
         quantise_x(2)
         quantise_x(3)
-        turn_plane(PACK - 1, grad_banks[1][:].rearrange("q s p -> q (s p)"), staging[3])
-        adv_term(0)
+        scores(0)
         softmax_sums(0)
         scores(1)
-        adv_term(1)
         softmax_sums(1)
         scores(2)
-        policy_terms(0)
-        adv_term(2)
         softmax_sums(2)
+        turn_plane(2, grad_banks[1][:].rearrange("q s p -> q (s p)"), x_grouped[1])
+        adv_term(0)
+        policy_terms(0)
         scores(3)
-        policy_terms(1)
-        adv_term(3)
         softmax_sums(3)
+        adv_term(1)
+        policy_terms(1)
+        turn_plane(3, product_banks[2][:], x_grouped[2])
+        adv_term(2)
+        adv_term(3)
         policy_terms(2)
-        finish_g(0)
         policy_terms(3)
-        for m in range(1, TILES):
-            finish_g(m)
-            rows_gradient(m - 1)
-        rows_gradient(TILES - 1)
+        finish_g(0)
+        quantise_by_slot(0, 2, low_by_i[:])
+        quantise_by_slot(2, 1, x_grouped[1][:].rearrange("q p s -> q (p s)"))
+        quantise_by_slot(3, 1, x_grouped[2][:].rearrange("q p s -> q (p s)"))
+        finish_g(1)
+        rows_gradient(0)
+        finish_g(2)
+        rows_gradient(1)
+        finish_g(3)
+        rows_gradient(2)
+        rows_gradient(3)

@@ -45,7 +45,7 @@ def tile_attend_gpgent_x_kernel(tc, xT, wT, adv, us, ts, wt, be, offs, out):
             nc.sync.dma_start(out=w_planes[t][:], in_=w_view[:, t, :])
         x_halves = []
         for h in range(2):
-            x_halves.append(stream.tile([P, PACK, R // 2], F32, name=f"staged{2 * h}", align_bytes=64))
+            x_halves.append(stream.tile([P, PACK, R // 2], F32, name=f"staged{h}", align_bytes=64))
             nc.sync.dma_start(out=x_halves[h][:], in_=x_view[:, :, h * (R // 2) : (h + 1) * (R // 2)])
         ident32 = keep.tile([P, P], F32, name="ident32")
         make_identity(nc, ident32[:])
@@ -80,14 +80,14 @@ def tile_attend_gpgent_x_kernel(tc, xT, wT, adv, us, ts, wt, be, offs, out):
         ts_cols = keep.tile([P, PACK], F32, name="ts_cols")
         nc.scalar.copy(ts_cols[:], turned[:, :, 0])
 
-        w_by_d = stream.tile([P, PACK, P, PACK], BF16, name="window", align_bytes=64)
+        w_by_d = stream.tile([P, SLOTS, PACK], BF16, name="window", align_bytes=64)
         low_planes = stream.tile([P, 2 * SLOTS], BF16, name="low_planes", align_bytes=64)[:]
         wd_codes = keep.tile([P, SLOTS], U32, name="wd_codes", align_bytes=64)
         wd_scales = keep.tile([P, SLOTS], U8, name="wd_scales", align_bytes=64)
         wi_scales = keep.tile([P, D], U8, name="wi_scales", align_bytes=64)
 
         def gather_plane(t):
-            nc.vector.tensor_copy(w_by_d[:, :, :, t].rearrange("p s q -> p q s"), w_planes[t][:].indirect(offsets[:]))
+            nc.vector.tensor_copy(w_by_d[:, :, t], w_planes[t][:].indirect(offsets[:]))
 
         x_grouped = [stream.tile([P, P, PACK], BF16, name=f"x_grouped{m}", align_bytes=64) for m in range(TILES)]
 
@@ -100,7 +100,7 @@ def tile_attend_gpgent_x_kernel(tc, xT, wT, adv, us, ts, wt, be, offs, out):
                 for u in range(2):
                     first = t * (SLOTS // 2) + u
                     nc.tensor.transpose(bank[:, 2 * t + u, :], words[:, first : (t + 1) * (SLOTS // 2) : 2], ident32[:])
-            nc.scalar.copy(w_by_d[:, :, :, 0:2], low_planes.rearrange("p (t q s) -> p s q t", t=2, s=PACK))
+            nc.scalar.copy(w_by_d[:, :, 0:2], low_planes.rearrange("p (t i) -> p i t", t=2))
             w_by_i = keep.tile([P, 2 * P * PACK], BF16, name="low_by_i", align_bytes=64)
             nc.scalar.copy(
                 w_by_i[:].bitcast(F32).rearrange("q (t p u) -> q t p u", t=2, u=2),
@@ -111,7 +111,7 @@ def tile_attend_gpgent_x_kernel(tc, xT, wT, adv, us, ts, wt, be, offs, out):
         def turn_plane(t, bank32, w_by_i):
             bank = bank32.bitcast(BF16)[:, 0 : PACK * P].rearrange("q (s p) -> q s p", s=PACK)
             for s in range(PACK):
-                nc.tensor.transpose(bank[:, s, :], w_by_d[:, s, :, t], ident16[:])
+                nc.tensor.transpose(bank[:, s, :], w_by_d[:, s::PACK, t], ident16[:])
             nc.scalar.copy(w_by_i[:], bank.rearrange("q s p -> q p s"))
 
         def quantise_by_slot(first, planes, w_by_i):
@@ -124,7 +124,7 @@ def tile_attend_gpgent_x_kernel(tc, xT, wT, adv, us, ts, wt, be, offs, out):
         def quantise_x(m):
             h, e = divmod(m, 2)
             grouped = x_grouped[m]
-            cast = nc.scalar.copy if m < 2 else nc.vector.tensor_copy
+            cast = nc.scalar.copy if m < 4 else nc.vector.tensor_copy
             cast(
                 grouped[:].rearrange("p (c i) t -> p c t i", i=4),
                 x_halves[h][:, :, e * P : (e + 1) * P].rearrange("p t (c i) -> p c t i", i=4),
@@ -161,7 +161,7 @@ def tile_attend_gpgent_x_kernel(tc, xT, wT, adv, us, ts, wt, be, offs, out):
 
         gather_plane(PACK - 1)
         nc.vector.quantize_mx(
-            out=wd_codes[:].bitcast(E4M3), scales=wd_scales[:], in_=w_by_d[:].rearrange("p s q t -> p (s q t)")
+            out=wd_codes[:].bitcast(E4M3), scales=wd_scales[:], in_=w_by_d[:].rearrange("p i t -> p (i t)")
         )
         state = {}
 
@@ -189,7 +189,7 @@ def tile_attend_gpgent_x_kernel(tc, xT, wT, adv, us, ts, wt, be, offs, out):
             )
             z = work.tile([P, PACK, P], F32, name="z", bufs=4)
             nc.vector.scalar_tensor_tensor(
-                z[:], acc[:].rearrange("r (s q) -> r s q", s=PACK), us_cols[:, m : m + 1], ts_rows[:],
+                z[:], acc[:].rearrange("r (q s) -> r s q", s=PACK), us_cols[:, m : m + 1], ts_rows[:],
                 ALU.mult, ALU.mult,
             )
             state["z", m] = z

@@ -21,50 +21,53 @@ AX = mybir.AxisListType
 P = 128
 PACK = 4
 TILES = R // P
+FOLD = T // P
+LINE = 4
+LEAD = 2
+LAST_PIECES = 2
 
 
 def tile_attend_gpgent_x_kernel(tc, xT, wT, adv, us, ts, wt, be, offs, out):
     nc = tc.nc
     with ExitStack() as ctx:
         keep = ctx.enter_context(tc.tile_pool(name="keep", bufs=1))
-        stream = ctx.enter_context(tc.tile_pool(name="stream", bufs=1))
+        reuse = ctx.enter_context(tc.tile_pool(name="reuse", bufs=1))
         work = ctx.enter_context(tc.tile_pool(name="work", bufs=2))
         psum = ctx.enter_context(tc.psum_pool(name="psum", bufs=1))
         grad_banks = [psum.tile([P, PACK, P], F32, name=f"grad{m}") for m in range(TILES)]
 
         offsets = keep.tile([P, SLOTS // 16], U16, name="offsets")
-        ts_folded = stream.tile([P, T // P], F32, name="small")
+        ts_folded = reuse.tile([P, FOLD], F32, name="small")
         nc.sync.dma_start(out=ts_folded[:], in_=ts[0:1, :].rearrange("o (p j) -> (o p) j", p=P))
 
         w_view = wT.rearrange("(p t) c -> p t c", t=PACK)
         x_view = xT.rearrange("(p t) r -> p t r", t=PACK)
-        w_planes = [stream.tile([P, T], F32, name=f"staged{t}", align_bytes=64) for t in range(PACK)]
+        w_planes = [reuse.tile([P, T], F32, name=f"staged{t}", align_bytes=64) for t in range(PACK)]
         nc.sync.dma_start(out=w_planes[0][:], in_=w_view[:, 0, :])
         nc.sync.dma_start(offsets[:], offs)
         for t in range(1, PACK):
             nc.sync.dma_start(out=w_planes[t][:], in_=w_view[:, t, :])
         x_halves = []
         for h in range(2):
-            x_halves.append(stream.tile([P, PACK, R // 2], F32, name=f"staged{h}", align_bytes=64))
+            x_halves.append(reuse.tile([P, PACK, R // 2], F32, name=f"staged{h}", align_bytes=64))
             nc.sync.dma_start(out=x_halves[h][:], in_=x_view[:, :, h * (R // 2) : (h + 1) * (R // 2)])
         ident32 = keep.tile([P, P], F32, name="ident32")
         make_identity(nc, ident32[:])
         ident16 = keep.tile([P, P], BF16, name="ident16")
         make_identity(nc, ident16[:])
 
-        warm = keep.tile([P, 1], F32, name="warm")
-        nc.scalar.activation(warm[:], ident32[:, 0:1], ACT.Exp)
-
-        ts_window = stream.tile([P, T], F32, name="window", align_bytes=64)
+        ts_window = reuse.tile([P, T], F32, name="window", align_bytes=64)
         window_view = ts_window[:].rearrange("m (p j) -> m p j", p=P)
-        for a in range(T // P // PACK):
+        for a in range(FOLD // PACK):
             spread = psum.tile([P, PACK, P], F32, name=f"product{a}")
             for j in range(PACK):
                 col = a * PACK + j
                 nc.tensor.transpose(spread[:, j, :], ts_folded[:, col : col + 1].to_broadcast([P, P]), ident32[:])
-            nc.scalar.copy(window_view[:, :, a * PACK : (a + 1) * PACK], spread[:].rearrange("m j p -> m p j"))
+            nc.scalar.activation(
+                window_view[:, :, a * PACK : (a + 1) * PACK], spread[:].rearrange("m j p -> m p j"), ACT.Copy
+            )
         product_banks = [psum.tile([P, SLOTS], F32, name=f"product{m}") for m in range(TILES)]
-        row_vecs = stream.tile([P, P], F32, name="small")
+        row_vecs = reuse.tile([P, P], F32, name="small")
         nc.gpsimd.memset(row_vecs[:], 0.0)
         for j, vec in enumerate((us, wt, be)):
             nc.sync.dma_start(
@@ -74,112 +77,110 @@ def tile_attend_gpgent_x_kernel(tc, xT, wT, adv, us, ts, wt, be, offs, out):
         nc.vector.tensor_copy(ts_listed[:], ts_window[:].indirect(offsets[:]))
         ts_rows = keep.tile([P, PACK, P], F32, name="ts_rows")
         nc.scalar.copy(ts_rows[:].rearrange("m s q -> m q s"), ts_listed[:].rearrange("m (q s) -> m q s", s=PACK))
-        turned = grad_banks[2]
         for s in range(PACK):
-            nc.tensor.transpose(turned[:, s, :], ts_rows[:, s, :], ident32[:])
+            nc.tensor.transpose(grad_banks[2][:, s, :], ts_rows[:, s, :], ident32[:])
         ts_cols = keep.tile([P, PACK], F32, name="ts_cols")
-        nc.scalar.copy(ts_cols[:], turned[:, :, 0])
+        nc.scalar.copy(ts_cols[:], grad_banks[2][:, :, 0])
 
-        w_by_d = stream.tile([P, SLOTS, PACK], BF16, name="window", align_bytes=64)
-        low_planes = stream.tile([P, 2 * SLOTS], BF16, name="low_planes", align_bytes=64)[:]
+        gathered = reuse.tile([P, (PACK + 2) * SLOTS], BF16, name="window", align_bytes=64)
+        w_by_d = gathered[:, 0 : PACK * SLOTS].rearrange("p (i t) -> p i t", t=PACK)
+        low_planes = gathered[:, PACK * SLOTS : (PACK + 2) * SLOTS]
         wd_codes = keep.tile([P, SLOTS], U32, name="wd_codes", align_bytes=64)
         wd_scales = keep.tile([P, SLOTS], U8, name="wd_scales", align_bytes=64)
+        wi_codes = keep.tile([P, D], U32, name="wi_codes", align_bytes=64)
         wi_scales = keep.tile([P, D], U8, name="wi_scales", align_bytes=64)
-
-        def gather_plane(t):
-            nc.vector.tensor_copy(w_by_d[:, :, t], w_planes[t][:].indirect(offsets[:]))
-
-        x_grouped = [stream.tile([P, P, PACK], BF16, name=f"x_grouped{m}", align_bytes=64) for m in range(TILES)]
-
-        def low_pair():
-            for t in range(2):
-                nc.vector.tensor_copy(low_planes[:, t * SLOTS : (t + 1) * SLOTS], w_planes[t][:].indirect(offsets[:]))
-            words = low_planes.bitcast(F32)
-            bank = grad_banks[0]
-            for t in range(2):
-                for u in range(2):
-                    first = t * (SLOTS // 2) + u
-                    nc.tensor.transpose(bank[:, 2 * t + u, :], words[:, first : (t + 1) * (SLOTS // 2) : 2], ident32[:])
-            nc.scalar.copy(w_by_d[:, :, 0:2], low_planes.rearrange("p (t i) -> p i t", t=2))
-            w_by_i = keep.tile([P, 2 * P * PACK], BF16, name="low_by_i", align_bytes=64)
-            nc.scalar.copy(
-                w_by_i[:].bitcast(F32).rearrange("q (t p u) -> q t p u", t=2, u=2),
-                bank[:].rearrange("q (t u) p -> q t p u", t=2),
-            )
-            return w_by_i
-
-        def turn_plane(t, bank32, w_by_i):
-            bank = bank32.bitcast(BF16)[:, 0 : PACK * P].rearrange("q (s p) -> q s p", s=PACK)
-            for s in range(PACK):
-                nc.tensor.transpose(bank[:, s, :], w_by_d[:, s::PACK, t], ident16[:])
-            nc.scalar.copy(w_by_i[:], bank.rearrange("q s p -> q p s"))
-
-        def quantise_by_slot(first, planes, w_by_i):
-            cols = slice(first * P, (first + planes) * P)
-            nc.vector.quantize_mx(out=wi_codes[:, cols].bitcast(E4M3), scales=wi_scales[:, cols], in_=w_by_i)
-
+        x_grouped = [reuse.tile([P, P, PACK], BF16, name=f"x_grouped{m}", align_bytes=64) for m in range(2)]
         x_codes = [keep.tile([P, P], U32, name=f"x_codes{m}", align_bytes=64) for m in range(TILES)]
         x_scales = [keep.tile([P, P], U8, name=f"x_scales{m}", align_bytes=64) for m in range(TILES)]
 
-        def quantise_x(m):
-            h, e = divmod(m, 2)
-            grouped = x_grouped[m]
-            cast = nc.scalar.copy if m < 4 else nc.vector.tensor_copy
-            cast(
-                grouped[:].rearrange("p (c i) t -> p c t i", i=4),
-                x_halves[h][:, :, e * P : (e + 1) * P].rearrange("p t (c i) -> p c t i", i=4),
+        def transpose_pairs(bank, plane):
+            words = plane.bitcast(F32)
+            for u in range(2):
+                nc.tensor.transpose(bank[:, u, :], words[:, u::2], ident32[:])
+
+        for t in range(2):
+            nc.vector.tensor_copy(low_planes[:, t * SLOTS : (t + 1) * SLOTS], w_planes[t][:].indirect(offsets[:]))
+        for t in range(2):
+            transpose_pairs(grad_banks[0][:, 2 * t : 2 * t + 2, :], low_planes[:, t * SLOTS : (t + 1) * SLOTS])
+        nc.scalar.copy(w_by_d[:, :, 0:2], low_planes.rearrange("p (t i) -> p i t", t=2))
+        low_by_i = keep.tile([P, 2 * P * PACK], BF16, name="low_by_i", align_bytes=64)
+        nc.scalar.copy(
+            low_by_i[:].bitcast(F32).rearrange("q (t p u) -> q t p u", t=2, u=2),
+            grad_banks[0][:].rearrange("q (t u) p -> q t p u", t=2),
+        )
+
+        nc.tensor.transpose(grad_banks[0][:, 0, :], row_vecs[:], ident32[:])
+        vec_cols = keep.tile([P, 3 * TILES], F32, name="vec_cols")
+        nc.vector.tensor_copy(vec_cols[:], grad_banks[0][:, 0, 0 : 3 * TILES])
+        us_cols = vec_cols[:, 0:TILES]
+        adv_scale = keep.tile([P, TILES], F32, name="adv_scale")
+        us_wt = keep.tile([P, TILES], F32, name="us_wt")
+        nc.gpsimd.tensor_tensor(us_wt[:], us_cols, vec_cols[:, TILES : 2 * TILES], ALU.mult)
+        nc.gpsimd.tensor_scalar(adv_scale[:], us_wt[:], -1.0, 0.0, ALU.mult, ALU.add)
+        numerators = keep.tile([P, TILES, 2], F32, name="numerators")
+        nc.gpsimd.memset(numerators[:], -1.0)
+        nc.gpsimd.tensor_tensor(numerators[:, :, 1], us_cols, vec_cols[:, 2 * TILES : 3 * TILES], ALU.mult)
+
+        nc.vector.tensor_copy(w_by_d[:, :, 2], w_planes[2][:].indirect(offsets[:]))
+        adv_tiles = []
+        for h in range(2):
+            pair = reuse.tile([P, 2 * SLOTS], F32, name=f"staged{2 + h}", align_bytes=64)
+            nc.sync.dma_start(
+                out=pair[:].rearrange("p (e i) -> p e i", e=2),
+                in_=adv[2 * h * P : 2 * (h + 1) * P, :].rearrange("(e p) i -> p e i", e=2),
             )
+            adv_tiles.extend(pair[:, e * SLOTS : (e + 1) * SLOTS] for e in range(2))
+        nc.vector.tensor_copy(w_by_d[:, :, 3], w_planes[3][:].indirect(offsets[:]))
+        nc.vector.quantize_mx(out=wd_codes[:].bitcast(E4M3), scales=wd_scales[:], in_=gathered[:, 0 : PACK * SLOTS])
+
+        for m in range(TILES):
+            h, e = divmod(m, 2)
+            grouped = x_grouped[e]
+            src = x_halves[h][:, :, e * P : (e + 1) * P]
+            if h == 0:
+                nc.scalar.copy(
+                    grouped[:].rearrange("p (c i) t -> p c t i", i=LINE),
+                    src.rearrange("p t (c i) -> p c t i", i=LINE),
+                )
+            else:
+                nc.vector.tensor_copy(grouped[:], src.rearrange("p t r -> p r t"))
             nc.vector.quantize_mx(
                 out=x_codes[m][:].bitcast(E4M3),
                 scales=x_scales[m][:],
                 in_=grouped[:].rearrange("p r t -> p (r t)"),
             )
 
-        low_by_i = low_pair()
-        vec_ps = grad_banks[2][:, 0, :]
-        nc.tensor.transpose(vec_ps, row_vecs[:], ident32[:])
-        vec_cols = keep.tile([P, 3 * TILES], F32, name="vec_cols")
-        nc.vector.tensor_copy(vec_cols[:], vec_ps[:, 0 : 3 * TILES])
-        us_cols = vec_cols[:, 0:TILES]
-        adv_scale = keep.tile([P, TILES], F32, name="adv_scale")
-        us_wt = keep.tile([P, TILES], F32, name="us_wt")
-        nc.gpsimd.tensor_tensor(us_wt[:], us_cols, vec_cols[:, TILES : 2 * TILES], ALU.mult)
-        nc.gpsimd.tensor_scalar(adv_scale[:], us_wt[:], -1.0, 0.0, ALU.mult, ALU.add)
-        consts = keep.tile([P, TILES, 2], F32, name="consts")
-        nc.gpsimd.memset(consts[:], -1.0)
-        nc.gpsimd.tensor_tensor(consts[:, :, 1], us_cols, vec_cols[:, 2 * TILES : 3 * TILES], ALU.mult)
-
-        gather_plane(2)
-        adv_tiles = []
-        for h in range(2):
-            pair = stream.tile([P, 2 * SLOTS], F32, name=("low_planes", "staged0")[h], align_bytes=64)
-            nc.sync.dma_start(
-                out=pair[:].rearrange("p (e i) -> p e i", e=2),
-                in_=adv[2 * h * P : 2 * (h + 1) * P, :].rearrange("(e p) i -> p e i", e=2),
-            )
-            adv_tiles.extend(pair[:, e * SLOTS : (e + 1) * SLOTS] for e in range(2))
-
-        gather_plane(PACK - 1)
-        nc.vector.quantize_mx(
-            out=wd_codes[:].bitcast(E4M3), scales=wd_scales[:], in_=w_by_d[:].rearrange("p i t -> p (i t)")
+        high = reuse.tile([P, 3 * SLOTS], BF16, name="staged0", align_bytes=64)
+        high_by_i = high[:, 0 : 2 * SLOTS]
+        last_plane = high[:, 2 * SLOTS : 3 * SLOTS]
+        bank16 = grad_banks[1][:].rearrange("q s p -> q (s p)").bitcast(BF16)[:, 0 : PACK * P]
+        bank16 = bank16.rearrange("q (s p) -> q s p", s=PACK)
+        for s in range(PACK):
+            nc.tensor.transpose(bank16[:, s, :], w_by_d[:, s::PACK, 2], ident16[:])
+        nc.scalar.copy(high_by_i[:, 0:SLOTS].rearrange("q (p s) -> q p s", s=PACK), bank16.rearrange("q s p -> q p s"))
+        nc.scalar.copy(last_plane, w_by_d[:, :, 3])
+        transpose_pairs(grad_banks[3][:, 0:2, :], last_plane)
+        nc.scalar.copy(
+            high_by_i[:, SLOTS : 2 * SLOTS].bitcast(F32).rearrange("q (p u) -> q p u", u=2),
+            grad_banks[3][:, 0:2, :].rearrange("q u p -> q p u"),
         )
-        state = {}
 
-        def add_turned(m, src, first, last):
+        z_tiles, e_tiles, neg_maxima, totals = [], [], [], []
+
+        def add_transposed(m, term, first, last):
             for s in range(PACK):
                 nc.tensor.matmul(
-                    state["grad", m][:, s, :],
-                    lhsT=src[:, s, :],
+                    grad_banks[m][:, s, :],
+                    lhsT=term[:, s, :],
                     rhs=ident32[:],
                     is_transpose=True,
                     start=(first and s == 0),
                     stop=(last and s == PACK - 1),
                 )
 
-        def scores(m):
-            acc = product_banks[m]
+        def scores_and_exponentials(m):
             nc.tensor.matmul_mx(
-                out=acc[:],
+                out=product_banks[m][:],
                 lhsT=x_codes[m][:].bitcast(E4M3),
                 lhsT_scale=x_scales[m][:],
                 rhs=wd_codes[:].bitcast(E4M3),
@@ -187,76 +188,73 @@ def tile_attend_gpgent_x_kernel(tc, xT, wT, adv, us, ts, wt, be, offs, out):
                 start=True,
                 stop=True,
             )
-            z = work.tile([P, PACK, P], F32, name="z", bufs=4)
+            z = work.tile([P, PACK, P], F32, name="z", bufs=TILES)
             nc.vector.scalar_tensor_tensor(
-                z[:], acc[:].rearrange("r (q s) -> r s q", s=PACK), us_cols[:, m : m + 1], ts_rows[:],
-                ALU.mult, ALU.mult,
+                z[:],
+                product_banks[m][:].rearrange("r (q s) -> r s q", s=PACK),
+                us_cols[:, m : m + 1],
+                ts_rows[:],
+                ALU.mult,
+                ALU.mult,
             )
-            state["z", m] = z
-
-        def softmax_sums(m):
-            z = state["z", m]
-            neg_max = work.tile([P, 1], F32, name="neg_max", bufs=4)
+            neg_max = work.tile([P, 1], F32, name="neg_max", bufs=TILES)
             nc.vector.tensor_reduce(neg_max[:], z[:].rearrange("r s q -> r (s q)"), AX.X, ALU.max, negate=True)
-            e = work.tile([P, PACK, P], F32, name="e", bufs=4)
-            tot = work.tile([P, 1], F32, name="tot", bufs=4)
+            e = work.tile([P, PACK, P], F32, name="e", bufs=TILES)
+            tot = work.tile([P, 1], F32, name="tot", bufs=TILES)
             nc.scalar.activation(e[:], z[:], ACT.Exp, bias=neg_max[:], accum_out=tot[:])
-            state["neg_max", m] = neg_max
-            state["e", m] = e
-            state["tot", m] = tot
+            z_tiles.append(z)
+            e_tiles.append(e)
+            neg_maxima.append(neg_max)
+            totals.append(tot)
 
-        def adv_term(m):
-            term = work.tile([P, PACK, P], F32, name="adv_term", bufs=4)
-            adv_sum = work.tile([P, 1], F32, name="adv_sum", bufs=4)
-            state["adv_sum", m] = adv_sum
+        def gradient_terms(m):
+            z, e = z_tiles[m], e_tiles[m]
+            a_term = work.tile([P, PACK, P], F32, name="a_term", bufs=TILES)
+            a_sum = neg_maxima[m - 2] if m >= 2 else work.tile([P, 1], F32, name="a_sum", bufs=TILES)
             nc.scalar.activation(
-                term[:].rearrange("r s q -> r q s"),
+                a_term[:].rearrange("r s q -> r q s"),
                 adv_tiles[m].rearrange("r (q s) -> r q s", s=PACK),
                 ACT.Copy,
                 scale=adv_scale[:, m : m + 1],
-                accum_out=adv_sum[:],
+                accum_out=a_sum[:],
             )
-            state["grad", m] = grad_banks[m]
-            add_turned(m, term, True, False)
+            add_transposed(m, a_term, True, False)
 
-        def policy_terms(m):
-            z, e = state["z", m], state["e", m]
-            inv = work.tile([P, 1], F32, name="inv", bufs=4)
-            nc.vector.reciprocal(inv[:], state["tot", m][:])
-            scaled = work.tile([P, 2], F32, name="scaled", bufs=4)
-            nc.vector.tensor_scalar(scaled[:], consts[:, m, :], inv[:], None, ALU.mult)
-            ze = work.tile([P, PACK, P], F32, name="ze", bufs=4)
-            ze_sum = work.tile([P, 1], F32, name="ze_sum", bufs=4)
-            nc.vector.scalar_tensor_tensor(ze[:], z[:], scaled[:, 1:2], e[:], ALU.mult, ALU.mult, accum_out=ze_sum[:])
-            add_turned(m, ze, False, False)
-            e_scale = work.tile([P, 1], F32, name="e_scale", bufs=4)
-            nc.vector.tensor_scalar(e_scale[:], ze_sum[:], state["adv_sum", m][:], scaled[:, 0:1], ALU.add, ALU.mult)
-            e_term = work.tile([P, PACK, P], F32, name="e_term", bufs=4)
-            pieces = 2 if m == TILES - 1 else 1
+            inv = work.tile([P, 1], F32, name="inv", bufs=TILES)
+            nc.vector.reciprocal(inv[:], totals[m][:])
+            ratios = work.tile([P, 2], F32, name="ratios", bufs=TILES)
+            nc.vector.tensor_scalar(ratios[:], numerators[:, m, :], inv[:], None, ALU.mult)
+            u_term = work.tile([P, PACK, P], F32, name="u_term", bufs=TILES)
+            u_sum = work.tile([P, 1], F32, name="u_sum", bufs=TILES)
+            nc.vector.scalar_tensor_tensor(
+                u_term[:], z[:], ratios[:, 1:2], e[:], ALU.mult, ALU.mult, accum_out=u_sum[:]
+            )
+            add_transposed(m, u_term, False, False)
+
+            e_scale = work.tile([P, 1], F32, name="e_scale", bufs=TILES)
+            nc.vector.tensor_scalar(e_scale[:], u_sum[:], a_sum[:], ratios[:, 0:1], ALU.add, ALU.mult)
+            e_term = work.tile([P, PACK, P], F32, name="e_term", bufs=TILES)
+            pieces = LAST_PIECES if m == TILES - 1 else 1
             for j in range(pieces):
                 part = slice(j * PACK // pieces, (j + 1) * PACK // pieces)
                 nc.scalar.activation(e_term[:, part, :], e[:, part, :], ACT.Copy, scale=e_scale[:])
-            add_turned(m, e_term, False, True)
+            add_transposed(m, e_term, False, True)
 
-        def finish_g(m):
+        def rows_gradient(m):
             g = work.tile([P, P, PACK], BF16, name="g", align_bytes=64)
             nc.vector.tensor_tensor(
                 g[:],
-                state["grad", m][:].rearrange("q s r -> q r s"),
+                grad_banks[m][:].rearrange("q s r -> q r s"),
                 ts_cols[:].unsqueeze(1).to_broadcast([P, P, PACK]),
                 ALU.mult,
             )
-            state["g", m] = g
-
-        def rows_gradient(m):
             g_codes = work.tile([P, P], U32, name="g_codes", align_bytes=64)
             g_scales = work.tile([P, P], U8, name="g_scales", align_bytes=64)
             nc.vector.quantize_mx(
-                out=g_codes[:].bitcast(E5M2), scales=g_scales[:], in_=state["g", m][:].rearrange("q r s -> q (r s)")
+                out=g_codes[:].bitcast(E5M2), scales=g_scales[:], in_=g[:].rearrange("q r s -> q (r s)")
             )
-            acc = product_banks[m]
             nc.tensor.matmul_mx(
-                out=acc[:],
+                out=product_banks[m][:],
                 lhsT=g_codes[:].bitcast(E5M2),
                 lhsT_scale=g_scales[:],
                 rhs=wi_codes[:].bitcast(E4M3),
@@ -264,47 +262,24 @@ def tile_attend_gpgent_x_kernel(tc, xT, wT, adv, us, ts, wt, be, offs, out):
                 start=True,
                 stop=True,
             )
-            res = work.tile([P, P, PACK], F32, name="res", bufs=4)
-            pieces = 2 if m == TILES - 1 else 1
+            res = work.tile([P, P, PACK], F32, name="res", bufs=TILES)
+            pieces = LAST_PIECES if m == TILES - 1 else 1
             for j in range(pieces):
                 part = slice(j * P // pieces, (j + 1) * P // pieces)
-                nc.scalar.copy(res[:, part, :], acc[:].rearrange("r (t p) -> r p t", t=PACK)[:, part, :])
+                nc.scalar.copy(res[:, part, :], product_banks[m][:].rearrange("r (t p) -> r p t", t=PACK)[:, part, :])
                 nc.sync.dma_start(
                     out=out[m * P : (m + 1) * P, j * D // pieces : (j + 1) * D // pieces],
                     in_=res[:, part, :].rearrange("r p t -> r (p t)"),
                 )
 
-        quantise_x(0)
-        quantise_x(1)
-        wi_codes = stream.tile([P, D], U32, name="x_grouped0", align_bytes=64)
-        quantise_x(2)
-        quantise_x(3)
-        scores(0)
-        softmax_sums(0)
-        scores(1)
-        softmax_sums(1)
-        scores(2)
-        softmax_sums(2)
-        turn_plane(2, grad_banks[1][:].rearrange("q s p -> q (s p)"), x_grouped[1])
-        adv_term(0)
-        policy_terms(0)
-        scores(3)
-        softmax_sums(3)
-        adv_term(1)
-        policy_terms(1)
-        turn_plane(3, product_banks[2][:], x_grouped[2])
-        adv_term(2)
-        adv_term(3)
-        policy_terms(2)
-        policy_terms(3)
-        finish_g(0)
-        quantise_by_slot(0, 2, low_by_i[:])
-        quantise_by_slot(2, 1, x_grouped[1][:].rearrange("q p s -> q (p s)"))
-        quantise_by_slot(3, 1, x_grouped[2][:].rearrange("q p s -> q (p s)"))
-        finish_g(1)
-        rows_gradient(0)
-        finish_g(2)
-        rows_gradient(1)
-        finish_g(3)
-        rows_gradient(2)
-        rows_gradient(3)
+        for m in range(LEAD):
+            scores_and_exponentials(m)
+        for m in range(TILES):
+            gradient_terms(m)
+            if m + LEAD < TILES:
+                scores_and_exponentials(m + LEAD)
+        for half, w_by_i in enumerate((low_by_i[:], high_by_i)):
+            cols = slice(half * D // 2, (half + 1) * D // 2)
+            nc.vector.quantize_mx(out=wi_codes[:, cols].bitcast(E4M3), scales=wi_scales[:, cols], in_=w_by_i)
+        for m in range(TILES):
+            rows_gradient(m)

@@ -23,7 +23,8 @@ PACK = 4
 TILES = R // P
 FOLD = T // P
 LINE = 4
-LEAD = 2
+SLOT_BYTES = 4 * T
+WINDOW_SLOT = PACK
 LAST_PIECES = 2
 
 
@@ -31,225 +32,234 @@ def tile_attend_gpgent_x_kernel(tc, xT, wT, adv, us, ts, wt, be, offs, out):
     nc = tc.nc
     with ExitStack() as ctx:
         keep = ctx.enter_context(tc.tile_pool(name="keep", bufs=1))
-        reuse = ctx.enter_context(tc.tile_pool(name="reuse", bufs=1))
-        work = ctx.enter_context(tc.tile_pool(name="work", bufs=2))
+        stage = ctx.enter_context(tc.tile_pool(name="stage", bufs=1))
         psum = ctx.enter_context(tc.psum_pool(name="psum", bufs=1))
         grad_banks = [psum.tile([P, PACK, P], F32, name=f"grad{m}") for m in range(TILES)]
 
-        offsets = keep.tile([P, SLOTS // 16], U16, name="offsets")
-        ts_folded = reuse.tile([P, FOLD], F32, name="small")
-        nc.sync.dma_start(out=ts_folded[:], in_=ts[0:1, :].rearrange("o (p j) -> (o p) j", p=P))
+        def staged(name, shape, dtype, slot, start=0):
+            return stage.tile(shape, dtype, name=name, align_bytes=64, offset=slot * SLOT_BYTES + start)
 
+        offsets = keep.tile([P, SLOTS // 16], U16, name="offsets")
+        ts_folded = keep.tile([P, FOLD], F32, name="ts_folded")
+        nc.sync.dma_start(out=ts_folded[:], in_=ts[0:1, :].rearrange("o (p j) -> (o p) j", p=P))
         w_view = wT.rearrange("(p t) c -> p t c", t=PACK)
         x_view = xT.rearrange("(p t) r -> p t r", t=PACK)
-        w_planes = [reuse.tile([P, T], F32, name=f"staged{t}", align_bytes=64) for t in range(PACK)]
+        w_planes = [staged(f"w_plane{t}", [P, T], F32, t) for t in range(PACK)]
         nc.sync.dma_start(out=w_planes[0][:], in_=w_view[:, 0, :])
         nc.sync.dma_start(offsets[:], offs)
         for t in range(1, PACK):
             nc.sync.dma_start(out=w_planes[t][:], in_=w_view[:, t, :])
-        x_halves = []
-        for h in range(2):
-            x_halves.append(reuse.tile([P, PACK, R // 2], F32, name=f"staged{h}", align_bytes=64))
-            nc.sync.dma_start(out=x_halves[h][:], in_=x_view[:, :, h * (R // 2) : (h + 1) * (R // 2)])
-        ident32 = keep.tile([P, P], F32, name="ident32")
-        make_identity(nc, ident32[:])
-        ident16 = keep.tile([P, P], BF16, name="ident16")
-        make_identity(nc, ident16[:])
+        row_vecs = keep.tile([P, P], F32, name="row_vecs")
+        nc.gpsimd.memset(row_vecs[:], 0.0)
+        for j, vec in enumerate((us, wt, be)):
+            nc.scalar.dma_start(
+                out=row_vecs[j * TILES : (j + 1) * TILES, :], in_=vec.rearrange("(m p) o -> m (p o)", p=P)
+            )
+        ident = keep.tile([P, P], F32, name="ident")
+        make_identity(nc, ident[:])
 
-        ts_window = reuse.tile([P, T], F32, name="window", align_bytes=64)
+        ts_window = staged("ts_window", [P, T], F32, WINDOW_SLOT)
         window_view = ts_window[:].rearrange("m (p j) -> m p j", p=P)
         for a in range(FOLD // PACK):
             spread = psum.tile([P, PACK, P], F32, name=f"product{a}")
             for j in range(PACK):
                 col = a * PACK + j
-                nc.tensor.transpose(spread[:, j, :], ts_folded[:, col : col + 1].to_broadcast([P, P]), ident32[:])
+                nc.tensor.transpose(spread[:, j, :], ts_folded[:, col : col + 1].to_broadcast([P, P]), ident[:])
             nc.scalar.activation(
                 window_view[:, :, a * PACK : (a + 1) * PACK], spread[:].rearrange("m j p -> m p j"), ACT.Copy
             )
         product_banks = [psum.tile([P, SLOTS], F32, name=f"product{m}") for m in range(TILES)]
-        row_vecs = reuse.tile([P, P], F32, name="small")
-        nc.gpsimd.memset(row_vecs[:], 0.0)
-        for j, vec in enumerate((us, wt, be)):
-            nc.sync.dma_start(
-                out=row_vecs[j * TILES : (j + 1) * TILES, :], in_=vec.rearrange("(m p) o -> m (p o)", p=P)
+
+        nc.tensor.transpose(grad_banks[1][:, 0, :], row_vecs[:], ident[:])
+        vec_cols = keep.tile([P, 3 * TILES], F32, name="vec_cols")
+        nc.scalar.copy(vec_cols[:], grad_banks[1][:, 0, 0 : 3 * TILES])
+        us_cols = vec_cols[:, 0:TILES]
+        neg_us = keep.tile([P, TILES], F32, name="neg_us")
+        nc.gpsimd.tensor_scalar(neg_us[:], us_cols, -1.0, 0.0, ALU.mult, ALU.add)
+        adv_scale = keep.tile([P, TILES], F32, name="adv_scale")
+        nc.gpsimd.tensor_tensor(adv_scale[:], neg_us[:], vec_cols[:, TILES : 2 * TILES], ALU.mult)
+        numerators = keep.tile([P, TILES, 3], F32, name="numerators")
+        nc.gpsimd.memset(numerators[:, :, 0], 1.0)
+        nc.gpsimd.tensor_tensor(numerators[:, :, 1], neg_us[:], vec_cols[:, 2 * TILES : 3 * TILES], ALU.mult)
+
+        def transpose_pairs(bank, planes):
+            words = planes.bitcast(F32)
+            for t in range(2):
+                for u in range(2):
+                    first = t * SLOTS // 2 + u
+                    nc.tensor.transpose(bank[:, 2 * t + u, :], words[:, first : (t + 1) * SLOTS // 2 : 2], ident[:])
+
+        wi_codes = keep.tile([P, D], U32, name="wi_codes", align_bytes=64)
+        wi_scales = keep.tile([P, D], U8, name="wi_scales", align_bytes=64)
+
+        def turn_planes(half, planes, bank):
+            transpose_pairs(bank, planes)
+            by_i = keep.tile([P, 2 * P * PACK], BF16, name=f"by_i{half}", align_bytes=64)
+            nc.scalar.copy(
+                by_i[:].bitcast(F32).rearrange("q (t p u) -> q t p u", t=2, u=2),
+                bank.rearrange("q (t u) p -> q t p u", t=2),
             )
+            return by_i
+
+        def quantize_by_i(half, by_i):
+            cols = slice(half * D // 2, (half + 1) * D // 2)
+            nc.vector.quantize_mx(out=wi_codes[:, cols].bitcast(E4M3), scales=wi_scales[:, cols], in_=by_i[:])
+
+        low_planes = keep.tile([P, 2 * SLOTS], BF16, name="low_planes", align_bytes=64)
+        for t in range(2):
+            nc.vector.tensor_copy(low_planes[:, t * SLOTS : (t + 1) * SLOTS], w_planes[t][:].indirect(offsets[:]))
         ts_listed = keep.tile([P, SLOTS], F32, name="ts_listed")
         nc.vector.tensor_copy(ts_listed[:], ts_window[:].indirect(offsets[:]))
+        low_by_i = turn_planes(0, low_planes[:], grad_banks[0][:])
+        gathered = staged("gathered", [P, PACK * SLOTS], BF16, WINDOW_SLOT)
+        w_by_d = gathered[:].rearrange("p (i t) -> p i t", t=PACK)
+        x_halves = [
+            staged("x_half0", [P, PACK, R // 2], F32, WINDOW_SLOT, SLOT_BYTES // 2),
+            staged("x_half1", [P, PACK, R // 2], F32, 2),
+        ]
+        nc.sync.dma_start(out=x_halves[0][:], in_=x_view[:, :, 0 : R // 2])
         ts_rows = keep.tile([P, PACK, P], F32, name="ts_rows")
         nc.scalar.copy(ts_rows[:].rearrange("m s q -> m q s"), ts_listed[:].rearrange("m (q s) -> m q s", s=PACK))
+        nc.scalar.copy(w_by_d[:, :, 0:2], low_planes[:].rearrange("p (t i) -> p i t", t=2))
         for s in range(PACK):
-            nc.tensor.transpose(grad_banks[2][:, s, :], ts_rows[:, s, :], ident32[:])
+            nc.tensor.transpose(grad_banks[2][:, s, :], ts_rows[:, s, :], ident[:])
         ts_cols = keep.tile([P, PACK], F32, name="ts_cols")
         nc.scalar.copy(ts_cols[:], grad_banks[2][:, :, 0])
 
-        gathered = reuse.tile([P, (PACK + 2) * SLOTS], BF16, name="window", align_bytes=64)
-        w_by_d = gathered[:, 0 : PACK * SLOTS].rearrange("p (i t) -> p i t", t=PACK)
-        low_planes = gathered[:, PACK * SLOTS : (PACK + 2) * SLOTS]
-        wd_codes = keep.tile([P, SLOTS], U32, name="wd_codes", align_bytes=64)
-        wd_scales = keep.tile([P, SLOTS], U8, name="wd_scales", align_bytes=64)
-        wi_codes = keep.tile([P, D], U32, name="wi_codes", align_bytes=64)
-        wi_scales = keep.tile([P, D], U8, name="wi_scales", align_bytes=64)
-        x_grouped = [reuse.tile([P, P, PACK], BF16, name=f"x_grouped{m}", align_bytes=64) for m in range(2)]
-        x_codes = [keep.tile([P, P], U32, name=f"x_codes{m}", align_bytes=64) for m in range(TILES)]
-        x_scales = [keep.tile([P, P], U8, name=f"x_scales{m}", align_bytes=64) for m in range(TILES)]
-
-        def transpose_pairs(bank, plane):
-            words = plane.bitcast(F32)
-            for u in range(2):
-                nc.tensor.transpose(bank[:, u, :], words[:, u::2], ident32[:])
-
-        for t in range(2):
-            nc.vector.tensor_copy(low_planes[:, t * SLOTS : (t + 1) * SLOTS], w_planes[t][:].indirect(offsets[:]))
-        for t in range(2):
-            transpose_pairs(grad_banks[0][:, 2 * t : 2 * t + 2, :], low_planes[:, t * SLOTS : (t + 1) * SLOTS])
-        nc.scalar.copy(w_by_d[:, :, 0:2], low_planes.rearrange("p (t i) -> p i t", t=2))
-        low_by_i = keep.tile([P, 2 * P * PACK], BF16, name="low_by_i", align_bytes=64)
-        nc.scalar.copy(
-            low_by_i[:].bitcast(F32).rearrange("q (t p u) -> q t p u", t=2, u=2),
-            grad_banks[0][:].rearrange("q (t u) p -> q t p u", t=2),
-        )
-
-        nc.tensor.transpose(grad_banks[0][:, 0, :], row_vecs[:], ident32[:])
-        vec_cols = keep.tile([P, 3 * TILES], F32, name="vec_cols")
-        nc.vector.tensor_copy(vec_cols[:], grad_banks[0][:, 0, 0 : 3 * TILES])
-        us_cols = vec_cols[:, 0:TILES]
-        adv_scale = keep.tile([P, TILES], F32, name="adv_scale")
-        us_wt = keep.tile([P, TILES], F32, name="us_wt")
-        nc.gpsimd.tensor_tensor(us_wt[:], us_cols, vec_cols[:, TILES : 2 * TILES], ALU.mult)
-        nc.gpsimd.tensor_scalar(adv_scale[:], us_wt[:], -1.0, 0.0, ALU.mult, ALU.add)
-        numerators = keep.tile([P, TILES, 2], F32, name="numerators")
-        nc.gpsimd.memset(numerators[:], -1.0)
-        nc.gpsimd.tensor_tensor(numerators[:, :, 1], us_cols, vec_cols[:, 2 * TILES : 3 * TILES], ALU.mult)
-
         nc.vector.tensor_copy(w_by_d[:, :, 2], w_planes[2][:].indirect(offsets[:]))
+        quantize_by_i(0, low_by_i)
+        nc.sync.dma_start(out=x_halves[1][:], in_=x_view[:, :, R // 2 : R])
+        nc.vector.tensor_copy(w_by_d[:, :, 3], w_planes[3][:].indirect(offsets[:]))
         adv_tiles = []
         for h in range(2):
-            pair = reuse.tile([P, 2 * SLOTS], F32, name=f"staged{2 + h}", align_bytes=64)
+            pair = staged(f"adv_pair{h}", [P, 2 * SLOTS], F32, 2 + h, SLOT_BYTES // 2)
             nc.sync.dma_start(
                 out=pair[:].rearrange("p (e i) -> p e i", e=2),
                 in_=adv[2 * h * P : 2 * (h + 1) * P, :].rearrange("(e p) i -> p e i", e=2),
             )
             adv_tiles.extend(pair[:, e * SLOTS : (e + 1) * SLOTS] for e in range(2))
-        nc.vector.tensor_copy(w_by_d[:, :, 3], w_planes[3][:].indirect(offsets[:]))
-        nc.vector.quantize_mx(out=wd_codes[:].bitcast(E4M3), scales=wd_scales[:], in_=gathered[:, 0 : PACK * SLOTS])
 
-        for m in range(TILES):
-            h, e = divmod(m, 2)
-            grouped = x_grouped[e]
-            src = x_halves[h][:, :, e * P : (e + 1) * P]
-            if h == 0:
-                nc.scalar.copy(
-                    grouped[:].rearrange("p (c i) t -> p c t i", i=LINE),
-                    src.rearrange("p t (c i) -> p c t i", i=LINE),
-                )
-            else:
-                nc.vector.tensor_copy(grouped[:], src.rearrange("p t r -> p r t"))
-            nc.vector.quantize_mx(
-                out=x_codes[m][:].bitcast(E4M3),
-                scales=x_scales[m][:],
-                in_=grouped[:].rearrange("p r t -> p (r t)"),
+        x_codes = [staged(f"x_codes{h}", [P, 2 * P], U32, 3, h * 2 * P * 4) for h in range(2)]
+        x_scales = [keep.tile([P, 2 * P], U8, name=f"x_scales{h}", align_bytes=64) for h in range(2)]
+        wd_codes = keep.tile([P, SLOTS], U32, name="wd_codes", align_bytes=64)
+        wd_scales = keep.tile([P, SLOTS], U8, name="wd_scales", align_bytes=64)
+
+        def group_rows(engine_copy, grouped, src):
+            engine_copy(
+                grouped.rearrange("p (c i t) -> p c t i", i=LINE, t=PACK), src.rearrange("p t (c i) -> p c t i", i=LINE)
             )
 
-        high = reuse.tile([P, 3 * SLOTS], BF16, name="staged0", align_bytes=64)
-        high_by_i = high[:, 0 : 2 * SLOTS]
-        last_plane = high[:, 2 * SLOTS : 3 * SLOTS]
-        bank16 = grad_banks[1][:].rearrange("q s p -> q (s p)").bitcast(BF16)[:, 0 : PACK * P]
-        bank16 = bank16.rearrange("q (s p) -> q s p", s=PACK)
-        for s in range(PACK):
-            nc.tensor.transpose(bank16[:, s, :], w_by_d[:, s::PACK, 2], ident16[:])
-        nc.scalar.copy(high_by_i[:, 0:SLOTS].rearrange("q (p s) -> q p s", s=PACK), bank16.rearrange("q s p -> q p s"))
-        nc.scalar.copy(last_plane, w_by_d[:, :, 3])
-        transpose_pairs(grad_banks[3][:, 0:2, :], last_plane)
-        nc.scalar.copy(
-            high_by_i[:, SLOTS : 2 * SLOTS].bitcast(F32).rearrange("q (p u) -> q p u", u=2),
-            grad_banks[3][:, 0:2, :].rearrange("q u p -> q p u"),
-        )
+        def quantize_rows(h, cols, grouped):
+            nc.vector.quantize_mx(out=x_codes[h][:, cols].bitcast(E4M3), scales=x_scales[h][:, cols], in_=grouped)
 
-        z_tiles, e_tiles, neg_maxima, totals = [], [], [], []
+        first_grouped = [staged(f"x_grouped{e}", [P, P * PACK], BF16, 0, e * P * PACK * 4) for e in range(2)]
+        for e in range(2):
+            group_rows(nc.scalar.copy, first_grouped[e][:], x_halves[0][:, :, e * P : (e + 1) * P])
+        nc.vector.quantize_mx(out=wd_codes[:].bitcast(E4M3), scales=wd_scales[:], in_=gathered[:])
+        quantize_rows(0, slice(0, P), first_grouped[0][:])
+        second_grouped = staged("x_grouped23", [P, 2 * P * PACK], BF16, 0)
+        group_rows(nc.vector.tensor_copy, second_grouped[:], x_halves[1][:])
+        quantize_rows(0, slice(P, 2 * P), first_grouped[1][:])
+
+        z = [keep.tile([P, PACK, P], F32, name=f"z{m}") for m in range(TILES)]
+        e = [keep.tile([P, PACK, P], F32, name=f"e{m}") for m in range(TILES)]
+        neg_max = [keep.tile([P, 1], F32, name=f"neg_max{m}") for m in range(TILES)]
+        totals = [keep.tile([P, 2], F32, name=f"totals{h}") for h in range(2)]
+        ratios = [keep.tile([P, 2, 3], F32, name=f"ratios{h}") for h in range(2)]
 
         def add_transposed(m, term, first, last):
             for s in range(PACK):
                 nc.tensor.matmul(
                     grad_banks[m][:, s, :],
                     lhsT=term[:, s, :],
-                    rhs=ident32[:],
+                    rhs=ident[:],
                     is_transpose=True,
                     start=(first and s == 0),
                     stop=(last and s == PACK - 1),
                 )
 
-        def scores_and_exponentials(m):
+        def scores(m):
+            h, cols = m // 2, slice((m % 2) * P, (m % 2 + 1) * P)
             nc.tensor.matmul_mx(
                 out=product_banks[m][:],
-                lhsT=x_codes[m][:].bitcast(E4M3),
-                lhsT_scale=x_scales[m][:],
+                lhsT=x_codes[h][:, cols].bitcast(E4M3),
+                lhsT_scale=x_scales[h][:, cols],
                 rhs=wd_codes[:].bitcast(E4M3),
                 rhs_scale=wd_scales[:],
                 start=True,
                 stop=True,
             )
-            z = work.tile([P, PACK, P], F32, name="z", bufs=TILES)
             nc.vector.scalar_tensor_tensor(
-                z[:],
+                z[m][:],
                 product_banks[m][:].rearrange("r (q s) -> r s q", s=PACK),
                 us_cols[:, m : m + 1],
                 ts_rows[:],
                 ALU.mult,
                 ALU.mult,
             )
-            neg_max = work.tile([P, 1], F32, name="neg_max", bufs=TILES)
-            nc.vector.tensor_reduce(neg_max[:], z[:].rearrange("r s q -> r (s q)"), AX.X, ALU.max, negate=True)
-            e = work.tile([P, PACK, P], F32, name="e", bufs=TILES)
-            tot = work.tile([P, 1], F32, name="tot", bufs=TILES)
-            nc.scalar.activation(e[:], z[:], ACT.Exp, bias=neg_max[:], accum_out=tot[:])
-            z_tiles.append(z)
-            e_tiles.append(e)
-            neg_maxima.append(neg_max)
-            totals.append(tot)
 
-        def gradient_terms(m):
-            z, e = z_tiles[m], e_tiles[m]
-            a_term = work.tile([P, PACK, P], F32, name="a_term", bufs=TILES)
-            a_sum = neg_maxima[m - 2] if m >= 2 else work.tile([P, 1], F32, name="a_sum", bufs=TILES)
+        def exponentials(m):
+            nc.vector.tensor_reduce(neg_max[m][:], z[m][:].rearrange("r s q -> r (s q)"), AX.X, ALU.max, negate=True)
+            nc.scalar.activation(
+                e[m][:], z[m][:], ACT.Exp, bias=neg_max[m][:], accum_out=totals[m // 2][:, m % 2 : m % 2 + 1]
+            )
+
+        def adv_term(m):
+            a_term = keep.tile([P, PACK, P], F32, name=f"a_term{m}")
             nc.scalar.activation(
                 a_term[:].rearrange("r s q -> r q s"),
                 adv_tiles[m].rearrange("r (q s) -> r q s", s=PACK),
                 ACT.Copy,
                 scale=adv_scale[:, m : m + 1],
-                accum_out=a_sum[:],
+                accum_out=numerators[:, m, 2:3],
             )
             add_transposed(m, a_term, True, False)
 
-            inv = work.tile([P, 1], F32, name="inv", bufs=TILES)
-            nc.vector.reciprocal(inv[:], totals[m][:])
-            ratios = work.tile([P, 2], F32, name="ratios", bufs=TILES)
-            nc.vector.tensor_scalar(ratios[:], numerators[:, m, :], inv[:], None, ALU.mult)
-            u_term = work.tile([P, PACK, P], F32, name="u_term", bufs=TILES)
-            u_sum = work.tile([P, 1], F32, name="u_sum", bufs=TILES)
+        def inverse(h):
+            inv = keep.tile([P, 2], F32, name=f"inv{h}")
+            nc.vector.reciprocal(inv[:], totals[h][:])
+            return inv
+
+        def row_ratios(h, inv):
             nc.vector.scalar_tensor_tensor(
-                u_term[:], z[:], ratios[:, 1:2], e[:], ALU.mult, ALU.mult, accum_out=u_sum[:]
+                ratios[h][:],
+                numerators[:, 2 * h : 2 * h + 2, :],
+                -1.0,
+                inv[:].unsqueeze(2).to_broadcast([P, 2, 3]),
+                ALU.mult,
+                ALU.mult,
+            )
+
+        def entropy_terms(m):
+            ratio = ratios[m // 2][:, m % 2, :]
+            u_term = keep.tile([P, PACK, P], F32, name=f"u_term{m}")
+            u_sum = keep.tile([P, 1], F32, name=f"u_sum{m}")
+            nc.vector.scalar_tensor_tensor(
+                u_term[:], z[m][:], ratio[:, 1:2], e[m][:], ALU.mult, ALU.mult, accum_out=u_sum[:]
             )
             add_transposed(m, u_term, False, False)
-
-            e_scale = work.tile([P, 1], F32, name="e_scale", bufs=TILES)
-            nc.vector.tensor_scalar(e_scale[:], u_sum[:], a_sum[:], ratios[:, 0:1], ALU.add, ALU.mult)
-            e_term = work.tile([P, PACK, P], F32, name="e_term", bufs=TILES)
+            e_scale = keep.tile([P, 1], F32, name=f"e_scale{m}")
+            nc.scalar.activation(e_scale[:], u_sum[:], ACT.Identity, bias=ratio[:, 2:3], scale=ratio[:, 0:1])
+            e_term = keep.tile([P, PACK, P], F32, name=f"e_term{m}")
             pieces = LAST_PIECES if m == TILES - 1 else 1
             for j in range(pieces):
                 part = slice(j * PACK // pieces, (j + 1) * PACK // pieces)
-                nc.scalar.activation(e_term[:, part, :], e[:, part, :], ACT.Copy, scale=e_scale[:])
+                nc.scalar.activation(e_term[:, part, :], e[m][:, part, :], ACT.Copy, scale=e_scale[:])
             add_transposed(m, e_term, False, True)
 
-        def rows_gradient(m):
-            g = work.tile([P, P, PACK], BF16, name="g", align_bytes=64)
+        def gradient(m):
+            g = keep.tile([P, P, PACK], BF16, name=f"g{m}", align_bytes=64)
             nc.vector.tensor_tensor(
                 g[:],
                 grad_banks[m][:].rearrange("q s r -> q r s"),
                 ts_cols[:].unsqueeze(1).to_broadcast([P, P, PACK]),
                 ALU.mult,
             )
-            g_codes = work.tile([P, P], U32, name="g_codes", align_bytes=64)
-            g_scales = work.tile([P, P], U8, name="g_scales", align_bytes=64)
+            return g
+
+        def rows_gradient(m, g):
+            g_codes = keep.tile([P, P], U32, name=f"g_codes{m}", align_bytes=64)
+            g_scales = keep.tile([P, P], U8, name=f"g_scales{m}", align_bytes=64)
             nc.vector.quantize_mx(
                 out=g_codes[:].bitcast(E5M2), scales=g_scales[:], in_=g[:].rearrange("q r s -> q (r s)")
             )
@@ -262,24 +272,51 @@ def tile_attend_gpgent_x_kernel(tc, xT, wT, adv, us, ts, wt, be, offs, out):
                 start=True,
                 stop=True,
             )
-            res = work.tile([P, P, PACK], F32, name="res", bufs=TILES)
+            res = keep.tile([P, P, PACK], F32, name=f"res{m}")
             pieces = LAST_PIECES if m == TILES - 1 else 1
             for j in range(pieces):
                 part = slice(j * P // pieces, (j + 1) * P // pieces)
-                nc.scalar.copy(res[:, part, :], product_banks[m][:].rearrange("r (t p) -> r p t", t=PACK)[:, part, :])
+                copy_out = nc.vector.tensor_copy if m == TILES - 1 else nc.scalar.copy
+                copy_out(res[:, part, :], product_banks[m][:].rearrange("r (t p) -> r p t", t=PACK)[:, part, :])
                 nc.sync.dma_start(
                     out=out[m * P : (m + 1) * P, j * D // pieces : (j + 1) * D // pieces],
                     in_=res[:, part, :].rearrange("r p t -> r (p t)"),
                 )
 
-        for m in range(LEAD):
-            scores_and_exponentials(m)
+        scores(0)
+        quantize_rows(1, slice(0, 2 * P), second_grouped[:])
+        high_planes = staged("high_planes", [P, 2 * SLOTS], BF16, 0)
+        nc.gpsimd.tensor_scalar(
+            high_planes[:].rearrange("p (t c i) -> p c t i", t=2, i=2 * LINE),
+            w_by_d[:, :, 2:4].rearrange("p (c i) t -> p c t i", i=2 * LINE),
+            1.0,
+            0.0,
+            ALU.mult,
+            ALU.add,
+        )
+        scores(1)
+        adv_term(0)
+        adv_term(1)
+        exponentials(0)
+        scores(2)
+        exponentials(1)
+        scores(3)
+        high_by_i = turn_planes(1, high_planes[:], product_banks[3][:].rearrange("q (s p) -> q s p", s=PACK))
+        adv_term(2)
+        exponentials(2)
+        inv = inverse(0)
+        exponentials(3)
+        adv_term(3)
+        row_ratios(0, inv)
+        entropy_terms(0)
+        inv = inverse(1)
+        entropy_terms(1)
+        quantize_by_i(1, high_by_i)
+        row_ratios(1, inv)
+        entropy_terms(2)
+        entropy_terms(3)
+        g = [gradient(0)]
         for m in range(TILES):
-            gradient_terms(m)
-            if m + LEAD < TILES:
-                scores_and_exponentials(m + LEAD)
-        for half, w_by_i in enumerate((low_by_i[:], high_by_i)):
-            cols = slice(half * D // 2, (half + 1) * D // 2)
-            nc.vector.quantize_mx(out=wi_codes[:, cols].bitcast(E4M3), scales=wi_scales[:, cols], in_=w_by_i)
-        for m in range(TILES):
-            rows_gradient(m)
+            if m + 1 < TILES:
+                g.append(gradient(m + 1))
+            rows_gradient(m, g[m])

@@ -92,14 +92,11 @@ def tile_attend_gpgent_x_kernel(tc, xT, wT, adv, us, ts, wt, be, offs, out):
         wi_codes = keep.tile([P, D], U32, name="wi_codes", align_bytes=64)
         wi_scales = keep.tile([P, D], U8, name="wi_scales", align_bytes=64)
 
-        def turn_planes(half, planes, bank):
-            transpose_pairs(bank, planes)
-            by_i = keep.tile([P, 2 * P * PACK], BF16, name=f"by_i{half}", align_bytes=64)
+        def leave_bank(by_i, bank):
             nc.scalar.copy(
                 by_i[:].bitcast(F32).rearrange("q (t p u) -> q t p u", t=2, u=2),
                 bank.rearrange("q (t u) p -> q t p u", t=2),
             )
-            return by_i
 
         def quantize_by_i(half, by_i):
             cols = slice(half * D // 2, (half + 1) * D // 2)
@@ -110,7 +107,9 @@ def tile_attend_gpgent_x_kernel(tc, xT, wT, adv, us, ts, wt, be, offs, out):
             nc.vector.tensor_copy(low_planes[:, t * SLOTS : (t + 1) * SLOTS], w_planes[t][:].indirect(offsets[:]))
         ts_listed = keep.tile([P, SLOTS], F32, name="ts_listed")
         nc.vector.tensor_copy(ts_listed[:], ts_window[:].indirect(offsets[:]))
-        low_by_i = turn_planes(0, low_planes[:], grad_banks[0][:])
+        transpose_pairs(grad_banks[0], low_planes[:])
+        low_by_i = keep.tile([P, 2 * P * PACK], BF16, name="low_by_i", align_bytes=64)
+        leave_bank(low_by_i, grad_banks[0][:])
         gathered = staged("gathered", [P, PACK * SLOTS], BF16, WINDOW_SLOT)
         w_by_d = gathered[:].rearrange("p (i t) -> p i t", t=PACK)
         x_halves = [
@@ -160,10 +159,11 @@ def tile_attend_gpgent_x_kernel(tc, xT, wT, adv, us, ts, wt, be, offs, out):
         second_grouped = staged("x_grouped23", [P, 2 * P * PACK], BF16, 0)
         group_rows(nc.vector.tensor_copy, second_grouped[:], x_halves[1][:])
         quantize_rows(0, slice(P, 2 * P), first_grouped[1][:])
+        quantize_rows(1, slice(0, 2 * P), second_grouped[:])
 
         z = [keep.tile([P, PACK, P], F32, name=f"z{m}") for m in range(TILES)]
         e = [keep.tile([P, PACK, P], F32, name=f"e{m}") for m in range(TILES)]
-        neg_max = [keep.tile([P, 1], F32, name=f"neg_max{m}") for m in range(TILES)]
+        neg_max = [staged(f"neg_max{m}", [P, 1], F32, 1, (m - 1) % TILES * 2 * SLOTS * 2) for m in range(TILES)]
         totals = [keep.tile([P, 2], F32, name=f"totals{h}") for h in range(2)]
         ratios = [keep.tile([P, 2, 3], F32, name=f"ratios{h}") for h in range(2)]
 
@@ -283,17 +283,17 @@ def tile_attend_gpgent_x_kernel(tc, xT, wT, adv, us, ts, wt, be, offs, out):
                     in_=res[:, part, :].rearrange("r p t -> r (p t)"),
                 )
 
+        high_pairs = staged("high_pairs", [P, 2, 2, P, 2], BF16, 0)
+        for t in range(2):
+            nc.gpsimd.tensor_scalar(
+                high_pairs[:, t, :, :, :],
+                w_by_d[:, :, 2 + t].rearrange("p (q u e) -> p u q e", u=2, e=2),
+                1.0,
+                0.0,
+                ALU.mult,
+                ALU.add,
+            )
         scores(0)
-        quantize_rows(1, slice(0, 2 * P), second_grouped[:])
-        high_planes = staged("high_planes", [P, 2 * SLOTS], BF16, 0)
-        nc.gpsimd.tensor_scalar(
-            high_planes[:].rearrange("p (t c i) -> p c t i", t=2, i=2 * LINE),
-            w_by_d[:, :, 2:4].rearrange("p (c i) t -> p c t i", i=2 * LINE),
-            1.0,
-            0.0,
-            ALU.mult,
-            ALU.add,
-        )
         scores(1)
         adv_term(0)
         adv_term(1)
@@ -301,17 +301,22 @@ def tile_attend_gpgent_x_kernel(tc, xT, wT, adv, us, ts, wt, be, offs, out):
         scores(2)
         exponentials(1)
         scores(3)
-        high_by_i = turn_planes(1, high_planes[:], product_banks[3][:].rearrange("q (s p) -> q s p", s=PACK))
+        high_bank = product_banks[1][:].rearrange("q (s p) -> q s p", s=PACK)
+        high_words = high_pairs[:].rearrange("p t u q e -> p (t u q e)").bitcast(F32)
+        for j in range(PACK):
+            nc.tensor.transpose(high_bank[:, j, :], high_words[:, j * P : (j + 1) * P], ident[:])
         adv_term(2)
+        adv_term(3)
+        high_by_i = staged("high_by_i", [P, 2 * P * PACK], BF16, 1)
+        leave_bank(high_by_i, high_bank)
         exponentials(2)
         inv = inverse(0)
         exponentials(3)
-        adv_term(3)
         row_ratios(0, inv)
+        quantize_by_i(1, high_by_i)
         entropy_terms(0)
         inv = inverse(1)
         entropy_terms(1)
-        quantize_by_i(1, high_by_i)
         row_ratios(1, inv)
         entropy_terms(2)
         entropy_terms(3)

@@ -111,7 +111,7 @@ def tile_attend_gpgent_x_kernel(tc, xT, wT, adv, us, ts, wt, be, offs, out):
         low_by_i = keep.tile([P, 2 * P * PACK], BF16, name="low_by_i", align_bytes=64)
         leave_bank(low_by_i, grad_banks[0][:])
         gathered = staged("gathered", [P, PACK * SLOTS], BF16, WINDOW_SLOT)
-        w_by_d = gathered[:].rearrange("p (i t) -> p i t", t=PACK)
+        w_by_d = gathered[:].rearrange("p (s q t) -> p q s t", s=PACK, t=PACK)
         x_halves = [
             staged("x_half0", [P, PACK, R // 2], F32, WINDOW_SLOT, SLOT_BYTES // 2),
             staged("x_half1", [P, PACK, R // 2], F32, 2),
@@ -119,16 +119,16 @@ def tile_attend_gpgent_x_kernel(tc, xT, wT, adv, us, ts, wt, be, offs, out):
         nc.sync.dma_start(out=x_halves[0][:], in_=x_view[:, :, 0 : R // 2])
         ts_rows = keep.tile([P, PACK, P], F32, name="ts_rows")
         nc.scalar.copy(ts_rows[:].rearrange("m s q -> m q s"), ts_listed[:].rearrange("m (q s) -> m q s", s=PACK))
-        nc.scalar.copy(w_by_d[:, :, 0:2], low_planes[:].rearrange("p (t i) -> p i t", t=2))
+        nc.scalar.copy(w_by_d[:, :, :, 0:2], low_planes[:].rearrange("p (t q s) -> p q s t", t=2, s=PACK))
         for s in range(PACK):
             nc.tensor.transpose(grad_banks[2][:, s, :], ts_rows[:, s, :], ident[:])
         ts_cols = keep.tile([P, PACK], F32, name="ts_cols")
         nc.scalar.copy(ts_cols[:], grad_banks[2][:, :, 0])
 
-        nc.vector.tensor_copy(w_by_d[:, :, 2], w_planes[2][:].indirect(offsets[:]))
+        nc.vector.tensor_copy(w_by_d[:, :, :, 2], w_planes[2][:].indirect(offsets[:]))
         quantize_by_i(0, low_by_i)
         nc.sync.dma_start(out=x_halves[1][:], in_=x_view[:, :, R // 2 : R])
-        nc.vector.tensor_copy(w_by_d[:, :, 3], w_planes[3][:].indirect(offsets[:]))
+        nc.vector.tensor_copy(w_by_d[:, :, :, 3], w_planes[3][:].indirect(offsets[:]))
         adv_tiles = []
         for h in range(2):
             pair = staged(f"adv_pair{h}", [P, 2 * SLOTS], F32, 2 + h, SLOT_BYTES // 2)
@@ -151,12 +151,12 @@ def tile_attend_gpgent_x_kernel(tc, xT, wT, adv, us, ts, wt, be, offs, out):
         def quantize_rows(h, cols, grouped):
             nc.vector.quantize_mx(out=x_codes[h][:, cols].bitcast(E4M3), scales=x_scales[h][:, cols], in_=grouped)
 
-        first_grouped = [staged(f"x_grouped{e}", [P, P * PACK], BF16, 0, e * P * PACK * 4) for e in range(2)]
+        first_grouped = [keep.tile([P, P * PACK], BF16, name=f"x_grouped{e}", align_bytes=64) for e in range(2)]
         for e in range(2):
             group_rows(nc.scalar.copy, first_grouped[e][:], x_halves[0][:, :, e * P : (e + 1) * P])
         nc.vector.quantize_mx(out=wd_codes[:].bitcast(E4M3), scales=wd_scales[:], in_=gathered[:])
         quantize_rows(0, slice(0, P), first_grouped[0][:])
-        second_grouped = staged("x_grouped23", [P, 2 * P * PACK], BF16, 0)
+        second_grouped = staged("x_grouped23", [P, 2 * P * PACK], BF16, WINDOW_SLOT, SLOT_BYTES // 2)
         group_rows(nc.vector.tensor_copy, second_grouped[:], x_halves[1][:])
         quantize_rows(0, slice(P, 2 * P), first_grouped[1][:])
         quantize_rows(1, slice(0, 2 * P), second_grouped[:])
@@ -164,8 +164,9 @@ def tile_attend_gpgent_x_kernel(tc, xT, wT, adv, us, ts, wt, be, offs, out):
         z = [keep.tile([P, PACK, P], F32, name=f"z{m}") for m in range(TILES)]
         e = [keep.tile([P, PACK, P], F32, name=f"e{m}") for m in range(TILES)]
         neg_max = [staged(f"neg_max{m}", [P, 1], F32, 1, (m - 1) % TILES * 2 * SLOTS * 2) for m in range(TILES)]
-        totals = [keep.tile([P, 2], F32, name=f"totals{h}") for h in range(2)]
-        ratios = [keep.tile([P, 2, 3], F32, name=f"ratios{h}") for h in range(2)]
+        totals = keep.tile([P, TILES], F32, name="totals")
+        inverses = keep.tile([P, TILES], F32, name="inverses")
+        ratios = keep.tile([P, TILES, 3], F32, name="ratios")
 
         def add_transposed(m, term, first, last):
             for s in range(PACK):
@@ -191,7 +192,7 @@ def tile_attend_gpgent_x_kernel(tc, xT, wT, adv, us, ts, wt, be, offs, out):
             )
             nc.vector.scalar_tensor_tensor(
                 z[m][:],
-                product_banks[m][:].rearrange("r (q s) -> r s q", s=PACK),
+                product_banks[m][:].rearrange("r (s q) -> r s q", s=PACK),
                 us_cols[:, m : m + 1],
                 ts_rows[:],
                 ALU.mult,
@@ -201,7 +202,7 @@ def tile_attend_gpgent_x_kernel(tc, xT, wT, adv, us, ts, wt, be, offs, out):
         def exponentials(m):
             nc.vector.tensor_reduce(neg_max[m][:], z[m][:].rearrange("r s q -> r (s q)"), AX.X, ALU.max, negate=True)
             nc.scalar.activation(
-                e[m][:], z[m][:], ACT.Exp, bias=neg_max[m][:], accum_out=totals[m // 2][:, m % 2 : m % 2 + 1]
+                e[m][:], z[m][:], ACT.Exp, bias=neg_max[m][:], accum_out=totals[:, m : m + 1]
             )
 
         def adv_term(m):
@@ -215,23 +216,21 @@ def tile_attend_gpgent_x_kernel(tc, xT, wT, adv, us, ts, wt, be, offs, out):
             )
             add_transposed(m, a_term, True, False)
 
-        def inverse(h):
-            inv = keep.tile([P, 2], F32, name=f"inv{h}")
-            nc.vector.reciprocal(inv[:], totals[h][:])
-            return inv
+        def inverse(first, last):
+            nc.vector.reciprocal(inverses[:, first:last], totals[:, first:last])
 
-        def row_ratios(h, inv):
+        def row_ratios(first, last):
             nc.vector.scalar_tensor_tensor(
-                ratios[h][:],
-                numerators[:, 2 * h : 2 * h + 2, :],
+                ratios[:, first:last, :],
+                numerators[:, first:last, :],
                 -1.0,
-                inv[:].unsqueeze(2).to_broadcast([P, 2, 3]),
+                inverses[:, first:last].unsqueeze(2).to_broadcast([P, last - first, 3]),
                 ALU.mult,
                 ALU.mult,
             )
 
         def entropy_terms(m):
-            ratio = ratios[m // 2][:, m % 2, :]
+            ratio = ratios[:, m, :]
             u_term = keep.tile([P, PACK, P], F32, name=f"u_term{m}")
             u_sum = keep.tile([P, 1], F32, name=f"u_sum{m}")
             nc.vector.scalar_tensor_tensor(
@@ -247,33 +246,38 @@ def tile_attend_gpgent_x_kernel(tc, xT, wT, adv, us, ts, wt, be, offs, out):
                 nc.scalar.activation(e_term[:, part, :], e[m][:, part, :], ACT.Copy, scale=e_scale[:])
             add_transposed(m, e_term, False, True)
 
-        def gradient(m):
-            g = keep.tile([P, P, PACK], BF16, name=f"g{m}", align_bytes=64)
+        g = [keep.tile([P, P, PACK], BF16, name=f"g{m}", align_bytes=64) for m in range(TILES)]
+        g_codes = [keep.tile([P, P], U32, name=f"g_codes{m}", align_bytes=64) for m in range(TILES)]
+        g_scales = [keep.tile([P, P], U8, name=f"g_scales{m}", align_bytes=64) for m in range(TILES)]
+
+        def gradient(m, rows=slice(0, P)):
+            pairs = (rows.stop - rows.start) // 2
             nc.vector.tensor_tensor(
-                g[:],
-                grad_banks[m][:].rearrange("q s r -> q r s"),
-                ts_cols[:].unsqueeze(1).to_broadcast([P, P, PACK]),
+                g[m][:, rows, :].rearrange("q (c i) s -> q c s i", i=2),
+                grad_banks[m][:, :, rows].rearrange("q s (c i) -> q c s i", i=2),
+                ts_cols[:].unsqueeze(1).unsqueeze(3).to_broadcast([P, pairs, PACK, 2]),
                 ALU.mult,
             )
-            return g
 
-        def rows_gradient(m, g):
-            g_codes = keep.tile([P, P], U32, name=f"g_codes{m}", align_bytes=64)
-            g_scales = keep.tile([P, P], U8, name=f"g_scales{m}", align_bytes=64)
+        def quantize_gradient(m, rows=slice(0, P)):
             nc.vector.quantize_mx(
-                out=g_codes[:].bitcast(E5M2), scales=g_scales[:], in_=g[:].rearrange("q r s -> q (r s)")
+                out=g_codes[m][:, rows].bitcast(E5M2),
+                scales=g_scales[m][:, rows],
+                in_=g[m][:, rows, :].rearrange("q r s -> q (r s)"),
             )
+
+        def rows_gradient(m):
             nc.tensor.matmul_mx(
                 out=product_banks[m][:],
-                lhsT=g_codes[:].bitcast(E5M2),
-                lhsT_scale=g_scales[:],
+                lhsT=g_codes[m][:].bitcast(E5M2),
+                lhsT_scale=g_scales[m][:],
                 rhs=wi_codes[:].bitcast(E4M3),
                 rhs_scale=wi_scales[:],
                 start=True,
                 stop=True,
             )
             res = keep.tile([P, P, PACK], F32, name=f"res{m}")
-            pieces = LAST_PIECES if m == TILES - 1 else 1
+            pieces = LAST_PIECES if m >= TILES - 2 else 1
             for j in range(pieces):
                 part = slice(j * P // pieces, (j + 1) * P // pieces)
                 copy_out = nc.vector.tensor_copy if m == TILES - 1 else nc.scalar.copy
@@ -283,11 +287,11 @@ def tile_attend_gpgent_x_kernel(tc, xT, wT, adv, us, ts, wt, be, offs, out):
                     in_=res[:, part, :].rearrange("r p t -> r (p t)"),
                 )
 
-        high_pairs = staged("high_pairs", [P, 2, 2, P, 2], BF16, 0)
+        high_pairs = staged("high_pairs", [P, 2, 2, P, 2], BF16, WINDOW_SLOT, SLOT_BYTES // 2)
         for t in range(2):
             nc.gpsimd.tensor_scalar(
                 high_pairs[:, t, :, :, :],
-                w_by_d[:, :, 2 + t].rearrange("p (q u e) -> p u q e", u=2, e=2),
+                w_by_d[:, :, :, 2 + t].rearrange("p q (u e) -> p u q e", u=2),
                 1.0,
                 0.0,
                 ALU.mult,
@@ -298,8 +302,8 @@ def tile_attend_gpgent_x_kernel(tc, xT, wT, adv, us, ts, wt, be, offs, out):
         adv_term(0)
         adv_term(1)
         exponentials(0)
-        scores(2)
         exponentials(1)
+        scores(2)
         scores(3)
         high_bank = product_banks[1][:].rearrange("q (s p) -> q s p", s=PACK)
         high_words = high_pairs[:].rearrange("p t u q e -> p (t u q e)").bitcast(F32)
@@ -309,19 +313,29 @@ def tile_attend_gpgent_x_kernel(tc, xT, wT, adv, us, ts, wt, be, offs, out):
         adv_term(3)
         high_by_i = staged("high_by_i", [P, 2 * P * PACK], BF16, 1)
         leave_bank(high_by_i, high_bank)
+        inverse(0, 2)
         exponentials(2)
-        inv = inverse(0)
+        row_ratios(0, 2)
         exponentials(3)
-        row_ratios(0, inv)
-        quantize_by_i(1, high_by_i)
         entropy_terms(0)
-        inv = inverse(1)
+        inverse(2, 3)
         entropy_terms(1)
-        row_ratios(1, inv)
+        row_ratios(2, 3)
+        inverse(3, 4)
         entropy_terms(2)
+        row_ratios(3, 4)
+        quantize_by_i(1, high_by_i)
         entropy_terms(3)
-        g = [gradient(0)]
-        for m in range(TILES):
-            if m + 1 < TILES:
-                g.append(gradient(m + 1))
-            rows_gradient(m, g[m])
+        gradient(0)
+        for m in range(TILES - 2):
+            gradient(m + 1)
+            quantize_gradient(m)
+            rows_gradient(m)
+        halves = (slice(0, P // 2), slice(P // 2, P))
+        gradient(3, halves[0])
+        quantize_gradient(2)
+        rows_gradient(2)
+        gradient(3, halves[1])
+        for rows in halves:
+            quantize_gradient(3, rows)
+        rows_gradient(3)

@@ -111,7 +111,7 @@ def tile_attend_gpgent_x_kernel(tc, xT, wT, adv, us, ts, wt, be, offs, out):
         low_by_i = keep.tile([P, 2 * P * PACK], BF16, name="low_by_i", align_bytes=64)
         leave_bank(low_by_i, grad_banks[0][:])
         gathered = staged("gathered", [P, PACK * SLOTS], BF16, WINDOW_SLOT)
-        w_by_d = gathered[:].rearrange("p (s q t) -> p q s t", s=PACK, t=PACK)
+        w_by_d = gathered[:].rearrange("p (i t) -> p i t", t=PACK)
         x_halves = [
             staged("x_half0", [P, PACK, R // 2], F32, WINDOW_SLOT, SLOT_BYTES // 2),
             staged("x_half1", [P, PACK, R // 2], F32, 2),
@@ -119,16 +119,20 @@ def tile_attend_gpgent_x_kernel(tc, xT, wT, adv, us, ts, wt, be, offs, out):
         nc.sync.dma_start(out=x_halves[0][:], in_=x_view[:, :, 0 : R // 2])
         ts_rows = keep.tile([P, PACK, P], F32, name="ts_rows")
         nc.scalar.copy(ts_rows[:].rearrange("m s q -> m q s"), ts_listed[:].rearrange("m (q s) -> m q s", s=PACK))
-        nc.scalar.copy(w_by_d[:, :, :, 0:2], low_planes[:].rearrange("p (t q s) -> p q s t", t=2, s=PACK))
+        nc.scalar.copy(w_by_d[:, :, 0:2], low_planes[:].rearrange("p (t i) -> p i t", t=2))
         for s in range(PACK):
             nc.tensor.transpose(grad_banks[2][:, s, :], ts_rows[:, s, :], ident[:])
         ts_cols = keep.tile([P, PACK], F32, name="ts_cols")
         nc.scalar.copy(ts_cols[:], grad_banks[2][:, :, 0])
 
-        nc.vector.tensor_copy(w_by_d[:, :, :, 2], w_planes[2][:].indirect(offsets[:]))
+        nc.vector.tensor_copy(w_by_d[:, :, 2], w_planes[2][:].indirect(offsets[:]))
         quantize_by_i(0, low_by_i)
         nc.sync.dma_start(out=x_halves[1][:], in_=x_view[:, :, R // 2 : R])
-        nc.vector.tensor_copy(w_by_d[:, :, :, 3], w_planes[3][:].indirect(offsets[:]))
+        for h in range(2):
+            nc.vector.tensor_copy(
+                w_by_d[:, h * SLOTS // 2 : (h + 1) * SLOTS // 2, 3],
+                w_planes[3][:].indirect(offsets[:, h * SLOTS // 32 : (h + 1) * SLOTS // 32]),
+            )
         adv_tiles = []
         for h in range(2):
             pair = staged(f"adv_pair{h}", [P, 2 * SLOTS], F32, 2 + h, SLOT_BYTES // 2)
@@ -154,7 +158,13 @@ def tile_attend_gpgent_x_kernel(tc, xT, wT, adv, us, ts, wt, be, offs, out):
         first_grouped = [keep.tile([P, P * PACK], BF16, name=f"x_grouped{e}", align_bytes=64) for e in range(2)]
         for e in range(2):
             group_rows(nc.scalar.copy, first_grouped[e][:], x_halves[0][:, :, e * P : (e + 1) * P])
-        nc.vector.quantize_mx(out=wd_codes[:].bitcast(E4M3), scales=wd_scales[:], in_=gathered[:])
+        for h in range(2):
+            cols = slice(h * SLOTS // 2, (h + 1) * SLOTS // 2)
+            nc.vector.quantize_mx(
+                out=wd_codes[:, cols].bitcast(E4M3),
+                scales=wd_scales[:, cols],
+                in_=gathered[:, PACK * cols.start : PACK * cols.stop],
+            )
         quantize_rows(0, slice(0, P), first_grouped[0][:])
         second_grouped = staged("x_grouped23", [P, 2 * P * PACK], BF16, WINDOW_SLOT, SLOT_BYTES // 2)
         group_rows(nc.vector.tensor_copy, second_grouped[:], x_halves[1][:])
@@ -192,7 +202,7 @@ def tile_attend_gpgent_x_kernel(tc, xT, wT, adv, us, ts, wt, be, offs, out):
             )
             nc.vector.scalar_tensor_tensor(
                 z[m][:],
-                product_banks[m][:].rearrange("r (s q) -> r s q", s=PACK),
+                product_banks[m][:].rearrange("r (q s) -> r s q", s=PACK),
                 us_cols[:, m : m + 1],
                 ts_rows[:],
                 ALU.mult,
@@ -291,7 +301,7 @@ def tile_attend_gpgent_x_kernel(tc, xT, wT, adv, us, ts, wt, be, offs, out):
         for t in range(2):
             nc.gpsimd.tensor_scalar(
                 high_pairs[:, t, :, :, :],
-                w_by_d[:, :, :, 2 + t].rearrange("p q (u e) -> p u q e", u=2),
+                w_by_d[:, :, 2 + t].rearrange("p (q u e) -> p u q e", u=2, e=2),
                 1.0,
                 0.0,
                 ALU.mult,

@@ -34,7 +34,7 @@ def tile_attend_gpgent_x_kernel(tc, xT, wT, adv, us, ts, wt, be, offs, out):
         keep = ctx.enter_context(tc.tile_pool(name="keep", bufs=1))
         stage = ctx.enter_context(tc.tile_pool(name="stage", bufs=1))
         psum = ctx.enter_context(tc.psum_pool(name="psum", bufs=1))
-        grad_banks = [psum.tile([P, PACK, P], F32, name=f"grad{m}") for m in range(TILES)]
+        out_banks = [psum.tile([P, PACK, P], F32, name=f"out{m}") for m in range(TILES)]
 
         def staged(name, shape, dtype, slot, start=0):
             return stage.tile(shape, dtype, name=name, align_bytes=64, offset=slot * SLOT_BYTES + start)
@@ -69,10 +69,11 @@ def tile_attend_gpgent_x_kernel(tc, xT, wT, adv, us, ts, wt, be, offs, out):
                 window_view[:, :, a * PACK : (a + 1) * PACK], spread[:].rearrange("m j p -> m p j"), ACT.Copy
             )
         product_banks = [psum.tile([P, SLOTS], F32, name=f"product{m}") for m in range(TILES)]
+        grad_banks = [bank[:].rearrange("q (s r) -> q s r", s=PACK) for bank in product_banks]
 
-        nc.tensor.transpose(grad_banks[1][:, 0, :], row_vecs[:], ident[:])
+        nc.tensor.transpose(out_banks[1][:, 0, :], row_vecs[:], ident[:])
         vec_cols = keep.tile([P, 3 * TILES], F32, name="vec_cols")
-        nc.scalar.copy(vec_cols[:], grad_banks[1][:, 0, 0 : 3 * TILES])
+        nc.scalar.copy(vec_cols[:], out_banks[1][:, 0, 0 : 3 * TILES])
         us_cols = vec_cols[:, 0:TILES]
         neg_us = keep.tile([P, TILES], F32, name="neg_us")
         nc.gpsimd.tensor_scalar(neg_us[:], us_cols, -1.0, 0.0, ALU.mult, ALU.add)
@@ -107,9 +108,9 @@ def tile_attend_gpgent_x_kernel(tc, xT, wT, adv, us, ts, wt, be, offs, out):
             nc.vector.tensor_copy(low_planes[:, t * SLOTS : (t + 1) * SLOTS], w_planes[t][:].indirect(offsets[:]))
         ts_listed = keep.tile([P, SLOTS], F32, name="ts_listed")
         nc.vector.tensor_copy(ts_listed[:], ts_window[:].indirect(offsets[:]))
-        transpose_pairs(grad_banks[0], low_planes[:])
+        transpose_pairs(out_banks[0], low_planes[:])
         low_by_i = keep.tile([P, 2 * P * PACK], BF16, name="low_by_i", align_bytes=64)
-        leave_bank(low_by_i, grad_banks[0][:])
+        leave_bank(low_by_i, out_banks[0][:])
         gathered = staged("gathered", [P, PACK * SLOTS], BF16, WINDOW_SLOT)
         w_by_d = gathered[:].rearrange("p (i t) -> p i t", t=PACK)
         x_halves = [
@@ -121,9 +122,9 @@ def tile_attend_gpgent_x_kernel(tc, xT, wT, adv, us, ts, wt, be, offs, out):
         nc.scalar.copy(ts_rows[:].rearrange("m s q -> m q s"), ts_listed[:].rearrange("m (q s) -> m q s", s=PACK))
         nc.scalar.copy(w_by_d[:, :, 0:2], low_planes[:].rearrange("p (t i) -> p i t", t=2))
         for s in range(PACK):
-            nc.tensor.transpose(grad_banks[2][:, s, :], ts_rows[:, s, :], ident[:])
+            nc.tensor.transpose(out_banks[2][:, s, :], ts_rows[:, s, :], ident[:])
         ts_cols = keep.tile([P, PACK], F32, name="ts_cols")
-        nc.scalar.copy(ts_cols[:], grad_banks[2][:, :, 0])
+        nc.scalar.copy(ts_cols[:], out_banks[2][:, :, 0])
 
         nc.vector.tensor_copy(w_by_d[:, :, 2], w_planes[2][:].indirect(offsets[:]))
         quantize_by_i(0, low_by_i)
@@ -261,11 +262,10 @@ def tile_attend_gpgent_x_kernel(tc, xT, wT, adv, us, ts, wt, be, offs, out):
         g_scales = [keep.tile([P, P], U8, name=f"g_scales{m}", align_bytes=64) for m in range(TILES)]
 
         def gradient(m, rows=slice(0, P)):
-            pairs = (rows.stop - rows.start) // 2
             nc.vector.tensor_tensor(
-                g[m][:, rows, :].rearrange("q (c i) s -> q c s i", i=2),
-                grad_banks[m][:, :, rows].rearrange("q s (c i) -> q c s i", i=2),
-                ts_cols[:].unsqueeze(1).unsqueeze(3).to_broadcast([P, pairs, PACK, 2]),
+                g[m][:, rows, :],
+                grad_banks[m][:, :, rows].rearrange("q s r -> q r s"),
+                ts_cols[:].unsqueeze(1).to_broadcast([P, rows.stop - rows.start, PACK]),
                 ALU.mult,
             )
 
@@ -278,7 +278,7 @@ def tile_attend_gpgent_x_kernel(tc, xT, wT, adv, us, ts, wt, be, offs, out):
 
         def rows_gradient(m):
             nc.tensor.matmul_mx(
-                out=product_banks[m][:],
+                out=out_banks[m][:].rearrange("r t p -> r (t p)"),
                 lhsT=g_codes[m][:].bitcast(E5M2),
                 lhsT_scale=g_scales[m][:],
                 rhs=wi_codes[:].bitcast(E4M3),
@@ -291,7 +291,7 @@ def tile_attend_gpgent_x_kernel(tc, xT, wT, adv, us, ts, wt, be, offs, out):
             for j in range(pieces):
                 part = slice(j * P // pieces, (j + 1) * P // pieces)
                 copy_out = nc.vector.tensor_copy if m == TILES - 1 else nc.scalar.copy
-                copy_out(res[:, part, :], product_banks[m][:].rearrange("r (t p) -> r p t", t=PACK)[:, part, :])
+                copy_out(res[:, part, :], out_banks[m][:].rearrange("r t p -> r p t")[:, part, :])
                 nc.sync.dma_start(
                     out=out[m * P : (m + 1) * P, j * D // pieces : (j + 1) * D // pieces],
                     in_=res[:, part, :].rearrange("r p t -> r (p t)"),
@@ -315,7 +315,7 @@ def tile_attend_gpgent_x_kernel(tc, xT, wT, adv, us, ts, wt, be, offs, out):
         exponentials(1)
         scores(2)
         scores(3)
-        high_bank = product_banks[1][:].rearrange("q (s p) -> q s p", s=PACK)
+        high_bank = out_banks[3][:]
         high_words = high_pairs[:].rearrange("p t u q e -> p (t u q e)").bitcast(F32)
         for j in range(PACK):
             nc.tensor.transpose(high_bank[:, j, :], high_words[:, j * P : (j + 1) * P], ident[:])
@@ -330,11 +330,11 @@ def tile_attend_gpgent_x_kernel(tc, xT, wT, adv, us, ts, wt, be, offs, out):
         entropy_terms(0)
         inverse(2, 3)
         entropy_terms(1)
-        row_ratios(2, 3)
         inverse(3, 4)
-        entropy_terms(2)
-        row_ratios(3, 4)
+        row_ratios(2, 3)
         quantize_by_i(1, high_by_i)
+        row_ratios(3, 4)
+        entropy_terms(2)
         entropy_terms(3)
         gradient(0)
         for m in range(TILES - 2):

@@ -25,6 +25,12 @@ FOLD = T // P
 LINE = 4
 SLOT_BYTES = 4 * T
 WINDOW_SLOT = PACK
+X_SLOT = 0
+ADV_SLOT = 1
+LOW_SLOT = PACK + 1
+MAX_SLOT = PACK + 2
+TERM_BYTES = 4 * SLOTS
+SECOND_GROUP = TERM_BYTES // 2 + 64
 LAST_PIECES = 2
 
 
@@ -71,18 +77,6 @@ def tile_attend_gpgent_x_kernel(tc, xT, wT, adv, us, ts, wt, be, offs, out):
         product_banks = [psum.tile([P, SLOTS], F32, name=f"product{m}") for m in range(TILES)]
         grad_banks = [bank[:].rearrange("q (s r) -> q s r", s=PACK) for bank in product_banks]
 
-        nc.tensor.transpose(out_banks[1][:, 0, :], row_vecs[:], ident[:])
-        vec_cols = keep.tile([P, 3 * TILES], F32, name="vec_cols")
-        nc.scalar.copy(vec_cols[:], out_banks[1][:, 0, 0 : 3 * TILES])
-        us_cols = vec_cols[:, 0:TILES]
-        neg_us = keep.tile([P, TILES], F32, name="neg_us")
-        nc.gpsimd.tensor_scalar(neg_us[:], us_cols, -1.0, 0.0, ALU.mult, ALU.add)
-        adv_scale = keep.tile([P, TILES], F32, name="adv_scale")
-        nc.gpsimd.tensor_tensor(adv_scale[:], neg_us[:], vec_cols[:, TILES : 2 * TILES], ALU.mult)
-        numerators = keep.tile([P, TILES, 3], F32, name="numerators")
-        nc.gpsimd.memset(numerators[:, :, 0], 1.0)
-        nc.gpsimd.tensor_tensor(numerators[:, :, 1], neg_us[:], vec_cols[:, 2 * TILES : 3 * TILES], ALU.mult)
-
         def transpose_pairs(bank, planes):
             words = planes.bitcast(F32)
             for t in range(2):
@@ -103,9 +97,21 @@ def tile_attend_gpgent_x_kernel(tc, xT, wT, adv, us, ts, wt, be, offs, out):
             cols = slice(half * D // 2, (half + 1) * D // 2)
             nc.vector.quantize_mx(out=wi_codes[:, cols].bitcast(E4M3), scales=wi_scales[:, cols], in_=by_i[:])
 
-        low_planes = keep.tile([P, 2 * SLOTS], BF16, name="low_planes", align_bytes=64)
+        low_planes = staged("low_planes", [P, 2 * SLOTS], BF16, LOW_SLOT)
         for t in range(2):
             nc.vector.tensor_copy(low_planes[:, t * SLOTS : (t + 1) * SLOTS], w_planes[t][:].indirect(offsets[:]))
+        x_halves = []
+        for h in range(2):
+            x_halves.append(staged(f"x_half{h}", [P, PACK, R // 2], F32, X_SLOT, h * SLOT_BYTES // 2))
+            nc.sync.dma_start(out=x_halves[h][:], in_=x_view[:, :, h * R // 2 : (h + 1) * R // 2])
+        adv_tiles = []
+        for h in range(2):
+            pair = staged(f"adv_pair{h}", [P, 2 * SLOTS], F32, ADV_SLOT, h * SLOT_BYTES // 2)
+            nc.sync.dma_start(
+                out=pair[:].rearrange("p (e i) -> p e i", e=2),
+                in_=adv[2 * h * P : 2 * (h + 1) * P, :].rearrange("(e p) i -> p e i", e=2),
+            )
+            adv_tiles.extend(pair[:, e * SLOTS : (e + 1) * SLOTS] for e in range(2))
         ts_listed = keep.tile([P, SLOTS], F32, name="ts_listed")
         nc.vector.tensor_copy(ts_listed[:], ts_window[:].indirect(offsets[:]))
         transpose_pairs(out_banks[0], low_planes[:])
@@ -113,37 +119,26 @@ def tile_attend_gpgent_x_kernel(tc, xT, wT, adv, us, ts, wt, be, offs, out):
         leave_bank(low_by_i, out_banks[0][:])
         gathered = staged("gathered", [P, PACK * SLOTS], BF16, WINDOW_SLOT)
         w_by_d = gathered[:].rearrange("p (i t) -> p i t", t=PACK)
-        x_halves = [
-            staged("x_half0", [P, PACK, R // 2], F32, WINDOW_SLOT, SLOT_BYTES // 2),
-            staged("x_half1", [P, PACK, R // 2], F32, 2),
-        ]
-        nc.sync.dma_start(out=x_halves[0][:], in_=x_view[:, :, 0 : R // 2])
         ts_rows = keep.tile([P, PACK, P], F32, name="ts_rows")
         nc.scalar.copy(ts_rows[:].rearrange("m s q -> m q s"), ts_listed[:].rearrange("m (q s) -> m q s", s=PACK))
         nc.scalar.copy(w_by_d[:, :, 0:2], low_planes[:].rearrange("p (t i) -> p i t", t=2))
         for s in range(PACK):
             nc.tensor.transpose(out_banks[2][:, s, :], ts_rows[:, s, :], ident[:])
-        ts_cols = keep.tile([P, PACK], F32, name="ts_cols")
-        nc.scalar.copy(ts_cols[:], out_banks[2][:, :, 0])
+
+        nc.tensor.transpose(out_banks[0][:, 0, :], row_vecs[:], ident[:])
+        vec_cols = staged("vec_cols", [P, 3, TILES], F32, LOW_SLOT, TERM_BYTES // 2)
+        nc.scalar.copy(vec_cols[:].rearrange("p j m -> p (j m)"), out_banks[0][:, 0, 0 : 3 * TILES])
+        us_cols = vec_cols[:, 0, :]
 
         nc.vector.tensor_copy(w_by_d[:, :, 2], w_planes[2][:].indirect(offsets[:]))
         quantize_by_i(0, low_by_i)
-        nc.sync.dma_start(out=x_halves[1][:], in_=x_view[:, :, R // 2 : R])
         for h in range(2):
             nc.vector.tensor_copy(
                 w_by_d[:, h * SLOTS // 2 : (h + 1) * SLOTS // 2, 3],
                 w_planes[3][:].indirect(offsets[:, h * SLOTS // 32 : (h + 1) * SLOTS // 32]),
             )
-        adv_tiles = []
-        for h in range(2):
-            pair = staged(f"adv_pair{h}", [P, 2 * SLOTS], F32, 2 + h, SLOT_BYTES // 2)
-            nc.sync.dma_start(
-                out=pair[:].rearrange("p (e i) -> p e i", e=2),
-                in_=adv[2 * h * P : 2 * (h + 1) * P, :].rearrange("(e p) i -> p e i", e=2),
-            )
-            adv_tiles.extend(pair[:, e * SLOTS : (e + 1) * SLOTS] for e in range(2))
 
-        x_codes = [staged(f"x_codes{h}", [P, 2 * P], U32, 3, h * 2 * P * 4) for h in range(2)]
+        x_codes = [staged(f"x_codes{h}", [P, 2 * P], U32, 3, h * 2 * TERM_BYTES) for h in range(2)]
         x_scales = [keep.tile([P, 2 * P], U8, name=f"x_scales{h}", align_bytes=64) for h in range(2)]
         wd_codes = keep.tile([P, SLOTS], U32, name="wd_codes", align_bytes=64)
         wd_scales = keep.tile([P, SLOTS], U8, name="wd_scales", align_bytes=64)
@@ -156,7 +151,7 @@ def tile_attend_gpgent_x_kernel(tc, xT, wT, adv, us, ts, wt, be, offs, out):
         def quantize_rows(h, cols, grouped):
             nc.vector.quantize_mx(out=x_codes[h][:, cols].bitcast(E4M3), scales=x_scales[h][:, cols], in_=grouped)
 
-        first_grouped = [keep.tile([P, P * PACK], BF16, name=f"x_grouped{e}", align_bytes=64) for e in range(2)]
+        first_grouped = [staged(f"x_grouped{e}", [P, P * PACK], BF16, LOW_SLOT, e * SECOND_GROUP) for e in range(2)]
         for e in range(2):
             group_rows(nc.scalar.copy, first_grouped[e][:], x_halves[0][:, :, e * P : (e + 1) * P])
         for h in range(2):
@@ -167,17 +162,27 @@ def tile_attend_gpgent_x_kernel(tc, xT, wT, adv, us, ts, wt, be, offs, out):
                 in_=gathered[:, PACK * cols.start : PACK * cols.stop],
             )
         quantize_rows(0, slice(0, P), first_grouped[0][:])
-        second_grouped = staged("x_grouped23", [P, 2 * P * PACK], BF16, WINDOW_SLOT, SLOT_BYTES // 2)
+        factors = staged("factors", [P, 4, TILES], F32, 3, TERM_BYTES)
+        nc.vector.scalar_tensor_tensor(
+            factors[:, 0:2, :],
+            vec_cols[:, 1:3, :],
+            -1.0,
+            us_cols.unsqueeze(1).to_broadcast([P, 2, TILES]),
+            ALU.mult,
+            ALU.mult,
+        )
+        nc.vector.memset(factors[:, 3, :], 1.0)
+        second_grouped = staged("x_grouped23", [P, 2 * P * PACK], BF16, X_SLOT)
         group_rows(nc.vector.tensor_copy, second_grouped[:], x_halves[1][:])
         quantize_rows(0, slice(P, 2 * P), first_grouped[1][:])
         quantize_rows(1, slice(0, 2 * P), second_grouped[:])
 
         z = [keep.tile([P, PACK, P], F32, name=f"z{m}") for m in range(TILES)]
         e = [keep.tile([P, PACK, P], F32, name=f"e{m}") for m in range(TILES)]
-        neg_max = [staged(f"neg_max{m}", [P, 1], F32, 1, (m - 1) % TILES * 2 * SLOTS * 2) for m in range(TILES)]
+        neg_max = [staged(f"neg_max{m}", [P, 1], F32, MAX_SLOT, m * TERM_BYTES) for m in range(TILES)]
         totals = keep.tile([P, TILES], F32, name="totals")
         inverses = keep.tile([P, TILES], F32, name="inverses")
-        ratios = keep.tile([P, TILES, 3], F32, name="ratios")
+        ratios = keep.tile([P, 3, TILES], F32, name="ratios")
 
         def add_transposed(m, term, first, last):
             for s in range(PACK):
@@ -216,14 +221,16 @@ def tile_attend_gpgent_x_kernel(tc, xT, wT, adv, us, ts, wt, be, offs, out):
                 e[m][:], z[m][:], ACT.Exp, bias=neg_max[m][:], accum_out=totals[:, m : m + 1]
             )
 
+        a_places = ((X_SLOT, TERM_BYTES), (LOW_SLOT, SECOND_GROUP), (X_SLOT, 2 * TERM_BYTES), (MAX_SLOT, TERM_BYTES))
+
         def adv_term(m):
-            a_term = keep.tile([P, PACK, P], F32, name=f"a_term{m}")
+            a_term = staged(f"a_term{m}", [P, PACK, P], F32, *a_places[m])
             nc.scalar.activation(
                 a_term[:].rearrange("r s q -> r q s"),
                 adv_tiles[m].rearrange("r (q s) -> r q s", s=PACK),
                 ACT.Copy,
-                scale=adv_scale[:, m : m + 1],
-                accum_out=numerators[:, m, 2:3],
+                scale=factors[:, 0, m : m + 1],
+                accum_out=factors[:, 2, m : m + 1],
             )
             add_transposed(m, a_term, True, False)
 
@@ -232,24 +239,25 @@ def tile_attend_gpgent_x_kernel(tc, xT, wT, adv, us, ts, wt, be, offs, out):
 
         def row_ratios(first, last):
             nc.vector.scalar_tensor_tensor(
-                ratios[:, first:last, :],
-                numerators[:, first:last, :],
+                ratios[:, :, first:last],
+                factors[:, 1:4, first:last],
                 -1.0,
-                inverses[:, first:last].unsqueeze(2).to_broadcast([P, last - first, 3]),
+                inverses[:, first:last].unsqueeze(1).to_broadcast([P, 3, last - first]),
                 ALU.mult,
                 ALU.mult,
             )
 
         def entropy_terms(m):
-            ratio = ratios[:, m, :]
             u_term = keep.tile([P, PACK, P], F32, name=f"u_term{m}")
             u_sum = keep.tile([P, 1], F32, name=f"u_sum{m}")
             nc.vector.scalar_tensor_tensor(
-                u_term[:], z[m][:], ratio[:, 1:2], e[m][:], ALU.mult, ALU.mult, accum_out=u_sum[:]
+                u_term[:], z[m][:], ratios[:, 0, m : m + 1], e[m][:], ALU.mult, ALU.mult, accum_out=u_sum[:]
             )
             add_transposed(m, u_term, False, False)
             e_scale = keep.tile([P, 1], F32, name=f"e_scale{m}")
-            nc.scalar.activation(e_scale[:], u_sum[:], ACT.Identity, bias=ratio[:, 2:3], scale=ratio[:, 0:1])
+            nc.scalar.activation(
+                e_scale[:], u_sum[:], ACT.Identity, bias=ratios[:, 1, m : m + 1], scale=ratios[:, 2, m : m + 1]
+            )
             e_term = keep.tile([P, PACK, P], F32, name=f"e_term{m}")
             pieces = LAST_PIECES if m == TILES - 1 else 1
             for j in range(pieces):
@@ -261,7 +269,7 @@ def tile_attend_gpgent_x_kernel(tc, xT, wT, adv, us, ts, wt, be, offs, out):
         g_codes = [keep.tile([P, P], U32, name=f"g_codes{m}", align_bytes=64) for m in range(TILES)]
         g_scales = [keep.tile([P, P], U8, name=f"g_scales{m}", align_bytes=64) for m in range(TILES)]
 
-        def gradient(m, rows=slice(0, P)):
+        def gradient(m, ts_cols, rows=slice(0, P)):
             nc.vector.tensor_tensor(
                 g[m][:, rows, :],
                 grad_banks[m][:, :, rows].rearrange("q s r -> q r s"),
@@ -297,7 +305,15 @@ def tile_attend_gpgent_x_kernel(tc, xT, wT, adv, us, ts, wt, be, offs, out):
                     in_=res[:, part, :].rearrange("r p t -> r (p t)"),
                 )
 
-        high_pairs = staged("high_pairs", [P, 2, 2, P, 2], BF16, WINDOW_SLOT, SLOT_BYTES // 2)
+        scores(0)
+        scores(1)
+        adv_term(0)
+        adv_term(1)
+        exponentials(0)
+        exponentials(1)
+        scores(2)
+        scores(3)
+        high_pairs = staged("high_pairs", [P, 2, 2, P, 2], BF16, 3, 2 * TERM_BYTES)
         for t in range(2):
             nc.gpsimd.tensor_scalar(
                 high_pairs[:, t, :, :, :],
@@ -307,21 +323,13 @@ def tile_attend_gpgent_x_kernel(tc, xT, wT, adv, us, ts, wt, be, offs, out):
                 ALU.mult,
                 ALU.add,
             )
-        scores(0)
-        scores(1)
-        adv_term(0)
-        adv_term(1)
-        exponentials(0)
-        exponentials(1)
-        scores(2)
-        scores(3)
         high_bank = out_banks[3][:]
         high_words = high_pairs[:].rearrange("p t u q e -> p (t u q e)").bitcast(F32)
         for j in range(PACK):
             nc.tensor.transpose(high_bank[:, j, :], high_words[:, j * P : (j + 1) * P], ident[:])
         adv_term(2)
         adv_term(3)
-        high_by_i = staged("high_by_i", [P, 2 * P * PACK], BF16, 1)
+        high_by_i = keep.tile([P, 2 * P * PACK], BF16, name="high_by_i", align_bytes=64)
         leave_bank(high_by_i, high_bank)
         inverse(0, 2)
         exponentials(2)
@@ -330,22 +338,24 @@ def tile_attend_gpgent_x_kernel(tc, xT, wT, adv, us, ts, wt, be, offs, out):
         entropy_terms(0)
         inverse(2, 3)
         entropy_terms(1)
-        inverse(3, 4)
         row_ratios(2, 3)
-        quantize_by_i(1, high_by_i)
-        row_ratios(3, 4)
+        inverse(3, 4)
+        ts_cols = staged("ts_cols", [P, PACK], F32, MAX_SLOT, 2 * TERM_BYTES)
+        nc.vector.tensor_copy(ts_cols[:], out_banks[2][:, :, 0])
         entropy_terms(2)
+        row_ratios(3, 4)
+        quantize_by_i(1, high_by_i)
         entropy_terms(3)
-        gradient(0)
+        gradient(0, ts_cols)
         for m in range(TILES - 2):
-            gradient(m + 1)
+            gradient(m + 1, ts_cols)
             quantize_gradient(m)
             rows_gradient(m)
         halves = (slice(0, P // 2), slice(P // 2, P))
-        gradient(3, halves[0])
+        gradient(3, ts_cols, halves[0])
         quantize_gradient(2)
         rows_gradient(2)
-        gradient(3, halves[1])
+        gradient(3, ts_cols, halves[1])
         for rows in halves:
             quantize_gradient(3, rows)
         rows_gradient(3)

@@ -105,13 +105,9 @@ def tile_attend_gpgent_x_kernel(tc, xT, wT, adv, us, ts, wt, be, offs, out):
             x_halves.append(staged(f"x_half{h}", [P, PACK, R // 2], F32, X_SLOT, h * SLOT_BYTES // 2))
             nc.sync.dma_start(out=x_halves[h][:], in_=x_view[:, :, h * R // 2 : (h + 1) * R // 2])
         adv_tiles = []
-        for h in range(2):
-            pair = staged(f"adv_pair{h}", [P, 2 * SLOTS], F32, ADV_SLOT, h * SLOT_BYTES // 2)
-            nc.sync.dma_start(
-                out=pair[:].rearrange("p (e i) -> p e i", e=2),
-                in_=adv[2 * h * P : 2 * (h + 1) * P, :].rearrange("(e p) i -> p e i", e=2),
-            )
-            adv_tiles.extend(pair[:, e * SLOTS : (e + 1) * SLOTS] for e in range(2))
+        for m in range(TILES):
+            adv_tiles.append(staged(f"adv{m}", [P, SLOTS], F32, ADV_SLOT, m * TERM_BYTES))
+            nc.sync.dma_start(out=adv_tiles[m][:], in_=adv[m * P : (m + 1) * P, :])
         ts_listed = keep.tile([P, SLOTS], F32, name="ts_listed")
         nc.vector.tensor_copy(ts_listed[:], ts_window[:].indirect(offsets[:]))
         transpose_pairs(out_banks[0], low_planes[:])
@@ -162,7 +158,7 @@ def tile_attend_gpgent_x_kernel(tc, xT, wT, adv, us, ts, wt, be, offs, out):
                 in_=gathered[:, PACK * cols.start : PACK * cols.stop],
             )
         quantize_rows(0, slice(0, P), first_grouped[0][:])
-        factors = staged("factors", [P, 4, TILES], F32, 3, TERM_BYTES)
+        factors = staged("factors", [P, 3, TILES], F32, 3, TERM_BYTES)
         nc.vector.scalar_tensor_tensor(
             factors[:, 0:2, :],
             vec_cols[:, 1:3, :],
@@ -171,7 +167,7 @@ def tile_attend_gpgent_x_kernel(tc, xT, wT, adv, us, ts, wt, be, offs, out):
             ALU.mult,
             ALU.mult,
         )
-        nc.vector.memset(factors[:, 3, :], 1.0)
+        nc.vector.memset(factors[:, 2, :], 1.0)
         second_grouped = staged("x_grouped23", [P, 2 * P * PACK], BF16, X_SLOT)
         group_rows(nc.vector.tensor_copy, second_grouped[:], x_halves[1][:])
         quantize_rows(0, slice(P, 2 * P), first_grouped[1][:])
@@ -182,7 +178,9 @@ def tile_attend_gpgent_x_kernel(tc, xT, wT, adv, us, ts, wt, be, offs, out):
         neg_max = [staged(f"neg_max{m}", [P, 1], F32, MAX_SLOT, m * TERM_BYTES) for m in range(TILES)]
         totals = keep.tile([P, TILES], F32, name="totals")
         inverses = keep.tile([P, TILES], F32, name="inverses")
-        ratios = keep.tile([P, 3, TILES], F32, name="ratios")
+        ratios = keep.tile([P, 2, TILES], F32, name="ratios")
+        a_sums = keep.tile([P, TILES], F32, name="a_sums")
+        u_sums = [keep.tile([P, 1], F32, name=f"u_sum{m}") for m in range(TILES)]
 
         def add_transposed(m, term, first, last):
             for s in range(PACK):
@@ -227,10 +225,10 @@ def tile_attend_gpgent_x_kernel(tc, xT, wT, adv, us, ts, wt, be, offs, out):
             a_term = staged(f"a_term{m}", [P, PACK, P], F32, *a_places[m])
             nc.scalar.activation(
                 a_term[:].rearrange("r s q -> r q s"),
-                adv_tiles[m].rearrange("r (q s) -> r q s", s=PACK),
+                adv_tiles[m][:].rearrange("r (q s) -> r q s", s=PACK),
                 ACT.Copy,
                 scale=factors[:, 0, m : m + 1],
-                accum_out=factors[:, 2, m : m + 1],
+                accum_out=a_sums[:, m : m + 1],
             )
             add_transposed(m, a_term, True, False)
 
@@ -240,23 +238,24 @@ def tile_attend_gpgent_x_kernel(tc, xT, wT, adv, us, ts, wt, be, offs, out):
         def row_ratios(first, last):
             nc.vector.scalar_tensor_tensor(
                 ratios[:, :, first:last],
-                factors[:, 1:4, first:last],
+                factors[:, 1:3, first:last],
                 -1.0,
-                inverses[:, first:last].unsqueeze(1).to_broadcast([P, 3, last - first]),
+                inverses[:, first:last].unsqueeze(1).to_broadcast([P, 2, last - first]),
                 ALU.mult,
                 ALU.mult,
             )
 
         def entropy_terms(m):
             u_term = keep.tile([P, PACK, P], F32, name=f"u_term{m}")
-            u_sum = keep.tile([P, 1], F32, name=f"u_sum{m}")
             nc.vector.scalar_tensor_tensor(
-                u_term[:], z[m][:], ratios[:, 0, m : m + 1], e[m][:], ALU.mult, ALU.mult, accum_out=u_sum[:]
+                u_term[:], z[m][:], ratios[:, 0, m : m + 1], e[m][:], ALU.mult, ALU.mult, accum_out=u_sums[m][:]
             )
             add_transposed(m, u_term, False, False)
+
+        def exponential_term(m):
             e_scale = keep.tile([P, 1], F32, name=f"e_scale{m}")
-            nc.scalar.activation(
-                e_scale[:], u_sum[:], ACT.Identity, bias=ratios[:, 1, m : m + 1], scale=ratios[:, 2, m : m + 1]
+            nc.vector.tensor_scalar(
+                e_scale[:], u_sums[m][:], a_sums[:, m : m + 1], ratios[:, 1, m : m + 1], ALU.add, ALU.mult
             )
             e_term = keep.tile([P, PACK, P], F32, name=f"e_term{m}")
             pieces = LAST_PIECES if m == TILES - 1 else 1
@@ -335,18 +334,22 @@ def tile_attend_gpgent_x_kernel(tc, xT, wT, adv, us, ts, wt, be, offs, out):
         exponentials(2)
         row_ratios(0, 2)
         exponentials(3)
+        ts_cols = staged("ts_cols", [P, PACK], F32, MAX_SLOT, 3 * TERM_BYTES)
+        nc.scalar.copy(ts_cols[:], out_banks[2][:, :, 0])
         entropy_terms(0)
         inverse(2, 3)
         entropy_terms(1)
         row_ratios(2, 3)
+        exponential_term(0)
         inverse(3, 4)
-        ts_cols = staged("ts_cols", [P, PACK], F32, MAX_SLOT, 2 * TERM_BYTES)
-        nc.vector.tensor_copy(ts_cols[:], out_banks[2][:, :, 0])
+        exponential_term(1)
         entropy_terms(2)
         row_ratios(3, 4)
         quantize_by_i(1, high_by_i)
+        exponential_term(2)
         entropy_terms(3)
         gradient(0, ts_cols)
+        exponential_term(3)
         for m in range(TILES - 2):
             gradient(m + 1, ts_cols)
             quantize_gradient(m)

@@ -158,7 +158,7 @@ def tile_attend_gpgent_x_kernel(tc, xT, wT, adv, us, ts, wt, be, offs, out):
                 in_=gathered[:, PACK * cols.start : PACK * cols.stop],
             )
         quantize_rows(0, slice(0, P), first_grouped[0][:])
-        factors = staged("factors", [P, 3, TILES], F32, 3, TERM_BYTES)
+        factors = staged("factors", [P, 4, TILES], F32, 3, TERM_BYTES)
         nc.vector.scalar_tensor_tensor(
             factors[:, 0:2, :],
             vec_cols[:, 1:3, :],
@@ -169,8 +169,8 @@ def tile_attend_gpgent_x_kernel(tc, xT, wT, adv, us, ts, wt, be, offs, out):
         )
         nc.vector.memset(factors[:, 2, :], 1.0)
         second_grouped = staged("x_grouped23", [P, 2 * P * PACK], BF16, X_SLOT)
-        group_rows(nc.vector.tensor_copy, second_grouped[:], x_halves[1][:])
         quantize_rows(0, slice(P, 2 * P), first_grouped[1][:])
+        group_rows(nc.vector.tensor_copy, second_grouped[:], x_halves[1][:])
         quantize_rows(1, slice(0, 2 * P), second_grouped[:])
 
         z = [keep.tile([P, PACK, P], F32, name=f"z{m}") for m in range(TILES)]
@@ -178,8 +178,7 @@ def tile_attend_gpgent_x_kernel(tc, xT, wT, adv, us, ts, wt, be, offs, out):
         neg_max = [staged(f"neg_max{m}", [P, 1], F32, MAX_SLOT, m * TERM_BYTES) for m in range(TILES)]
         totals = keep.tile([P, TILES], F32, name="totals")
         inverses = keep.tile([P, TILES], F32, name="inverses")
-        ratios = keep.tile([P, 2, TILES], F32, name="ratios")
-        a_sums = keep.tile([P, TILES], F32, name="a_sums")
+        ratios = keep.tile([P, 3, TILES], F32, name="ratios")
         u_sums = [keep.tile([P, 1], F32, name=f"u_sum{m}") for m in range(TILES)]
 
         def add_transposed(m, term, first, last):
@@ -204,6 +203,8 @@ def tile_attend_gpgent_x_kernel(tc, xT, wT, adv, us, ts, wt, be, offs, out):
                 start=True,
                 stop=True,
             )
+
+        def scaled_scores(m):
             nc.vector.scalar_tensor_tensor(
                 z[m][:],
                 product_banks[m][:].rearrange("r (q s) -> r s q", s=PACK),
@@ -228,7 +229,7 @@ def tile_attend_gpgent_x_kernel(tc, xT, wT, adv, us, ts, wt, be, offs, out):
                 adv_tiles[m][:].rearrange("r (q s) -> r q s", s=PACK),
                 ACT.Copy,
                 scale=factors[:, 0, m : m + 1],
-                accum_out=a_sums[:, m : m + 1],
+                accum_out=factors[:, 3, m : m + 1],
             )
             add_transposed(m, a_term, True, False)
 
@@ -238,9 +239,9 @@ def tile_attend_gpgent_x_kernel(tc, xT, wT, adv, us, ts, wt, be, offs, out):
         def row_ratios(first, last):
             nc.vector.scalar_tensor_tensor(
                 ratios[:, :, first:last],
-                factors[:, 1:3, first:last],
+                factors[:, 1:4, first:last],
                 -1.0,
-                inverses[:, first:last].unsqueeze(1).to_broadcast([P, 2, last - first]),
+                inverses[:, first:last].unsqueeze(1).to_broadcast([P, 3, last - first]),
                 ALU.mult,
                 ALU.mult,
             )
@@ -254,9 +255,11 @@ def tile_attend_gpgent_x_kernel(tc, xT, wT, adv, us, ts, wt, be, offs, out):
 
         def exponential_term(m):
             e_scale = keep.tile([P, 1], F32, name=f"e_scale{m}")
-            nc.vector.tensor_scalar(
-                e_scale[:], u_sums[m][:], a_sums[:, m : m + 1], ratios[:, 1, m : m + 1], ALU.add, ALU.mult
-            )
+            neg_inverse, a_part = ratios[:, 1, m : m + 1], ratios[:, 2, m : m + 1]
+            if m in (0, TILES - 1):
+                nc.scalar.activation(e_scale[:], u_sums[m][:], ACT.Identity, bias=a_part, scale=neg_inverse)
+            else:
+                nc.vector.tensor_scalar(e_scale[:], u_sums[m][:], neg_inverse, a_part, ALU.mult, ALU.add)
             e_term = keep.tile([P, PACK, P], F32, name=f"e_term{m}")
             pieces = LAST_PIECES if m == TILES - 1 else 1
             for j in range(pieces):
@@ -304,14 +307,16 @@ def tile_attend_gpgent_x_kernel(tc, xT, wT, adv, us, ts, wt, be, offs, out):
                     in_=res[:, part, :].rearrange("r p t -> r (p t)"),
                 )
 
-        scores(0)
-        scores(1)
+        for m in range(TILES):
+            scores(m)
+        scaled_scores(0)
+        scaled_scores(1)
         adv_term(0)
         adv_term(1)
         exponentials(0)
         exponentials(1)
-        scores(2)
-        scores(3)
+        scaled_scores(2)
+        scaled_scores(3)
         high_pairs = staged("high_pairs", [P, 2, 2, P, 2], BF16, 3, 2 * TERM_BYTES)
         for t in range(2):
             nc.gpsimd.tensor_scalar(
@@ -328,32 +333,33 @@ def tile_attend_gpgent_x_kernel(tc, xT, wT, adv, us, ts, wt, be, offs, out):
             nc.tensor.transpose(high_bank[:, j, :], high_words[:, j * P : (j + 1) * P], ident[:])
         adv_term(2)
         adv_term(3)
-        high_by_i = keep.tile([P, 2 * P * PACK], BF16, name="high_by_i", align_bytes=64)
+        high_by_i = staged("high_by_i", [P, 2 * P * PACK], BF16, ADV_SLOT, 3 * TERM_BYTES)
         leave_bank(high_by_i, high_bank)
         inverse(0, 2)
         exponentials(2)
         row_ratios(0, 2)
         exponentials(3)
-        ts_cols = staged("ts_cols", [P, PACK], F32, MAX_SLOT, 3 * TERM_BYTES)
+        ts_cols = staged("ts_cols", [P, PACK], F32, MAX_SLOT)
         nc.scalar.copy(ts_cols[:], out_banks[2][:, :, 0])
         entropy_terms(0)
         inverse(2, 3)
+        exponential_term(0)
         entropy_terms(1)
         row_ratios(2, 3)
-        exponential_term(0)
         inverse(3, 4)
         exponential_term(1)
         entropy_terms(2)
         row_ratios(3, 4)
-        quantize_by_i(1, high_by_i)
         exponential_term(2)
         entropy_terms(3)
-        gradient(0, ts_cols)
+        quantize_by_i(1, high_by_i)
         exponential_term(3)
-        for m in range(TILES - 2):
-            gradient(m + 1, ts_cols)
+        for m in range(2):
+            gradient(m, ts_cols)
+        for m in range(2):
             quantize_gradient(m)
             rows_gradient(m)
+        gradient(2, ts_cols)
         halves = (slice(0, P // 2), slice(P // 2, P))
         gradient(3, ts_cols, halves[0])
         quantize_gradient(2)

@@ -341,6 +341,16 @@ def tile_attend_gpgent_x_kernel(tc, xT, wT, adv, us, ts, wt, be, offs, out):
         exponentials(3)
         ts_cols = staged("ts_cols", [P, PACK], F32, MAX_SLOT)
         nc.scalar.copy(ts_cols[:], out_banks[2][:, :, 0])
+        for bank in out_banks[2:4]:
+            nc.tensor.matmul_mx(
+                out=bank[:].rearrange("r t p -> r (t p)"),
+                lhsT=x_codes[0][:, 0:P].bitcast(E4M3),
+                lhsT_scale=x_scales[0][:, 0:P],
+                rhs=wd_codes[:].bitcast(E4M3),
+                rhs_scale=wd_scales[:],
+                start=True,
+                stop=True,
+            )
         entropy_terms(0)
         inverse(2, 3)
         exponential_term(0)

@@ -30,7 +30,7 @@ ADV_SLOT = 1
 LOW_SLOT = PACK + 1
 MAX_SLOT = PACK + 2
 TERM_BYTES = 4 * SLOTS
-SECOND_GROUP = TERM_BYTES // 2 + 64
+GROUP_BYTES = 2 * P * PACK
 LAST_PIECES = 2
 
 
@@ -53,14 +53,14 @@ def tile_attend_gpgent_x_kernel(tc, xT, wT, adv, us, ts, wt, be, offs, out):
         w_planes = [staged(f"w_plane{t}", [P, T], F32, t) for t in range(PACK)]
         nc.sync.dma_start(out=w_planes[0][:], in_=w_view[:, 0, :])
         nc.sync.dma_start(offsets[:], offs)
-        for t in range(1, PACK):
-            nc.sync.dma_start(out=w_planes[t][:], in_=w_view[:, t, :])
         row_vecs = keep.tile([P, P], F32, name="row_vecs")
         nc.gpsimd.memset(row_vecs[:], 0.0)
         for j, vec in enumerate((us, wt, be)):
-            nc.scalar.dma_start(
+            nc.sync.dma_start(
                 out=row_vecs[j * TILES : (j + 1) * TILES, :], in_=vec.rearrange("(m p) o -> m (p o)", p=P)
             )
+        for t in range(1, PACK):
+            nc.sync.dma_start(out=w_planes[t][:], in_=w_view[:, t, :])
         ident = keep.tile([P, P], F32, name="ident")
         make_identity(nc, ident[:])
 
@@ -74,6 +74,11 @@ def tile_attend_gpgent_x_kernel(tc, xT, wT, adv, us, ts, wt, be, offs, out):
             nc.scalar.activation(
                 window_view[:, :, a * PACK : (a + 1) * PACK], spread[:].rearrange("m j p -> m p j"), ACT.Copy
             )
+        vec_bank = psum.tile([P, P], F32, name=f"product{TILES - 1}")
+        nc.tensor.transpose(vec_bank[:], row_vecs[:], ident[:])
+        vec_cols = keep.tile([P, 3, TILES], F32, name="vec_cols")
+        nc.scalar.copy(vec_cols[:].rearrange("p j m -> p (j m)"), vec_bank[:, 0 : 3 * TILES])
+        us_cols = vec_cols[:, 0, :]
         product_banks = [psum.tile([P, SLOTS], F32, name=f"product{m}") for m in range(TILES)]
         grad_banks = [bank[:].rearrange("q (s r) -> q s r", s=PACK) for bank in product_banks]
 
@@ -120,13 +125,20 @@ def tile_attend_gpgent_x_kernel(tc, xT, wT, adv, us, ts, wt, be, offs, out):
         nc.scalar.copy(w_by_d[:, :, 0:2], low_planes[:].rearrange("p (t i) -> p i t", t=2))
         for s in range(PACK):
             nc.tensor.transpose(out_banks[2][:, s, :], ts_rows[:, s, :], ident[:])
-
-        nc.tensor.transpose(out_banks[0][:, 0, :], row_vecs[:], ident[:])
-        vec_cols = staged("vec_cols", [P, 3, TILES], F32, LOW_SLOT, TERM_BYTES // 2)
-        nc.scalar.copy(vec_cols[:].rearrange("p j m -> p (j m)"), out_banks[0][:, 0, 0 : 3 * TILES])
-        us_cols = vec_cols[:, 0, :]
+        ts_cols = keep.tile([P, PACK], F32, name="ts_cols")
+        nc.scalar.copy(ts_cols[:], out_banks[2][:, :, 0])
 
         nc.vector.tensor_copy(w_by_d[:, :, 2], w_planes[2][:].indirect(offsets[:]))
+        factors = keep.tile([P, 4, TILES], F32, name="factors")
+        nc.vector.scalar_tensor_tensor(
+            factors[:, 0:2, :],
+            vec_cols[:, 1:3, :],
+            -1.0,
+            us_cols.unsqueeze(1).to_broadcast([P, 2, TILES]),
+            ALU.mult,
+            ALU.mult,
+        )
+        nc.vector.memset(factors[:, 2, :], 1.0)
         quantize_by_i(0, low_by_i)
         for h in range(2):
             nc.vector.tensor_copy(
@@ -147,30 +159,26 @@ def tile_attend_gpgent_x_kernel(tc, xT, wT, adv, us, ts, wt, be, offs, out):
         def quantize_rows(h, cols, grouped):
             nc.vector.quantize_mx(out=x_codes[h][:, cols].bitcast(E4M3), scales=x_scales[h][:, cols], in_=grouped)
 
-        first_grouped = [staged(f"x_grouped{e}", [P, P * PACK], BF16, LOW_SLOT, e * SECOND_GROUP) for e in range(2)]
+        first_grouped = [
+            staged(f"x_grouped{e}", [P, P * PACK], BF16, LOW_SLOT, (1 - e) * GROUP_BYTES) for e in range(2)
+        ]
         for e in range(2):
             group_rows(nc.scalar.copy, first_grouped[e][:], x_halves[0][:, :, e * P : (e + 1) * P])
-        for h in range(2):
+
+        def quantize_by_d(h):
             cols = slice(h * SLOTS // 2, (h + 1) * SLOTS // 2)
             nc.vector.quantize_mx(
                 out=wd_codes[:, cols].bitcast(E4M3),
                 scales=wd_scales[:, cols],
                 in_=gathered[:, PACK * cols.start : PACK * cols.stop],
             )
+
+        quantize_by_d(0)
         quantize_rows(0, slice(0, P), first_grouped[0][:])
-        factors = staged("factors", [P, 4, TILES], F32, 3, TERM_BYTES)
-        nc.vector.scalar_tensor_tensor(
-            factors[:, 0:2, :],
-            vec_cols[:, 1:3, :],
-            -1.0,
-            us_cols.unsqueeze(1).to_broadcast([P, 2, TILES]),
-            ALU.mult,
-            ALU.mult,
-        )
-        nc.vector.memset(factors[:, 2, :], 1.0)
-        second_grouped = staged("x_grouped23", [P, 2 * P * PACK], BF16, X_SLOT)
-        quantize_rows(0, slice(P, 2 * P), first_grouped[1][:])
+        quantize_by_d(1)
+        second_grouped = staged("x_grouped23", [P, 2 * P * PACK], BF16, LOW_SLOT, GROUP_BYTES)
         group_rows(nc.vector.tensor_copy, second_grouped[:], x_halves[1][:])
+        quantize_rows(0, slice(P, 2 * P), first_grouped[1][:])
         quantize_rows(1, slice(0, 2 * P), second_grouped[:])
 
         z = [keep.tile([P, PACK, P], F32, name=f"z{m}") for m in range(TILES)]
@@ -220,10 +228,8 @@ def tile_attend_gpgent_x_kernel(tc, xT, wT, adv, us, ts, wt, be, offs, out):
                 e[m][:], z[m][:], ACT.Exp, bias=neg_max[m][:], accum_out=totals[:, m : m + 1]
             )
 
-        a_places = ((X_SLOT, TERM_BYTES), (LOW_SLOT, SECOND_GROUP), (X_SLOT, 2 * TERM_BYTES), (MAX_SLOT, TERM_BYTES))
-
         def adv_term(m):
-            a_term = staged(f"a_term{m}", [P, PACK, P], F32, *a_places[m])
+            a_term = staged(f"a_term{m}", [P, PACK, P], F32, X_SLOT, m * TERM_BYTES)
             nc.scalar.activation(
                 a_term[:].rearrange("r s q -> r q s"),
                 adv_tiles[m][:].rearrange("r (q s) -> r q s", s=PACK),
@@ -231,7 +237,7 @@ def tile_attend_gpgent_x_kernel(tc, xT, wT, adv, us, ts, wt, be, offs, out):
                 scale=factors[:, 0, m : m + 1],
                 accum_out=factors[:, 3, m : m + 1],
             )
-            add_transposed(m, a_term, True, False)
+            return a_term
 
         def inverse(first, last):
             nc.vector.reciprocal(inverses[:, first:last], totals[:, first:last])
@@ -256,7 +262,7 @@ def tile_attend_gpgent_x_kernel(tc, xT, wT, adv, us, ts, wt, be, offs, out):
         def exponential_term(m):
             e_scale = keep.tile([P, 1], F32, name=f"e_scale{m}")
             neg_inverse, a_part = ratios[:, 1, m : m + 1], ratios[:, 2, m : m + 1]
-            if m in (0, TILES - 1):
+            if m != 1:
                 nc.scalar.activation(e_scale[:], u_sums[m][:], ACT.Identity, bias=a_part, scale=neg_inverse)
             else:
                 nc.vector.tensor_scalar(e_scale[:], u_sums[m][:], neg_inverse, a_part, ALU.mult, ALU.add)
@@ -309,15 +315,16 @@ def tile_attend_gpgent_x_kernel(tc, xT, wT, adv, us, ts, wt, be, offs, out):
 
         for m in range(TILES):
             scores(m)
+        a_terms = [adv_term(m) for m in range(TILES)]
         scaled_scores(0)
         scaled_scores(1)
-        adv_term(0)
-        adv_term(1)
+        for m in range(2):
+            add_transposed(m, a_terms[m], True, False)
         exponentials(0)
         exponentials(1)
         scaled_scores(2)
         scaled_scores(3)
-        high_pairs = staged("high_pairs", [P, 2, 2, P, 2], BF16, 3, 2 * TERM_BYTES)
+        high_pairs = staged("high_pairs", [P, 2, 2, P, 2], BF16, LOW_SLOT, GROUP_BYTES)
         for t in range(2):
             nc.gpsimd.tensor_scalar(
                 high_pairs[:, t, :, :, :],
@@ -331,50 +338,42 @@ def tile_attend_gpgent_x_kernel(tc, xT, wT, adv, us, ts, wt, be, offs, out):
         high_words = high_pairs[:].rearrange("p t u q e -> p (t u q e)").bitcast(F32)
         for j in range(PACK):
             nc.tensor.transpose(high_bank[:, j, :], high_words[:, j * P : (j + 1) * P], ident[:])
-        adv_term(2)
-        adv_term(3)
-        high_by_i = staged("high_by_i", [P, 2 * P * PACK], BF16, ADV_SLOT, 3 * TERM_BYTES)
+        high_by_i = staged("high_by_i", [P, 2 * P * PACK], BF16, MAX_SLOT)
         leave_bank(high_by_i, high_bank)
-        inverse(0, 2)
         exponentials(2)
-        row_ratios(0, 2)
+        inverse(0, 2)
         exponentials(3)
-        ts_cols = staged("ts_cols", [P, PACK], F32, MAX_SLOT)
-        nc.scalar.copy(ts_cols[:], out_banks[2][:, :, 0])
-        for bank in out_banks[2:4]:
+        row_ratios(0, 2)
+        quantize_by_i(1, high_by_i)
+        for m in range(2, TILES):
+            add_transposed(m, a_terms[m], True, False)
+        for bank in out_banks[1:3]:
             nc.tensor.matmul_mx(
                 out=bank[:].rearrange("r t p -> r (t p)"),
                 lhsT=x_codes[0][:, 0:P].bitcast(E4M3),
                 lhsT_scale=x_scales[0][:, 0:P],
-                rhs=wd_codes[:].bitcast(E4M3),
-                rhs_scale=wd_scales[:],
+                rhs=wi_codes[:].bitcast(E4M3),
+                rhs_scale=wi_scales[:],
                 start=True,
                 stop=True,
             )
         entropy_terms(0)
-        inverse(2, 3)
+        inverse(2, 4)
         exponential_term(0)
         entropy_terms(1)
-        row_ratios(2, 3)
-        inverse(3, 4)
+        row_ratios(2, 4)
         exponential_term(1)
         entropy_terms(2)
-        row_ratios(3, 4)
         exponential_term(2)
         entropy_terms(3)
-        quantize_by_i(1, high_by_i)
         exponential_term(3)
-        for m in range(2):
-            gradient(m, ts_cols)
-        for m in range(2):
-            quantize_gradient(m)
-            rows_gradient(m)
-        gradient(2, ts_cols)
         halves = (slice(0, P // 2), slice(P // 2, P))
-        gradient(3, ts_cols, halves[0])
-        quantize_gradient(2)
-        rows_gradient(2)
-        gradient(3, ts_cols, halves[1])
+        gradient(0, ts_cols)
+        for m in range(1, TILES):
+            gradient(m, ts_cols, halves[0])
+            quantize_gradient(m - 1)
+            rows_gradient(m - 1)
+            gradient(m, ts_cols, halves[1])
         for rows in halves:
-            quantize_gradient(3, rows)
-        rows_gradient(3)
+            quantize_gradient(TILES - 1, rows)
+        rows_gradient(TILES - 1)

@@ -47,7 +47,7 @@ def tile_attend_gpgent_x_kernel(tc, xT, wT, adv, us, ts, wt, be, offs, out):
 
         offsets = keep.tile([P, SLOTS // 16], U16, name="offsets")
         ts_folded = keep.tile([P, FOLD], F32, name="ts_folded")
-        nc.sync.dma_start(out=ts_folded[:], in_=ts[0:1, :].rearrange("o (p j) -> (o p) j", p=P))
+        nc.scalar.dma_start(out=ts_folded[:], in_=ts[0:1, :].rearrange("o (p j) -> (o p) j", p=P))
         w_view = wT.rearrange("(p t) c -> p t c", t=PACK)
         x_view = xT.rearrange("(p t) r -> p t r", t=PACK)
         w_planes = [staged(f"w_plane{t}", [P, T], F32, t) for t in range(PACK)]
@@ -56,7 +56,7 @@ def tile_attend_gpgent_x_kernel(tc, xT, wT, adv, us, ts, wt, be, offs, out):
         row_vecs = keep.tile([P, P], F32, name="row_vecs")
         nc.gpsimd.memset(row_vecs[:], 0.0)
         for j, vec in enumerate((us, wt, be)):
-            nc.sync.dma_start(
+            nc.scalar.dma_start(
                 out=row_vecs[j * TILES : (j + 1) * TILES, :], in_=vec.rearrange("(m p) o -> m (p o)", p=P)
             )
         for t in range(1, PACK):
@@ -177,9 +177,10 @@ def tile_attend_gpgent_x_kernel(tc, xT, wT, adv, us, ts, wt, be, offs, out):
         quantize_rows(0, slice(0, P), first_grouped[0][:])
         quantize_by_d(1)
         second_grouped = staged("x_grouped23", [P, 2 * P * PACK], BF16, LOW_SLOT, GROUP_BYTES)
-        group_rows(nc.vector.tensor_copy, second_grouped[:], x_halves[1][:])
+        late_grouped = [second_grouped[:, e * P * PACK : (e + 1) * P * PACK] for e in range(2)]
+        group_rows(nc.vector.tensor_copy, late_grouped[0], x_halves[1][:, :, 0:P])
         quantize_rows(0, slice(P, 2 * P), first_grouped[1][:])
-        quantize_rows(1, slice(0, 2 * P), second_grouped[:])
+        group_rows(nc.scalar.copy, late_grouped[1], x_halves[1][:, :, P : 2 * P])
 
         z = [keep.tile([P, PACK, P], F32, name=f"z{m}") for m in range(TILES)]
         e = [keep.tile([P, PACK, P], F32, name=f"e{m}") for m in range(TILES)]
@@ -200,24 +201,29 @@ def tile_attend_gpgent_x_kernel(tc, xT, wT, adv, us, ts, wt, be, offs, out):
                     stop=(last and s == PACK - 1),
                 )
 
-        def scores(m):
+        def score_bank(m, slots):
+            bank = out_banks[m][:].rearrange("r t p -> r (t p)") if slots.start else product_banks[m][:]
+            return bank[:, 0 : slots.stop - slots.start]
+
+        def scores(m, slots=slice(0, SLOTS)):
             h, cols = m // 2, slice((m % 2) * P, (m % 2 + 1) * P)
             nc.tensor.matmul_mx(
-                out=product_banks[m][:],
+                out=score_bank(m, slots),
                 lhsT=x_codes[h][:, cols].bitcast(E4M3),
                 lhsT_scale=x_scales[h][:, cols],
-                rhs=wd_codes[:].bitcast(E4M3),
-                rhs_scale=wd_scales[:],
+                rhs=wd_codes[:, slots].bitcast(E4M3),
+                rhs_scale=wd_scales[:, slots],
                 start=True,
                 stop=True,
             )
 
-        def scaled_scores(m):
+        def scaled_scores(m, slots=slice(0, SLOTS)):
+            places = slice(slots.start // PACK, slots.stop // PACK)
             nc.vector.scalar_tensor_tensor(
-                z[m][:],
-                product_banks[m][:].rearrange("r (q s) -> r s q", s=PACK),
+                z[m][:, :, places],
+                score_bank(m, slots).rearrange("r (q s) -> r s q", s=PACK),
                 us_cols[:, m : m + 1],
-                ts_rows[:],
+                ts_rows[:, :, places],
                 ALU.mult,
                 ALU.mult,
             )
@@ -229,7 +235,8 @@ def tile_attend_gpgent_x_kernel(tc, xT, wT, adv, us, ts, wt, be, offs, out):
             )
 
         def adv_term(m):
-            a_term = staged(f"a_term{m}", [P, PACK, P], F32, X_SLOT, m * TERM_BYTES)
+            place = ((X_SLOT, 2 * TERM_BYTES), (X_SLOT, 3 * TERM_BYTES), (ADV_SLOT, 0), (MAX_SLOT, 0))[m]
+            a_term = staged(f"a_term{m}", [P, PACK, P], F32, *place)
             nc.scalar.activation(
                 a_term[:].rearrange("r s q -> r q s"),
                 adv_tiles[m][:].rearrange("r (q s) -> r q s", s=PACK),
@@ -259,19 +266,18 @@ def tile_attend_gpgent_x_kernel(tc, xT, wT, adv, us, ts, wt, be, offs, out):
             )
             add_transposed(m, u_term, False, False)
 
-        def exponential_term(m):
-            e_scale = keep.tile([P, 1], F32, name=f"e_scale{m}")
+        e_scales = [keep.tile([P, 1], F32, name=f"e_scale{m}") for m in range(TILES)]
+        e_terms = [keep.tile([P, PACK, P], F32, name=f"e_term{m}") for m in range(TILES)]
+
+        def exponential_factor(m):
             neg_inverse, a_part = ratios[:, 1, m : m + 1], ratios[:, 2, m : m + 1]
             if m != 1:
-                nc.scalar.activation(e_scale[:], u_sums[m][:], ACT.Identity, bias=a_part, scale=neg_inverse)
+                nc.scalar.activation(e_scales[m][:], u_sums[m][:], ACT.Identity, bias=a_part, scale=neg_inverse)
             else:
-                nc.vector.tensor_scalar(e_scale[:], u_sums[m][:], neg_inverse, a_part, ALU.mult, ALU.add)
-            e_term = keep.tile([P, PACK, P], F32, name=f"e_term{m}")
-            pieces = LAST_PIECES if m == TILES - 1 else 1
-            for j in range(pieces):
-                part = slice(j * PACK // pieces, (j + 1) * PACK // pieces)
-                nc.scalar.activation(e_term[:, part, :], e[m][:, part, :], ACT.Copy, scale=e_scale[:])
-            add_transposed(m, e_term, False, True)
+                nc.vector.tensor_scalar(e_scales[m][:], u_sums[m][:], neg_inverse, a_part, ALU.mult, ALU.add)
+
+        def exponential_term(m, part=slice(0, PACK)):
+            nc.scalar.activation(e_terms[m][:, part, :], e[m][:, part, :], ACT.Copy, scale=e_scales[m][:])
 
         g = [keep.tile([P, P, PACK], BF16, name=f"g{m}", align_bytes=64) for m in range(TILES)]
         g_codes = [keep.tile([P, P], U32, name=f"g_codes{m}", align_bytes=64) for m in range(TILES)]
@@ -303,20 +309,25 @@ def tile_attend_gpgent_x_kernel(tc, xT, wT, adv, us, ts, wt, be, offs, out):
                 stop=True,
             )
             res = keep.tile([P, P, PACK], F32, name=f"res{m}")
-            pieces = LAST_PIECES if m >= TILES - 2 else 1
-            for j in range(pieces):
-                part = slice(j * P // pieces, (j + 1) * P // pieces)
+            cuts = ((0, P), (0, P // 2, P), (0, P // 2, P), (0, P // 2, 3 * P // 4, P))[m]
+            for j in range(len(cuts) - 1):
+                part = slice(cuts[j], cuts[j + 1])
                 copy_out = nc.vector.tensor_copy if m == TILES - 1 else nc.scalar.copy
                 copy_out(res[:, part, :], out_banks[m][:].rearrange("r t p -> r p t")[:, part, :])
                 nc.sync.dma_start(
-                    out=out[m * P : (m + 1) * P, j * D // pieces : (j + 1) * D // pieces],
+                    out=out[m * P : (m + 1) * P, PACK * part.start : PACK * part.stop],
                     in_=res[:, part, :].rearrange("r p t -> r (p t)"),
                 )
 
-        for m in range(TILES):
-            scores(m)
-        a_terms = [adv_term(m) for m in range(TILES)]
-        scaled_scores(0)
+        slot_halves = (slice(0, SLOTS // 2), slice(SLOTS // 2, SLOTS))
+        for slots in slot_halves:
+            scores(0, slots)
+        scores(1)
+        a_terms = [adv_term(m) for m in range(TILES - 1)]
+        for e_half, slots in enumerate(slot_halves):
+            scaled_scores(0, slots)
+            quantize_rows(1, slice(e_half * P, (e_half + 1) * P), late_grouped[e_half])
+            scores(2 + e_half)
         scaled_scores(1)
         for m in range(2):
             add_transposed(m, a_terms[m], True, False)
@@ -345,8 +356,8 @@ def tile_attend_gpgent_x_kernel(tc, xT, wT, adv, us, ts, wt, be, offs, out):
         exponentials(3)
         row_ratios(0, 2)
         quantize_by_i(1, high_by_i)
-        for m in range(2, TILES):
-            add_transposed(m, a_terms[m], True, False)
+        add_transposed(2, a_terms[2], True, False)
+        last_a_term = adv_term(TILES - 1)
         for bank in out_banks[1:3]:
             nc.tensor.matmul_mx(
                 out=bank[:].rearrange("r t p -> r (t p)"),
@@ -357,19 +368,32 @@ def tile_attend_gpgent_x_kernel(tc, xT, wT, adv, us, ts, wt, be, offs, out):
                 start=True,
                 stop=True,
             )
+        quarter_pairs = (slice(0, PACK // 2), slice(PACK // 2, PACK))
         entropy_terms(0)
         inverse(2, 4)
+        exponential_factor(0)
         exponential_term(0)
+        add_transposed(0, e_terms[0], False, True)
         entropy_terms(1)
+        add_transposed(TILES - 1, last_a_term, True, False)
         row_ratios(2, 4)
+        exponential_factor(1)
         exponential_term(1)
+        add_transposed(1, e_terms[1], False, True)
         entropy_terms(2)
-        exponential_term(2)
         entropy_terms(3)
-        exponential_term(3)
+        exponential_factor(2)
+        exponential_term(2, quarter_pairs[0])
+        exponential_factor(3)
+        exponential_term(2, quarter_pairs[1])
+        add_transposed(2, e_terms[2], False, True)
+        for part in quarter_pairs:
+            exponential_term(3, part)
         halves = (slice(0, P // 2), slice(P // 2, P))
         gradient(0, ts_cols)
         for m in range(1, TILES):
+            if m == 2:
+                add_transposed(3, e_terms[3], False, True)
             gradient(m, ts_cols, halves[0])
             quantize_gradient(m - 1)
             rows_gradient(m - 1)

@@ -94,13 +94,18 @@ def tile_attend_gpgent_x_kernel(tc, xT, wT, adv, us, ts, wt, be, offs, out):
 
         def leave_bank(by_i, bank):
             nc.scalar.copy(
-                by_i[:].bitcast(F32).rearrange("q (t p u) -> q t p u", t=2, u=2),
-                bank.rearrange("q (t u) p -> q t p u", t=2),
+                by_i[:].bitcast(F32).rearrange("q (h t p u) -> q t h p u", h=2, t=2, u=2),
+                bank.rearrange("q (t u) (h p) -> q t h p u", t=2, h=2),
             )
 
         def quantize_by_i(half, by_i):
-            cols = slice(half * D // 2, (half + 1) * D // 2)
-            nc.vector.quantize_mx(out=wi_codes[:, cols].bitcast(E4M3), scales=wi_scales[:, cols], in_=by_i[:])
+            for h in range(2):
+                cols = slice((2 * h + half) * P, (2 * h + half + 1) * P)
+                nc.vector.quantize_mx(
+                    out=wi_codes[:, cols].bitcast(E4M3),
+                    scales=wi_scales[:, cols],
+                    in_=by_i[:, h * P * PACK : (h + 1) * P * PACK],
+                )
 
         low_planes = staged("low_planes", [P, 2 * SLOTS], BF16, LOW_SLOT)
         for t in range(2):
@@ -298,26 +303,42 @@ def tile_attend_gpgent_x_kernel(tc, xT, wT, adv, us, ts, wt, be, offs, out):
                 in_=g[m][:, rows, :].rearrange("q r s -> q (r s)"),
             )
 
-        def rows_gradient(m):
+        def gradient_product(m, bank, features):
             nc.tensor.matmul_mx(
-                out=out_banks[m][:].rearrange("r t p -> r (t p)"),
+                out=bank,
                 lhsT=g_codes[m][:].bitcast(E5M2),
                 lhsT_scale=g_scales[m][:],
-                rhs=wi_codes[:].bitcast(E4M3),
-                rhs_scale=wi_scales[:],
+                rhs=wi_codes[:, features].bitcast(E4M3),
+                rhs_scale=wi_scales[:, features],
                 start=True,
                 stop=True,
             )
-            res = keep.tile([P, P, PACK], F32, name=f"res{m}")
-            cuts = ((0, P), (0, P // 2, P), (0, P // 2, P), (0, P // 2, 3 * P // 4, P))[m]
-            for j in range(len(cuts) - 1):
-                part = slice(cuts[j], cuts[j + 1])
-                copy_out = nc.vector.tensor_copy if m == TILES - 1 else nc.scalar.copy
-                copy_out(res[:, part, :], out_banks[m][:].rearrange("r t p -> r p t")[:, part, :])
-                nc.sync.dma_start(
-                    out=out[m * P : (m + 1) * P, PACK * part.start : PACK * part.stop],
-                    in_=res[:, part, :].rearrange("r p t -> r (p t)"),
-                )
+
+        def store_half(m, h, bank, copy_out, queue):
+            res = keep.tile([P, P // 2, PACK], F32, name=f"res{m}_{h}")
+            copy_out(res[:], bank.rearrange("r (t p) -> r p t", t=PACK))
+            queue.dma_start(
+                out=out[m * P : (m + 1) * P, h * D // 2 : (h + 1) * D // 2], in_=res[:].rearrange("r p t -> r (p t)")
+            )
+
+        def rows_gradient(m):
+            bank = out_banks[m][:].rearrange("r t p -> r (t p)")
+            halves_of_d = (slice(0, D // 2), slice(D // 2, D))
+            if m == TILES - 1:
+                banks = (bank[:, halves_of_d[0]], product_banks[0][:, halves_of_d[0]])
+                for h in range(2):
+                    gradient_product(m, banks[h], halves_of_d[h])
+                store_half(m, 0, banks[0], nc.scalar.copy, nc.scalar)
+                store_half(m, 1, banks[1], nc.vector.tensor_copy, nc.sync)
+            elif m == 0:
+                gradient_product(m, bank, slice(0, D))
+                res = keep.tile([P, 2, P // 2, PACK], F32, name=f"res{m}")
+                nc.scalar.copy(res[:], bank.rearrange("r (h t p) -> r h p t", h=2, t=PACK))
+                nc.sync.dma_start(out=out[0:P, :], in_=res[:].rearrange("r h p t -> r (h p t)"))
+            else:
+                gradient_product(m, bank, slice(0, D))
+                for h in range(2):
+                    store_half(m, h, bank[:, halves_of_d[h]], nc.scalar.copy, nc.sync)
 
         slot_halves = (slice(0, SLOTS // 2), slice(SLOTS // 2, SLOTS))
         for slots in slot_halves:

@@ -81,6 +81,7 @@ def tile_attend_gpgent_x_kernel(tc, xT, wT, adv, us, ts, wt, be, offs, out):
         us_cols = vec_cols[:, 0, :]
         product_banks = [psum.tile([P, SLOTS], F32, name=f"product{m}") for m in range(TILES)]
         grad_banks = [bank[:].rearrange("q (s r) -> q s r", s=PACK) for bank in product_banks]
+        grad_banks = grad_banks[0:2] + [out_banks[3][:]] + grad_banks[3:]
 
         def transpose_pairs(bank, planes):
             words = planes.bitcast(F32)
@@ -325,7 +326,7 @@ def tile_attend_gpgent_x_kernel(tc, xT, wT, adv, us, ts, wt, be, offs, out):
             bank = out_banks[m][:].rearrange("r t p -> r (t p)")
             halves_of_d = (slice(0, D // 2), slice(D // 2, D))
             if m == TILES - 1:
-                banks = (bank[:, halves_of_d[0]], product_banks[0][:, halves_of_d[0]])
+                banks = (product_banks[2][:, halves_of_d[0]], product_banks[0][:, halves_of_d[0]])
                 for h in range(2):
                     gradient_product(m, banks[h], halves_of_d[h])
                 store_half(m, 0, banks[0], nc.scalar.copy, nc.scalar)
@@ -379,13 +380,13 @@ def tile_attend_gpgent_x_kernel(tc, xT, wT, adv, us, ts, wt, be, offs, out):
         quantize_by_i(1, high_by_i)
         add_transposed(2, a_terms[2], True, False)
         last_a_term = adv_term(TILES - 1)
-        for bank in out_banks[1:3]:
+        for bank, features in ((out_banks[1], slice(0, D)), (out_banks[2], slice(D - P, D))):
             nc.tensor.matmul_mx(
-                out=bank[:].rearrange("r t p -> r (t p)"),
+                out=bank[:].rearrange("r t p -> r (t p)")[:, features],
                 lhsT=x_codes[0][:, 0:P].bitcast(E4M3),
                 lhsT_scale=x_scales[0][:, 0:P],
-                rhs=wi_codes[:].bitcast(E4M3),
-                rhs_scale=wi_scales[:],
+                rhs=wi_codes[:, features].bitcast(E4M3),
+                rhs_scale=wi_scales[:, features],
                 start=True,
                 stop=True,
             )

@@ -81,7 +81,7 @@ def tile_attend_gpgent_x_kernel(tc, xT, wT, adv, us, ts, wt, be, offs, out):
         us_cols = vec_cols[:, 0, :]
         product_banks = [psum.tile([P, SLOTS], F32, name=f"product{m}") for m in range(TILES)]
         grad_banks = [bank[:].rearrange("q (s r) -> q s r", s=PACK) for bank in product_banks]
-        grad_banks = grad_banks[0:2] + [out_banks[3][:]] + grad_banks[3:]
+        grad_banks = grad_banks[0:3] + [out_banks[3][:]]
 
         def transpose_pairs(bank, planes):
             words = planes.bitcast(F32)
@@ -241,7 +241,7 @@ def tile_attend_gpgent_x_kernel(tc, xT, wT, adv, us, ts, wt, be, offs, out):
             )
 
         def adv_term(m):
-            place = ((X_SLOT, 2 * TERM_BYTES), (X_SLOT, 3 * TERM_BYTES), (ADV_SLOT, 0), (MAX_SLOT, 0))[m]
+            place = ((X_SLOT, 2 * TERM_BYTES), (X_SLOT, 3 * TERM_BYTES), (ADV_SLOT, 0), (LOW_SLOT, GROUP_BYTES))[m]
             a_term = staged(f"a_term{m}", [P, PACK, P], F32, *place)
             nc.scalar.activation(
                 a_term[:].rearrange("r s q -> r q s"),
@@ -326,7 +326,7 @@ def tile_attend_gpgent_x_kernel(tc, xT, wT, adv, us, ts, wt, be, offs, out):
             bank = out_banks[m][:].rearrange("r t p -> r (t p)")
             halves_of_d = (slice(0, D // 2), slice(D // 2, D))
             if m == TILES - 1:
-                banks = (product_banks[2][:, halves_of_d[0]], product_banks[0][:, halves_of_d[0]])
+                banks = (product_banks[3][:, halves_of_d[0]], product_banks[0][:, halves_of_d[0]])
                 for h in range(2):
                     gradient_product(m, banks[h], halves_of_d[h])
                 store_half(m, 0, banks[0], nc.scalar.copy, nc.scalar)
@@ -373,13 +373,13 @@ def tile_attend_gpgent_x_kernel(tc, xT, wT, adv, us, ts, wt, be, offs, out):
             nc.tensor.transpose(high_bank[:, j, :], high_words[:, j * P : (j + 1) * P], ident[:])
         high_by_i = staged("high_by_i", [P, 2 * P * PACK], BF16, MAX_SLOT)
         leave_bank(high_by_i, high_bank)
+        add_transposed(2, a_terms[2], True, False)
+        add_transposed(TILES - 1, adv_term(TILES - 1), True, False)
         exponentials(2)
         inverse(0, 2)
         exponentials(3)
         row_ratios(0, 2)
         quantize_by_i(1, high_by_i)
-        add_transposed(2, a_terms[2], True, False)
-        last_a_term = adv_term(TILES - 1)
         for bank, features in ((out_banks[1], slice(0, D)), (out_banks[2], slice(D - P, D))):
             nc.tensor.matmul_mx(
                 out=bank[:].rearrange("r t p -> r (t p)")[:, features],
@@ -392,14 +392,13 @@ def tile_attend_gpgent_x_kernel(tc, xT, wT, adv, us, ts, wt, be, offs, out):
             )
         quarter_pairs = (slice(0, PACK // 2), slice(PACK // 2, PACK))
         entropy_terms(0)
-        inverse(2, 4)
         exponential_factor(0)
         exponential_term(0)
         add_transposed(0, e_terms[0], False, True)
         entropy_terms(1)
-        add_transposed(TILES - 1, last_a_term, True, False)
-        row_ratios(2, 4)
+        inverse(2, 4)
         exponential_factor(1)
+        row_ratios(2, 4)
         exponential_term(1)
         add_transposed(1, e_terms[1], False, True)
         entropy_terms(2)

@@ -277,7 +277,7 @@ def tile_attend_gpgent_x_kernel(tc, xT, wT, adv, us, ts, wt, be, offs, out):
 
         def exponential_factor(m):
             neg_inverse, a_part = ratios[:, 1, m : m + 1], ratios[:, 2, m : m + 1]
-            if m != 1:
+            if m != 0:
                 nc.scalar.activation(e_scales[m][:], u_sums[m][:], ACT.Identity, bias=a_part, scale=neg_inverse)
             else:
                 nc.vector.tensor_scalar(e_scales[m][:], u_sums[m][:], neg_inverse, a_part, ALU.mult, ALU.add)
@@ -367,6 +367,8 @@ def tile_attend_gpgent_x_kernel(tc, xT, wT, adv, us, ts, wt, be, offs, out):
                 ALU.mult,
                 ALU.add,
             )
+        products = keep.tile([P, PACK, P], F32, name="products")
+        nc.gpsimd.tensor_tensor(products[:], z[1][:], e[1][:], ALU.mult)
         high_bank = out_banks[3][:]
         high_words = high_pairs[:].rearrange("p t u q e -> p (t u q e)").bitcast(F32)
         for j in range(PACK):
@@ -392,17 +394,19 @@ def tile_attend_gpgent_x_kernel(tc, xT, wT, adv, us, ts, wt, be, offs, out):
             )
         quarter_pairs = (slice(0, PACK // 2), slice(PACK // 2, PACK))
         entropy_terms(0)
-        exponential_factor(0)
-        exponential_term(0)
-        add_transposed(0, e_terms[0], False, True)
-        entropy_terms(1)
+        second_term = keep.tile([P, PACK, P], F32, name="second_term")
+        nc.scalar.activation(second_term[:], products[:], ACT.Copy, scale=ratios[:, 0, 1:2], accum_out=u_sums[1][:])
+        add_transposed(1, second_term, False, False)
         inverse(2, 4)
-        exponential_factor(1)
+        exponential_factor(0)
         row_ratios(2, 4)
-        exponential_term(1)
-        add_transposed(1, e_terms[1], False, True)
+        nc.vector.tensor_scalar(e_terms[0][:], e[0][:], e_scales[0][:], None, ALU.mult)
+        add_transposed(0, e_terms[0], False, True)
         entropy_terms(2)
+        exponential_factor(1)
+        exponential_term(1)
         entropy_terms(3)
+        add_transposed(1, e_terms[1], False, True)
         exponential_factor(2)
         exponential_term(2, quarter_pairs[0])
         exponential_factor(3)

@@ -81,7 +81,7 @@ def tile_attend_gpgent_x_kernel(tc, xT, wT, adv, us, ts, wt, be, offs, out):
         us_cols = vec_cols[:, 0, :]
         product_banks = [psum.tile([P, SLOTS], F32, name=f"product{m}") for m in range(TILES)]
         grad_banks = [bank[:].rearrange("q (s r) -> q s r", s=PACK) for bank in product_banks]
-        grad_banks = grad_banks[0:3] + [out_banks[3][:]]
+        grad_banks = [grad_banks[0], grad_banks[2], grad_banks[3], out_banks[3][:]]
 
         def transpose_pairs(bank, planes):
             words = planes.bitcast(F32)
@@ -326,7 +326,7 @@ def tile_attend_gpgent_x_kernel(tc, xT, wT, adv, us, ts, wt, be, offs, out):
             bank = out_banks[m][:].rearrange("r t p -> r (t p)")
             halves_of_d = (slice(0, D // 2), slice(D // 2, D))
             if m == TILES - 1:
-                banks = (product_banks[3][:, halves_of_d[0]], product_banks[0][:, halves_of_d[0]])
+                banks = (product_banks[1][:, halves_of_d[0]], product_banks[0][:, halves_of_d[0]])
                 for h in range(2):
                     gradient_product(m, banks[h], halves_of_d[h])
                 store_half(m, 0, banks[0], nc.scalar.copy, nc.scalar)
@@ -351,8 +351,7 @@ def tile_attend_gpgent_x_kernel(tc, xT, wT, adv, us, ts, wt, be, offs, out):
             quantize_rows(1, slice(e_half * P, (e_half + 1) * P), late_grouped[e_half])
             scores(2 + e_half)
         scaled_scores(1)
-        for m in range(2):
-            add_transposed(m, a_terms[m], True, False)
+        add_transposed(0, a_terms[0], True, False)
         exponentials(0)
         exponentials(1)
         scaled_scores(2)
@@ -375,6 +374,7 @@ def tile_attend_gpgent_x_kernel(tc, xT, wT, adv, us, ts, wt, be, offs, out):
             nc.tensor.transpose(high_bank[:, j, :], high_words[:, j * P : (j + 1) * P], ident[:])
         high_by_i = staged("high_by_i", [P, 2 * P * PACK], BF16, MAX_SLOT)
         leave_bank(high_by_i, high_bank)
+        add_transposed(1, a_terms[1], True, False)
         add_transposed(2, a_terms[2], True, False)
         add_transposed(TILES - 1, adv_term(TILES - 1), True, False)
         exponentials(2)

@@ -81,7 +81,7 @@ def tile_attend_gpgent_x_kernel(tc, xT, wT, adv, us, ts, wt, be, offs, out):
         us_cols = vec_cols[:, 0, :]
         product_banks = [psum.tile([P, SLOTS], F32, name=f"product{m}") for m in range(TILES)]
         grad_banks = [bank[:].rearrange("q (s r) -> q s r", s=PACK) for bank in product_banks]
-        grad_banks = [grad_banks[0], grad_banks[2], grad_banks[3], out_banks[3][:]]
+        grad_banks = [grad_banks[0], grad_banks[3], out_banks[3][:], grad_banks[1]]
 
         def transpose_pairs(bank, planes):
             words = planes.bitcast(F32)
@@ -326,7 +326,7 @@ def tile_attend_gpgent_x_kernel(tc, xT, wT, adv, us, ts, wt, be, offs, out):
             bank = out_banks[m][:].rearrange("r t p -> r (t p)")
             halves_of_d = (slice(0, D // 2), slice(D // 2, D))
             if m == TILES - 1:
-                banks = (product_banks[1][:, halves_of_d[0]], product_banks[0][:, halves_of_d[0]])
+                banks = (product_banks[2][:, halves_of_d[0]], product_banks[0][:, halves_of_d[0]])
                 for h in range(2):
                     gradient_product(m, banks[h], halves_of_d[h])
                 store_half(m, 0, banks[0], nc.scalar.copy, nc.scalar)
@@ -385,10 +385,10 @@ def tile_attend_gpgent_x_kernel(tc, xT, wT, adv, us, ts, wt, be, offs, out):
         for bank, features in ((out_banks[1], slice(0, D)), (out_banks[2], slice(D - P, D))):
             nc.tensor.matmul_mx(
                 out=bank[:].rearrange("r t p -> r (t p)")[:, features],
-                lhsT=x_codes[0][:, 0:P].bitcast(E4M3),
-                lhsT_scale=x_scales[0][:, 0:P],
-                rhs=wi_codes[:, features].bitcast(E4M3),
-                rhs_scale=wi_scales[:, features],
+                lhsT=wi_codes[:, P : 2 * P].bitcast(E4M3),
+                lhsT_scale=wi_scales[:, P : 2 * P],
+                rhs=wd_codes[:, features].bitcast(E4M3),
+                rhs_scale=wd_scales[:, features],
                 start=True,
                 stop=True,
             )

@@ -99,8 +99,8 @@ def tile_attend_gpgent_x_kernel(tc, xT, wT, adv, us, ts, wt, be, offs, out):
                 bank.rearrange("q (t u) (h p) -> q t h p u", t=2, h=2),
             )
 
-        def quantize_by_i(half, by_i):
-            for h in range(2):
+        def quantize_by_i(half, by_i, feature_halves=(0, 1)):
+            for h in feature_halves:
                 cols = slice((2 * h + half) * P, (2 * h + half + 1) * P)
                 nc.vector.quantize_mx(
                     out=wi_codes[:, cols].bitcast(E4M3),
@@ -196,8 +196,8 @@ def tile_attend_gpgent_x_kernel(tc, xT, wT, adv, us, ts, wt, be, offs, out):
         ratios = keep.tile([P, 3, TILES], F32, name="ratios")
         u_sums = [keep.tile([P, 1], F32, name=f"u_sum{m}") for m in range(TILES)]
 
-        def add_transposed(m, term, first, last):
-            for s in range(PACK):
+        def add_transposed(m, term, first, last, quarters=slice(0, PACK)):
+            for s in range(quarters.start, quarters.stop):
                 nc.tensor.matmul(
                     grad_banks[m][:, s, :],
                     lhsT=term[:, s, :],
@@ -377,11 +377,11 @@ def tile_attend_gpgent_x_kernel(tc, xT, wT, adv, us, ts, wt, be, offs, out):
         add_transposed(1, a_terms[1], True, False)
         add_transposed(2, a_terms[2], True, False)
         add_transposed(TILES - 1, adv_term(TILES - 1), True, False)
-        exponentials(2)
         inverse(0, 2)
-        exponentials(3)
+        exponentials(2)
         row_ratios(0, 2)
-        quantize_by_i(1, high_by_i)
+        exponentials(3)
+        quantize_by_i(1, high_by_i, (0,))
         for bank, features in ((out_banks[1], slice(0, D)), (out_banks[2], slice(D - P, D))):
             nc.tensor.matmul_mx(
                 out=bank[:].rearrange("r t p -> r (t p)")[:, features],
@@ -394,9 +394,10 @@ def tile_attend_gpgent_x_kernel(tc, xT, wT, adv, us, ts, wt, be, offs, out):
             )
         quarter_pairs = (slice(0, PACK // 2), slice(PACK // 2, PACK))
         entropy_terms(0)
-        second_term = keep.tile([P, PACK, P], F32, name="second_term")
+        second_term = staged("second_term", [P, PACK, P], F32, MAX_SLOT, 2 * TERM_BYTES)
         nc.scalar.activation(second_term[:], products[:], ACT.Copy, scale=ratios[:, 0, 1:2], accum_out=u_sums[1][:])
         add_transposed(1, second_term, False, False)
+        quantize_by_i(1, high_by_i, (1,))
         inverse(2, 4)
         exponential_factor(0)
         row_ratios(2, 4)
@@ -416,9 +417,10 @@ def tile_attend_gpgent_x_kernel(tc, xT, wT, adv, us, ts, wt, be, offs, out):
             exponential_term(3, part)
         halves = (slice(0, P // 2), slice(P // 2, P))
         gradient(0, ts_cols)
+        add_transposed(3, e_terms[3], False, True, quarter_pairs[0])
         for m in range(1, TILES):
             if m == 2:
-                add_transposed(3, e_terms[3], False, True)
+                add_transposed(3, e_terms[3], False, True, quarter_pairs[1])
             gradient(m, ts_cols, halves[0])
             quantize_gradient(m - 1)
             rows_gradient(m - 1)

@@ -99,8 +99,8 @@ def tile_attend_gpgent_x_kernel(tc, xT, wT, adv, us, ts, wt, be, offs, out):
                 bank.rearrange("q (t u) (h p) -> q t h p u", t=2, h=2),
             )
 
-        def quantize_by_i(half, by_i, feature_halves=(0, 1)):
-            for h in feature_halves:
+        def quantize_by_i(half, by_i):
+            for h in range(2):
                 cols = slice((2 * h + half) * P, (2 * h + half + 1) * P)
                 nc.vector.quantize_mx(
                     out=wi_codes[:, cols].bitcast(E4M3),
@@ -368,12 +368,28 @@ def tile_attend_gpgent_x_kernel(tc, xT, wT, adv, us, ts, wt, be, offs, out):
             )
         products = keep.tile([P, PACK, P], F32, name="products")
         nc.gpsimd.tensor_tensor(products[:], z[1][:], e[1][:], ALU.mult)
-        high_bank = out_banks[3][:]
         high_words = high_pairs[:].rearrange("p t u q e -> p (t u q e)").bitcast(F32)
         for j in range(PACK):
-            nc.tensor.transpose(high_bank[:, j, :], high_words[:, j * P : (j + 1) * P], ident[:])
-        high_by_i = staged("high_by_i", [P, 2 * P * PACK], BF16, MAX_SLOT)
-        leave_bank(high_by_i, high_bank)
+            nc.tensor.transpose(out_banks[3 - j // 2][:, j % 2, :], high_words[:, j * P : (j + 1) * P], ident[:])
+
+        def leave_plane(t, start):
+            by_i = staged(f"by_i{t}", [P, P * PACK], BF16, MAX_SLOT, start)
+            nc.scalar.copy(
+                by_i[:].bitcast(F32).rearrange("q (h p u) -> q h p u", h=2, u=2),
+                out_banks[5 - t][:, 0:2, :].rearrange("q u (h p) -> q h p u", h=2),
+            )
+            return by_i
+
+        def quantize_plane(t, by_i):
+            for h in range(2):
+                cols = slice(h * D // 2 + t * P // 2, h * D // 2 + (t + 1) * P // 2)
+                nc.vector.quantize_mx(
+                    out=wi_codes[:, cols].bitcast(E4M3),
+                    scales=wi_scales[:, cols],
+                    in_=by_i[:, h * D // 2 : (h + 1) * D // 2],
+                )
+
+        by_i2 = leave_plane(2, 0)
         add_transposed(1, a_terms[1], True, False)
         add_transposed(2, a_terms[2], True, False)
         add_transposed(TILES - 1, adv_term(TILES - 1), True, False)
@@ -381,12 +397,12 @@ def tile_attend_gpgent_x_kernel(tc, xT, wT, adv, us, ts, wt, be, offs, out):
         exponentials(2)
         row_ratios(0, 2)
         exponentials(3)
-        quantize_by_i(1, high_by_i, (0,))
-        for bank, features in ((out_banks[1], slice(0, D)), (out_banks[2], slice(D - P, D))):
+        quantize_plane(2, by_i2)
+        for bank, features in ((out_banks[1], slice(0, D)), (out_banks[0], slice(D - P, D))):
             nc.tensor.matmul_mx(
                 out=bank[:].rearrange("r t p -> r (t p)")[:, features],
-                lhsT=wi_codes[:, P : 2 * P].bitcast(E4M3),
-                lhsT_scale=wi_scales[:, P : 2 * P],
+                lhsT=wi_codes[:, P // 2 : 3 * P // 2].bitcast(E4M3),
+                lhsT_scale=wi_scales[:, P // 2 : 3 * P // 2],
                 rhs=wd_codes[:, features].bitcast(E4M3),
                 rhs_scale=wd_scales[:, features],
                 start=True,
@@ -397,7 +413,6 @@ def tile_attend_gpgent_x_kernel(tc, xT, wT, adv, us, ts, wt, be, offs, out):
         second_term = staged("second_term", [P, PACK, P], F32, MAX_SLOT, 2 * TERM_BYTES)
         nc.scalar.activation(second_term[:], products[:], ACT.Copy, scale=ratios[:, 0, 1:2], accum_out=u_sums[1][:])
         add_transposed(1, second_term, False, False)
-        quantize_by_i(1, high_by_i, (1,))
         inverse(2, 4)
         exponential_factor(0)
         row_ratios(2, 4)
@@ -405,8 +420,10 @@ def tile_attend_gpgent_x_kernel(tc, xT, wT, adv, us, ts, wt, be, offs, out):
         add_transposed(0, e_terms[0], False, True)
         entropy_terms(2)
         exponential_factor(1)
+        by_i3 = leave_plane(3, 3 * TERM_BYTES)
         exponential_term(1)
         entropy_terms(3)
+        quantize_plane(3, by_i3)
         add_transposed(1, e_terms[1], False, True)
         exponential_factor(2)
         exponential_term(2, quarter_pairs[0])

@@ -380,8 +380,8 @@ def tile_attend_gpgent_x_kernel(tc, xT, wT, adv, us, ts, wt, be, offs, out):
             )
             return by_i
 
-        def quantize_plane(t, by_i):
-            for h in range(2):
+        def quantize_plane(t, by_i, feature_halves=(0, 1)):
+            for h in feature_halves:
                 cols = slice(h * D // 2 + t * P // 2, h * D // 2 + (t + 1) * P // 2)
                 nc.vector.quantize_mx(
                     out=wi_codes[:, cols].bitcast(E4M3),
@@ -397,7 +397,7 @@ def tile_attend_gpgent_x_kernel(tc, xT, wT, adv, us, ts, wt, be, offs, out):
         exponentials(2)
         row_ratios(0, 2)
         exponentials(3)
-        quantize_plane(2, by_i2)
+        quantize_plane(2, by_i2, (0,))
         for bank, features in ((out_banks[1], slice(0, D)), (out_banks[0], slice(D - P, D))):
             nc.tensor.matmul_mx(
                 out=bank[:].rearrange("r t p -> r (t p)")[:, features],
@@ -413,6 +413,7 @@ def tile_attend_gpgent_x_kernel(tc, xT, wT, adv, us, ts, wt, be, offs, out):
         second_term = staged("second_term", [P, PACK, P], F32, MAX_SLOT, 2 * TERM_BYTES)
         nc.scalar.activation(second_term[:], products[:], ACT.Copy, scale=ratios[:, 0, 1:2], accum_out=u_sums[1][:])
         add_transposed(1, second_term, False, False)
+        quantize_plane(2, by_i2, (1,))
         inverse(2, 4)
         exponential_factor(0)
         row_ratios(2, 4)

from contextlib import ExitStack

import concourse.mybir as mybir
from concourse.masks import make_identity

R, D, SLOTS, T = 512, 512, 512, 2048
FLOPS = 2 * 2 * R * D * SLOTS
BYTES = 4 * (D * R + D * T + R * SLOTS + T + 3 * R + R * D) + 2 * 128 * SLOTS // 16

F32 = mybir.dt.float32
BF16 = mybir.dt.bfloat16
U32 = mybir.dt.uint32
U16 = mybir.dt.uint16
U8 = mybir.dt.uint8
E4M3 = mybir.dt.float8_e4m3fn_x4
E5M2 = mybir.dt.float8_e5m2_x4
ALU = mybir.AluOpType
ACT = mybir.ActivationFunctionType
AX = mybir.AxisListType

P = 128
PACK = 4
TILES = R // P
FOLD = T // P
LINE = 4
SLOT_BYTES = 4 * T
WINDOW_SLOT = PACK
X_SLOT = 0
ADV_SLOT = 1
LOW_SLOT = PACK + 1
MAX_SLOT = PACK + 2
TERM_BYTES = 4 * SLOTS
GROUP_BYTES = 2 * P * PACK
LAST_PIECES = 2


def tile_attend_gpgent_x_kernel(tc, xT, wT, adv, us, ts, wt, be, offs, out):
    nc = tc.nc
    with ExitStack() as ctx:
        keep = ctx.enter_context(tc.tile_pool(name="keep", bufs=1))
        stage = ctx.enter_context(tc.tile_pool(name="stage", bufs=1))
        psum = ctx.enter_context(tc.psum_pool(name="psum", bufs=1))
        out_banks = [psum.tile([P, PACK, P], F32, name=f"out{m}") for m in range(TILES)]

        def staged(name, shape, dtype, slot, start=0):
            return stage.tile(shape, dtype, name=name, align_bytes=64, offset=slot * SLOT_BYTES + start)

        offsets = keep.tile([P, SLOTS // 16], U16, name="offsets")
        ts_folded = keep.tile([P, FOLD], F32, name="ts_folded")
        nc.scalar.dma_start(out=ts_folded[:], in_=ts[0:1, :].rearrange("o (p j) -> (o p) j", p=P))
        w_view = wT.rearrange("(p t) c -> p t c", t=PACK)
        x_view = xT.rearrange("(p t) r -> p t r", t=PACK)
        w_planes = [staged(f"w_plane{t}", [P, T], F32, t) for t in range(PACK)]
        nc.sync.dma_start(out=w_planes[0][:], in_=w_view[:, 0, :])
        nc.sync.dma_start(offsets[:], offs)
        row_vecs = keep.tile([P, P], F32, name="row_vecs")
        nc.gpsimd.memset(row_vecs[:], 0.0)
        for j, vec in enumerate((us, wt, be)):
            nc.scalar.dma_start(
                out=row_vecs[j * TILES : (j + 1) * TILES, :], in_=vec.rearrange("(m p) o -> m (p o)", p=P)
            )
        for t in range(1, PACK):
            nc.sync.dma_start(out=w_planes[t][:], in_=w_view[:, t, :])
        ident = keep.tile([P, P], F32, name="ident")
        make_identity(nc, ident[:])

        ts_window = staged("ts_window", [P, T], F32, WINDOW_SLOT)
        window_view = ts_window[:].rearrange("m (p j) -> m p j", p=P)
        for a in range(FOLD // PACK):
            spread = psum.tile([P, PACK, P], F32, name=f"product{a}")
            for j in range(PACK):
                col = a * PACK + j
                nc.tensor.transpose(spread[:, j, :], ts_folded[:, col : col + 1].to_broadcast([P, P]), ident[:])
            nc.scalar.activation(
                window_view[:, :, a * PACK : (a + 1) * PACK], spread[:].rearrange("m j p -> m p j"), ACT.Copy
            )
        vec_bank = psum.tile([P, P], F32, name=f"product{TILES - 1}")
        nc.tensor.transpose(vec_bank[:], row_vecs[:], ident[:])
        vec_cols = keep.tile([P, 3, TILES], F32, name="vec_cols")
        nc.scalar.copy(vec_cols[:].rearrange("p j m -> p (j m)"), vec_bank[:, 0 : 3 * TILES])
        us_cols = vec_cols[:, 0, :]
        product_banks = [psum.tile([P, SLOTS], F32, name=f"product{m}") for m in range(TILES)]
        grad_banks = [bank[:].rearrange("q (s r) -> q s r", s=PACK) for bank in product_banks]
        grad_banks = [grad_banks[0], grad_banks[3], out_banks[3][:], grad_banks[1]]

        def transpose_pairs(bank, planes):
            words = planes.bitcast(F32)
            for t in range(2):
                for u in range(2):
                    first = t * SLOTS // 2 + u
                    nc.tensor.transpose(bank[:, 2 * t + u, :], words[:, first : (t + 1) * SLOTS // 2 : 2], ident[:])

        wi_codes = keep.tile([P, D], U32, name="wi_codes", align_bytes=64)
        wi_scales = keep.tile([P, D], U8, name="wi_scales", align_bytes=64)

        def leave_bank(by_i, bank):
            nc.scalar.copy(
                by_i[:].bitcast(F32).rearrange("q (h t p u) -> q t h p u", h=2, t=2, u=2),
                bank.rearrange("q (t u) (h p) -> q t h p u", t=2, h=2),
            )

        def quantize_by_i(half, by_i):
            for h in range(2):
                cols = slice((2 * h + half) * P, (2 * h + half + 1) * P)
                nc.vector.quantize_mx(
                    out=wi_codes[:, cols].bitcast(E4M3),
                    scales=wi_scales[:, cols],
                    in_=by_i[:, h * P * PACK : (h + 1) * P * PACK],
                )

        low_planes = staged("low_planes", [P, 2 * SLOTS], BF16, LOW_SLOT)
        for t in range(2):
            nc.vector.tensor_copy(low_planes[:, t * SLOTS : (t + 1) * SLOTS], w_planes[t][:].indirect(offsets[:]))
        x_halves = []
        for h in range(2):
            x_halves.append(staged(f"x_half{h}", [P, PACK, R // 2], F32, X_SLOT, h * SLOT_BYTES // 2))
            nc.sync.dma_start(out=x_halves[h][:], in_=x_view[:, :, h * R // 2 : (h + 1) * R // 2])
        adv_tiles = []
        for m in range(TILES):
            adv_tiles.append(staged(f"adv{m}", [P, SLOTS], F32, ADV_SLOT, m * TERM_BYTES))
            nc.sync.dma_start(out=adv_tiles[m][:], in_=adv[m * P : (m + 1) * P, :])
        ts_listed = keep.tile([P, SLOTS], F32, name="ts_listed")
        nc.vector.tensor_copy(ts_listed[:], ts_window[:].indirect(offsets[:]))
        transpose_pairs(out_banks[0], low_planes[:])
        low_by_i = keep.tile([P, 2 * P * PACK], BF16, name="low_by_i", align_bytes=64)
        leave_bank(low_by_i, out_banks[0][:])
        gathered = staged("gathered", [P, PACK * SLOTS], BF16, WINDOW_SLOT)
        w_by_d = gathered[:].rearrange("p (i t) -> p i t", t=PACK)
        ts_rows = keep.tile([P, PACK, P], F32, name="ts_rows")
        nc.scalar.copy(ts_rows[:].rearrange("m s q -> m q s"), ts_listed[:].rearrange("m (q s) -> m q s", s=PACK))
        nc.scalar.copy(w_by_d[:, :, 0:2], low_planes[:].rearrange("p (t i) -> p i t", t=2))
        for s in range(PACK):
            nc.tensor.transpose(out_banks[2][:, s, :], ts_rows[:, s, :], ident[:])
        ts_cols = keep.tile([P, PACK], F32, name="ts_cols")
        nc.scalar.copy(ts_cols[:], out_banks[2][:, :, 0])

        nc.vector.tensor_copy(w_by_d[:, :, 2], w_planes[2][:].indirect(offsets[:]))
        factors = keep.tile([P, 4, TILES], F32, name="factors")
        nc.vector.scalar_tensor_tensor(
            factors[:, 0:2, :],
            vec_cols[:, 1:3, :],
            -1.0,
            us_cols.unsqueeze(1).to_broadcast([P, 2, TILES]),
            ALU.mult,
            ALU.mult,
        )
        nc.vector.memset(factors[:, 2, :], 1.0)
        quantize_by_i(0, low_by_i)
        for h in range(2):
            nc.vector.tensor_copy(
                w_by_d[:, h * SLOTS // 2 : (h + 1) * SLOTS // 2, 3],
                w_planes[3][:].indirect(offsets[:, h * SLOTS // 32 : (h + 1) * SLOTS // 32]),
            )

        x_codes = [staged(f"x_codes{h}", [P, 2 * P], U32, 3, h * 2 * TERM_BYTES) for h in range(2)]
        x_scales = [keep.tile([P, 2 * P], U8, name=f"x_scales{h}", align_bytes=64) for h in range(2)]
        wd_codes = keep.tile([P, SLOTS], U32, name="wd_codes", align_bytes=64)
        wd_scales = keep.tile([P, SLOTS], U8, name="wd_scales", align_bytes=64)

        def group_rows(engine_copy, grouped, src):
            engine_copy(
                grouped.rearrange("p (c i t) -> p c t i", i=LINE, t=PACK), src.rearrange("p t (c i) -> p c t i", i=LINE)
            )

        def quantize_rows(h, cols, grouped):
            nc.vector.quantize_mx(out=x_codes[h][:, cols].bitcast(E4M3), scales=x_scales[h][:, cols], in_=grouped)

        first_grouped = [
            staged(f"x_grouped{e}", [P, P * PACK], BF16, LOW_SLOT, (1 - e) * GROUP_BYTES) for e in range(2)
        ]
        for e in range(2):
            group_rows(nc.scalar.copy, first_grouped[e][:], x_halves[0][:, :, e * P : (e + 1) * P])

        def quantize_by_d(h):
            cols = slice(h * SLOTS // 2, (h + 1) * SLOTS // 2)
            nc.vector.quantize_mx(
                out=wd_codes[:, cols].bitcast(E4M3),
                scales=wd_scales[:, cols],
                in_=gathered[:, PACK * cols.start : PACK * cols.stop],
            )

        quantize_by_d(0)
        quantize_rows(0, slice(0, P), first_grouped[0][:])
        quantize_by_d(1)
        second_grouped = staged("x_grouped23", [P, 2 * P * PACK], BF16, LOW_SLOT, GROUP_BYTES)
        late_grouped = [second_grouped[:, e * P * PACK : (e + 1) * P * PACK] for e in range(2)]
        group_rows(nc.vector.tensor_copy, late_grouped[0], x_halves[1][:, :, 0:P])
        quantize_rows(0, slice(P, 2 * P), first_grouped[1][:])
        group_rows(nc.scalar.copy, late_grouped[1], x_halves[1][:, :, P : 2 * P])

        z = [keep.tile([P, PACK, P], F32, name=f"z{m}") for m in range(TILES)]
        e = [keep.tile([P, PACK, P], F32, name=f"e{m}") for m in range(TILES)]
        neg_max = [staged(f"neg_max{m}", [P, 1], F32, MAX_SLOT, m * TERM_BYTES) for m in range(TILES)]
        totals = keep.tile([P, TILES], F32, name="totals")
        inverses = keep.tile([P, TILES], F32, name="inverses")
        ratios = keep.tile([P, 3, TILES], F32, name="ratios")
        u_sums = [keep.tile([P, 1], F32, name=f"u_sum{m}") for m in range(TILES)]

        def add_transposed(m, term, first, last, quarters=slice(0, PACK)):
            for s in range(quarters.start, quarters.stop):
                nc.tensor.matmul(
                    grad_banks[m][:, s, :],
                    lhsT=term[:, s, :],
                    rhs=ident[:],
                    is_transpose=True,
                    start=(first and s == 0),
                    stop=(last and s == PACK - 1),
                )

        def score_bank(m, slots):
            bank = out_banks[m][:].rearrange("r t p -> r (t p)") if slots.start else product_banks[m][:]
            return bank[:, 0 : slots.stop - slots.start]

        def scores(m, slots=slice(0, SLOTS)):
            h, cols = m // 2, slice((m % 2) * P, (m % 2 + 1) * P)
            nc.tensor.matmul_mx(
                out=score_bank(m, slots),
                lhsT=x_codes[h][:, cols].bitcast(E4M3),
                lhsT_scale=x_scales[h][:, cols],
                rhs=wd_codes[:, slots].bitcast(E4M3),
                rhs_scale=wd_scales[:, slots],
                start=True,
                stop=True,
            )

        def scaled_scores(m, slots=slice(0, SLOTS)):
            places = slice(slots.start // PACK, slots.stop // PACK)
            nc.vector.scalar_tensor_tensor(
                z[m][:, :, places],
                score_bank(m, slots).rearrange("r (q s) -> r s q", s=PACK),
                us_cols[:, m : m + 1],
                ts_rows[:, :, places],
                ALU.mult,
                ALU.mult,
            )

        def exponentials(m):
            nc.vector.tensor_reduce(neg_max[m][:], z[m][:].rearrange("r s q -> r (s q)"), AX.X, ALU.max, negate=True)
            nc.scalar.activation(
                e[m][:], z[m][:], ACT.Exp, bias=neg_max[m][:], accum_out=totals[:, m : m + 1]
            )

        def adv_term(m):
            place = ((X_SLOT, 2 * TERM_BYTES), (X_SLOT, 3 * TERM_BYTES), (ADV_SLOT, 0), (LOW_SLOT, GROUP_BYTES))[m]
            a_term = staged(f"a_term{m}", [P, PACK, P], F32, *place)
            nc.scalar.activation(
                a_term[:].rearrange("r s q -> r q s"),
                adv_tiles[m][:].rearrange("r (q s) -> r q s", s=PACK),
                ACT.Copy,
                scale=factors[:, 0, m : m + 1],
                accum_out=factors[:, 3, m : m + 1],
            )
            return a_term

        def inverse(first, last):
            nc.vector.reciprocal(inverses[:, first:last], totals[:, first:last])

        def row_ratios(first, last):
            nc.vector.scalar_tensor_tensor(
                ratios[:, :, first:last],
                factors[:, 1:4, first:last],
                -1.0,
                inverses[:, first:last].unsqueeze(1).to_broadcast([P, 3, last - first]),
                ALU.mult,
                ALU.mult,
            )

        def entropy_terms(m):
            u_term = keep.tile([P, PACK, P], F32, name=f"u_term{m}")
            nc.vector.scalar_tensor_tensor(
                u_term[:], z[m][:], ratios[:, 0, m : m + 1], e[m][:], ALU.mult, ALU.mult, accum_out=u_sums[m][:]
            )
            add_transposed(m, u_term, False, False)

        e_scales = [keep.tile([P, 1], F32, name=f"e_scale{m}") for m in range(TILES)]
        e_terms = [keep.tile([P, PACK, P], F32, name=f"e_term{m}") for m in range(TILES)]

        def exponential_factor(m):
            neg_inverse, a_part = ratios[:, 1, m : m + 1], ratios[:, 2, m : m + 1]
            if m != 0:
                nc.scalar.activation(e_scales[m][:], u_sums[m][:], ACT.Identity, bias=a_part, scale=neg_inverse)
            else:
                nc.vector.tensor_scalar(e_scales[m][:], u_sums[m][:], neg_inverse, a_part, ALU.mult, ALU.add)

        def exponential_term(m, part=slice(0, PACK)):
            nc.scalar.activation(e_terms[m][:, part, :], e[m][:, part, :], ACT.Copy, scale=e_scales[m][:])

        g = [keep.tile([P, P, PACK], BF16, name=f"g{m}", align_bytes=64) for m in range(TILES)]
        g_codes = [keep.tile([P, P], U32, name=f"g_codes{m}", align_bytes=64) for m in range(TILES)]
        g_scales = [keep.tile([P, P], U8, name=f"g_scales{m}", align_bytes=64) for m in range(TILES)]

        def gradient(m, ts_cols, rows=slice(0, P)):
            nc.vector.tensor_tensor(
                g[m][:, rows, :],
                grad_banks[m][:, :, rows].rearrange("q s r -> q r s"),
                ts_cols[:].unsqueeze(1).to_broadcast([P, rows.stop - rows.start, PACK]),
                ALU.mult,
            )

        def quantize_gradient(m, rows=slice(0, P)):
            nc.vector.quantize_mx(
                out=g_codes[m][:, rows].bitcast(E5M2),
                scales=g_scales[m][:, rows],
                in_=g[m][:, rows, :].rearrange("q r s -> q (r s)"),
            )

        def gradient_product(m, bank, features):
            nc.tensor.matmul_mx(
                out=bank,
                lhsT=g_codes[m][:].bitcast(E5M2),
                lhsT_scale=g_scales[m][:],
                rhs=wi_codes[:, features].bitcast(E4M3),
                rhs_scale=wi_scales[:, features],
                start=True,
                stop=True,
            )

        def store_half(m, h, bank, copy_out, queue):
            res = keep.tile([P, P // 2, PACK], F32, name=f"res{m}_{h}")
            copy_out(res[:], bank.rearrange("r (t p) -> r p t", t=PACK))
            queue.dma_start(
                out=out[m * P : (m + 1) * P, h * D // 2 : (h + 1) * D // 2], in_=res[:].rearrange("r p t -> r (p t)")
            )

        def rows_gradient(m):
            bank = out_banks[m][:].rearrange("r t p -> r (t p)")
            halves_of_d = (slice(0, D // 2), slice(D // 2, D))
            if m == TILES - 1:
                banks = (product_banks[2][:, halves_of_d[0]], product_banks[0][:, halves_of_d[0]])
                for h in range(2):
                    gradient_product(m, banks[h], halves_of_d[h])
                store_half(m, 0, banks[0], nc.scalar.copy, nc.scalar)
                store_half(m, 1, banks[1], nc.vector.tensor_copy, nc.sync)
            elif m == 0:
                gradient_product(m, bank, slice(0, D))
                res = keep.tile([P, 2, P // 2, PACK], F32, name=f"res{m}")
                nc.scalar.copy(res[:], bank.rearrange("r (h t p) -> r h p t", h=2, t=PACK))
                nc.sync.dma_start(out=out[0:P, :], in_=res[:].rearrange("r h p t -> r (h p t)"))
            else:
                gradient_product(m, bank, slice(0, D))
                for h in range(2):
                    store_half(m, h, bank[:, halves_of_d[h]], nc.scalar.copy, nc.sync)

        slot_halves = (slice(0, SLOTS // 2), slice(SLOTS // 2, SLOTS))
        for slots in slot_halves:
            scores(0, slots)
        scores(1)
        a_terms = [adv_term(m) for m in range(TILES - 1)]
        for e_half, slots in enumerate(slot_halves):
            scaled_scores(0, slots)
            quantize_rows(1, slice(e_half * P, (e_half + 1) * P), late_grouped[e_half])
            scores(2 + e_half)
        scaled_scores(1)
        add_transposed(0, a_terms[0], True, False)
        exponentials(0)
        exponentials(1)
        scaled_scores(2)
        scaled_scores(3)
        high_pairs = staged("high_pairs", [P, 2, 2, P, 2], BF16, LOW_SLOT, GROUP_BYTES)
        for t in range(2):
            nc.gpsimd.tensor_scalar(
                high_pairs[:, t, :, :, :],
                w_by_d[:, :, 2 + t].rearrange("p (q u e) -> p u q e", u=2, e=2),
                1.0,
                0.0,
                ALU.mult,
                ALU.add,
            )
        products = keep.tile([P, PACK, P], F32, name="products")
        nc.gpsimd.tensor_tensor(products[:], z[1][:], e[1][:], ALU.mult)
        high_words = high_pairs[:].rearrange("p t u q e -> p (t u q e)").bitcast(F32)
        for j in range(PACK):
            nc.tensor.transpose(out_banks[3 - j // 2][:, j % 2, :], high_words[:, j * P : (j + 1) * P], ident[:])

        def leave_plane(t, start):
            by_i = staged(f"by_i{t}", [P, P * PACK], BF16, MAX_SLOT, start)
            nc.scalar.copy(
                by_i[:].bitcast(F32).rearrange("q (h p u) -> q h p u", h=2, u=2),
                out_banks[5 - t][:, 0:2, :].rearrange("q u (h p) -> q h p u", h=2),
            )
            return by_i

        def quantize_plane(t, by_i, feature_halves=(0, 1)):
            for h in feature_halves:
                cols = slice(h * D // 2 + t * P // 2, h * D // 2 + (t + 1) * P // 2)
                nc.vector.quantize_mx(
                    out=wi_codes[:, cols].bitcast(E4M3),
                    scales=wi_scales[:, cols],
                    in_=by_i[:, h * D // 2 : (h + 1) * D // 2],
                )

        by_i2 = leave_plane(2, 0)
        add_transposed(1, a_terms[1], True, False)
        add_transposed(2, a_terms[2], True, False)
        add_transposed(TILES - 1, adv_term(TILES - 1), True, False)
        inverse(0, 2)
        exponentials(2)
        row_ratios(0, 2)
        exponentials(3)
        quantize_plane(2, by_i2, (0,))
        for bank, features in ((out_banks[1], slice(0, D)), (out_banks[0], slice(D - P, D))):
            nc.tensor.matmul_mx(
                out=bank[:].rearrange("r t p -> r (t p)")[:, features],
                lhsT=wi_codes[:, P // 2 : 3 * P // 2].bitcast(E4M3),
                lhsT_scale=wi_scales[:, P // 2 : 3 * P // 2],
                rhs=wd_codes[:, features].bitcast(E4M3),
                rhs_scale=wd_scales[:, features],
                start=True,
                stop=True,
            )
        quarter_pairs = (slice(0, PACK // 2), slice(PACK // 2, PACK))
        entropy_terms(0)
        second_term = staged("second_term", [P, PACK, P], F32, MAX_SLOT, 2 * TERM_BYTES)
        nc.scalar.activation(second_term[:], products[:], ACT.Copy, scale=ratios[:, 0, 1:2], accum_out=u_sums[1][:])
        add_transposed(1, second_term, False, False)
        quantize_plane(2, by_i2, (1,))
        inverse(2, 4)
        exponential_factor(0)
        row_ratios(2, 4)
        nc.vector.tensor_scalar(e_terms[0][:], e[0][:], e_scales[0][:], None, ALU.mult)
        add_transposed(0, e_terms[0], False, True)
        entropy_terms(2)
        exponential_factor(1)
        by_i3 = leave_plane(3, 3 * TERM_BYTES)
        exponential_term(1)
        entropy_terms(3)
        quantize_plane(3, by_i3)
        add_transposed(1, e_terms[1], False, True)
        exponential_factor(2)
        exponential_term(2, quarter_pairs[0])
        exponential_factor(3)
        exponential_term(2, quarter_pairs[1])
        add_transposed(2, e_terms[2], False, True)
        for part in quarter_pairs:
            exponential_term(3, part)
        halves = (slice(0, P // 2), slice(P // 2, P))
        gradient(0, ts_cols)
        add_transposed(3, e_terms[3], False, True, quarter_pairs[0])
        for m in range(1, TILES):
            if m == 2:
                add_transposed(3, e_terms[3], False, True, quarter_pairs[1])
            gradient(m, ts_cols, halves[0])
            quantize_gradient(m - 1)
            rows_gradient(m - 1)
            gradient(m, ts_cols, halves[1])
        for rows in halves:
            quantize_gradient(TILES - 1, rows)
        rows_gradient(TILES - 1)
